import numpy as np, ml_dtypes
CORES = [23,119,17,113]
N = 4
import mx_ref
BF = ml_dtypes.bfloat16
def gentries(a):
    return np.ascontiguousarray(a.reshape(8, 16, -1).transpose(0, 2, 1)).reshape(8, -1)
def gtable(e):
    e = np.asarray(e); return np.ascontiguousarray(e.reshape(8, -1, 16).transpose(0, 2, 1)).reshape(128, -1).astype(np.int32)
def gcols(t, e):
    v = np.concatenate([t.reshape(8, 16, -1, 4), np.zeros((8, 16, 1, 4), BF)], axis=2)
    return np.ascontiguousarray(np.stack([v[g][:, e[g]] for g in range(8)])).reshape(128, -1)
def tile(rs):
    return np.stack(rs, axis=2).reshape(128, -1).astype(BF)
def pick(q, e):
    c = np.concatenate([q[0].reshape(128, -1, 4), np.zeros((128, 1, 4), np.uint8)], axis=1); s = np.concatenate([q[1], np.ones((16, 1), np.uint8)], axis=1)
    return (np.ascontiguousarray(c[:, e].reshape(128, -1)), np.ascontiguousarray(s[:, e]))
def join(*qs):
    return (np.concatenate([q[0] for q in qs], axis=1), np.concatenate([q[1] for q in qs], axis=1))
def put(q, e, v):
    c, s = q[0].reshape(128, -1, 4).copy(), q[1].copy(); c[:, e] = v[0].reshape(128, -1, 4); s[:, e] = v[1]
    return (c.reshape(128, -1), s)
def pk(c, s):
    return (np.ascontiguousarray(c), mx_ref.live(s))
def emit(q):
    return q[0], q[1]
def packed(v, rng):
    q = [mx_ref.quantize(np.ascontiguousarray(v[r])) for r in range(N)]
    return np.stack([a for a, b in q]), np.stack([mx_ref.plane(b, rng) for a, b in q])
def values_of_codes():
    e, c = np.zeros((128, 128, 4), np.float32), np.zeros((128, 2, 4), np.uint8)
    e[np.arange(128), np.arange(128), 0] = 1
    c[:127, :, 0] = np.arange(256).reshape(2, 128).T[:127]
    return mx_ref.matmul(mx_ref.quantize(e.reshape(128, 512).astype(BF)), (c.reshape(128, 8), np.full((16, 2), 127, np.uint8))).T.reshape(-1).astype(np.float64)
CODE_VALUE, SCALE_VALUE = values_of_codes(), 2.0 ** (np.arange(256) - 127.0)
def decode(q):
    return (CODE_VALUE[q[0]].reshape(16, 8, -1, 4) * SCALE_VALUE[q[1]][:, None, :, None] + 0.0).reshape(128, -1).astype(np.float32)
def f(rng, *shape):
    return mx_ref.flush((rng.standard_normal(shape, dtype=np.float32) * np.exp2(rng.integers(-2, 3, shape[:-1] + (1,)))).astype(BF))
def wide(rng, *shape, cols=0):
    v = rng.standard_normal(shape, dtype=np.float32) * np.exp2(rng.integers(-12, 13, shape)).astype(np.float32)
    if cols: v *= np.repeat(np.exp2(rng.integers(-cols, cols + 1, shape[:-2] + (1, shape[-1] // 4))) * (rng.random(shape[:-2] + (1, shape[-1] // 4)) > 0.0625), 4, axis=-1).astype(np.float32)
    return mx_ref.flush(v.astype(BF))
C, H, E, R = 320, 96, 416, 3
def big(v):
    v = v.astype(np.float32)
    v[np.abs(v) < np.float32(2.0 ** -16)] = 0
    return v.astype(BF)
def numbers_of(rng):
    return {"x": big(f(rng, N, 128, 4 * C)), "u": np.array(f(rng, N, 128, 512)), "v": np.array(f(rng, N, 128, 512))}
def stored(a):
    return np.stack([gtable(a[r]) for r in range(N)])
def lists(rng):
    return {"lf": stored(rng.integers(0, E, (N, 8, E))), "rt": stored(rng.integers(0, E, (N, 8, E)))}
def layers(rng, still=[]):
    w = big(f(rng, N, 128, 2048)).reshape(N, 8, 16, 4, 8, 16, 4)
    for i in still:
        w[:, :, i] = 0
        w[:, :, :, :, :, i] = 0
    return w
def weights(rng, w):
    c, p = packed(np.ascontiguousarray(w).reshape(N, 128, 2048), rng)
    return {"wc": c, "ws": p}
def setup_inputs(rng):
    return {**numbers_of(rng), **lists(rng), **weights(rng, layers(rng))}
def setup_inputs_ties(rng):
    d = numbers_of(rng)
    o = rng.permutation(N)
    x = d["x"].reshape(N, 8, 16, C, 4)
    x[:, :, 0] = 0
    x[:, :, 0, :, 0] = rng.integers(-2, 3, (N, 8, C)).astype(np.float32).astype(BF)
    u = d["u"].reshape(N, 128, 128, 4)
    u[:, :, ::16] = 0
    for h in range(0, 128, 16): u[:, h, h, 0] = 1
    u[o[0], :, ::16] = 0
    e = lists(rng)
    e["rt"][o[1]] = e["lf"][o[1]]
    return {"x": x.reshape(N, 128, 4 * C), "u": u.reshape(N, 128, 512), "v": d["v"], **e, **weights(rng, layers(rng, [0]))}
def setup_inputs_near(rng):
    d = numbers_of(rng)
    kind = rng.permutation(8) % 4
    x = d["x"].astype(np.float32).reshape(N, 8, 16, C, 4)
    c = rng.integers(0, 2, (N, 8, C)) * 2.0 - 1.0
    s = rng.integers(0, 16, (N, 8, C))
    x[:, :, 0] = 0
    x[:, :, 8:] = 0
    x[:, :, 0, :, 0] = c
    x[:, :, 8] = c[:, :, :, None] * ((s[:, :, :, None] >> np.arange(4)) & 1) * np.exp2(np.arange(4) - 23.0)
    x[:, :, 11, :, 0] = c * 2.0 ** -10
    u = d["u"].reshape(N, 128, 128, 4)
    u[:, :, ::16] = 0
    for g in range(8):
        h, m = 16 * g, 1.0 if kind[g] == 0 else 2.0 ** -30
        if kind[g] < 2:
            u[:, h, h, 0] = m
            u[:, h + 11, h, 0] = m
        if kind[g] < 3: u[:, h + 8, h] = m
        else:
            a = rng.integers(0, 2, (N, C))
            x[:, g, 8:] = 0
            x[:, g, 10, :, 0] = c[:, g] * a * 1.125 * 2.0 ** -30
            x[:, g, 10, :, 1] = c[:, g] * (1 - a) * 1.25 * 2.0 ** -30
            u[:, h + 10, h, 0] = m * 1.125
            u[:, h + 10, h, 1] = m
    x = (x + np.float32(0.0)).reshape(N, 128, 4 * C).astype(BF)
    return {"x": x, "u": u.reshape(N, 128, 512), "v": d["v"], **lists(rng), **weights(rng, layers(rng, [0, 8, 9, 10, 11, 12, 13, 14, 15]))}
def setup_inputs_twice(rng):
    d = numbers_of(rng)
    x = (2 * rng.integers(0, 8, (N, 8, 16, C, 4)) + 1) * np.exp2(rng.integers(-17, -15, (N, 8, 16, C, 4))) * (rng.integers(0, 2, (N, 8, 16, C, 4)) * 2.0 - 1.0)
    x[:, :, ::8, :, 0] = np.where(rng.random((N, 8, 2, C)) < 0.5, 1.96875, 1.75) * (rng.integers(0, 2, (N, 8, 2, C)) * 2.0 - 1.0)
    a = int(rng.integers(1, 8))
    x[:, a, ::8, :, 0] = 1.75
    t = np.arange(C) % 4 == rng.integers(0, 4, (N, 1))
    x[:, 0] = np.where(t[:, None, :, None], 0.0, x[:, 0])
    x[:, 0, ::8, :, 0] = np.where(t[:, None], 1.75 * 2.0 ** -24 * (rng.integers(0, 2, (N, 2, C)) * 2.0 - 1.0), x[:, 0, ::8, :, 0])
    u = d["u"].reshape(N, 128, 128, 4)
    u[:, ::8, ::16] = 0
    w = np.zeros((N, 128, 4, 128, 4), np.float32)
    i = np.arange(128)
    for b in range(4): w[:, i, b, i, b] = -32
    w[:, i[::16], 0, i[::16], 0] = -36
    w[:, i[8::16], 0, i[8::16], 0] = -18
    w[:, :, :, :16] = 0
    w[:, :, :, 16 * a:16 * a + 16] = 0
    m = np.arange(16)
    k = np.where(np.arange(N) % 2 == rng.integers(0, 2), 1.0, -1.0)[:, None]
    for b in range(4): w[:, 16 * a + m, b, m, b] = 32 * k
    w[:, 16 * a + m[::8], 0, m[::8], 0] = 36 * k
    e = rng.integers(0, E, (2, N, 8, E))
    for r in range(N):
        e[:, r, 0, :C] = rng.permutation(np.concatenate([np.arange(H), np.arange(C, E), H + rng.permutation(C - H)[:C - 2 * H]]))
    return {"x": x.astype(np.float32).reshape(N, 128, 4 * C).astype(BF), "u": u.reshape(N, 128, 512), "v": d["v"], "lf": stored(e[0]), "rt": stored(e[1]), **weights(rng, w.astype(BF))}
def setup_inputs_ends(rng):
    d = numbers_of(rng)
    e = rng.permutation(N)
    h = rng.permutation(8)
    most = 1.34375 * 2.0 ** 28
    x = (0.6 + 0.4 * rng.random((N, 8, 16, C, 4))) * most
    x[e[::2]] = most
    c = rng.integers(0, 2, (N, 1, 1, C, 1)) * 2.0 - 1.0
    c[e[1]] = c[e[1], 0, 0, 0, 0]
    x = x * c
    x[:, h[4:], 8:] = (rng.integers(0, 2, (N, 4, 8, C, 4)) * 2.0 - 1.0) * 2.0 ** -30
    u = d["u"].reshape(N, 128, 128, 4)
    u[:, :, ::16] = 0
    for g in h[:4]: u[:, :, 16 * g] = (2.0 ** 30 * (1.0 - 0.1 * rng.random((N, 128, 4))) * rng.choice([-1.0, 1.0], (N, 1, 1))).astype(np.float32).astype(BF)
    for g in h[4:]: u[:, 16 * g + 8:16 * g + 16, 16 * g] = 2.0 ** -30
    u[e[2], :, ::16] = 0
    v = d["v"]
    v[e[:2]] = (2.0 ** 30 * rng.choice([-1.0, 1.0], (2, 128, 512))).astype(np.float32).astype(BF)
    a = rng.integers(0, 2, (2, N, 8, E)) * (E - 1)
    a[:, e[0]] = E - 1
    a[:, e[1]] = 0
    a[:, e[2]] = np.argsort(rng.random((2, 8, E)), axis=2)
    p, m = np.arange(C), rng.permutation(C)
    for g, k in enumerate(rng.permutation(8)):
        t = rng.permutation(E)
        if k == 0: t = np.concatenate([rng.permutation(C), C + rng.permutation(H)])
        elif H * (k - 1) < C: t = np.concatenate([C + rng.permutation(H), rng.permutation(C)])
        a[0, e[2], g, np.concatenate([p[np.roll(m, -H * (k - 1))], np.setdiff1d(np.arange(E), p)])] = t
        p = a[0, e[2], g, p]
    a[:, e[3]] = rng.integers(0, C, (2, 8, E))
    w = np.zeros((N, 128, 4, 128, 4), np.float32)
    i = np.flatnonzero(np.arange(128) % 16 < 8)
    k = rng.choice([-4.0, 4.0], (N, 1))
    for b in range(4): w[:, i, b, i, b] = k
    v = (np.where(v < 0, -1.0, 1.0) * np.where(rng.permutation(N) % 2, 2.0 ** -30, 2.0 ** 30)[:, None, None]).astype(np.float32).astype(BF)
    return {"x": x.astype(np.float32).reshape(N, 128, 4 * C).astype(BF), "u": u.reshape(N, 128, 512), "v": v, "lf": stored(a[0]), "rt": stored(a[1]), **weights(rng, w.astype(BF))}
def setup_inputs_spread(rng):
    d = numbers_of(rng)
    w = (layers(rng).astype(np.float32) * np.float32(0.125)).astype(BF)
    return {"x": big(wide(rng, N, 128, 4 * C, cols=4)), "u": d["u"], "v": d["v"], **lists(rng), **weights(rng, w)}
def check_inputs(d):
    b = []
    for k in ("x", "u", "v"):
        a = np.abs(d[k].astype(np.float32))
        if not (np.isfinite(a).all() and ((a == 0) | (a >= 2.0 ** -30) & (a <= 2.0 ** 30)).all()): b.append("a value of " + k)
    for k in ("lf", "rt"):
        if not ((d[k] >= 0) & (d[k] < E)).all(): b.append("an entry of " + k)
    none, least, most = [emit(mx_ref.quantize(np.full((128, 16), k, np.float32).astype(BF)))[1][0, 0] for k in (0.0, 2.0 ** -30, 2.0 ** 30)]
    size = 0.0
    for r in range(N):
        if ((d["wc"][r] == 0x7F) | (d["wc"][r] == 0xFF)).any(): b.append("wc: a code that is no number")
        s = mx_ref.live(d["ws"][r])
        if ((s != none) & ((s < least) | (s > most))).any(): b.append("ws: a scale out of range")
        full = ((d["wc"][r] & 0x7F) != 0).reshape(16, 8, 512, 4).any(axis=(1, 3))
        if (full & (s == none)).any(): b.append("wc: a code other than zero at the scale of zeros")
        with np.errstate(all="ignore"):
            size = np.maximum(size, np.max(np.sum(np.abs(decode(pk(d["wc"][r], d["ws"][r])).astype(np.float64)).reshape(128, 512, 4), axis=(0, 2))))
    with np.errstate(all="ignore"):
        if not np.max(np.abs(d["x"].astype(np.float64))) * (1.125 + 2.5 * size * 2.0 ** -5) ** 3 <= 2.0 ** 30: b.append("the sizes of x and W together")
    return b
def reference(x, u, v, lf, rt, wc, ws):
    qu = [mx_ref.quantize(u[r]) for r in range(N)]
    lay = [pk(wc[r], ws[r]) for r in range(N)]
    left = [gentries(lf[r]) for r in range(N)]
    right = [gentries(rt[r]) for r in range(N)]
    now = [x[r] for r in range(N)]
    took = np.zeros((N, 8, C), np.int64)
    for t in range(R):
        q = [mx_ref.quantize(now[r]) for r in range(N)]
        edge = [pick(q[r], np.arange(H)) for r in range(N)]
        own = [decode(q[r]) for r in range(N)]
        flux, back = [], []
        for r in range(N):
            e = (r + 1) % N
            s = np.abs(mx_ref.matmul(qu[r], join(q[r], edge[e]))[::16])
            l, k = np.arange(C), np.arange(C)
            for g in range(8):
                a, b = left[r][g, l], right[r][g, k]
                first = s[g, a] <= s[g, b]
                took[r, g] = np.where(first, a, b)
                l, k = np.where(first, a, l), np.where(first, k, b)
            window = np.concatenate([own[r], own[e][:, :4 * H]], axis=1).astype(BF)
            z = mx_ref.quantize(gcols(window, took[r]))
            h = mx_ref.quantize(tile([mx_ref.matmul(pick(lay[r], np.arange(128 * b, 128 * b + 128)), z) * np.float32(0.03125) for b in range(4)]))
            c = np.full((8, E), -1)
            for g in range(8):
                i, j = np.unique(took[r, g], return_index=True)
                c[g, i] = j
            w = gcols(decode(h).astype(BF), c)
            flux.append(w[:, :4 * C].astype(np.float32))
            back.append(decode(mx_ref.quantize(np.ascontiguousarray(w[:, 4 * C:]))))
        for r in range(N):
            n = own[r] - flux[r]
            n[:, :4 * H] = n[:, :4 * H] - back[(r - 1) % N]
            now[r] = n.astype(BF)
    y, on = np.zeros((N, 128, C), np.float32), np.zeros((N, 8, C), np.float32)
    oc, osc = np.zeros((N, 128, 4 * C), np.uint8), np.zeros((N, 16, C), np.uint8)
    for r in range(N):
        q = mx_ref.quantize(now[r])
        y[r] = mx_ref.matmul(mx_ref.quantize(v[r]), q)
        on[r] = took[r]
        oc[r], osc[r] = emit(q)
    return {"y": y, "on": on, "oc": oc, "osc": osc}

@@ -1,0 +1,450 @@
+from concourse.mybir import dt, AluOpType as ALU, ActivationFunctionType as AF
+
+ROUNDS = 3
+C, H, E = 320, 96, 416
+SCRATCH = {}
+
+
+def _declare(kind, names):
+    for w in names.split():
+        n, c = w.split(":")
+        SCRATCH[n] = ("psum" if n.startswith("ps") else "sbuf", [128, int(c)], kind)
+
+
+_declare("bfloat16", "xt:1280 ut:512 vin:512 eb:516 vt:1664 mt:1280 tb:1280 tt:1344 ub:512")
+_declare("int32", "lri:52 pi:8 pa:8 pb:8 pq:8")
+_declare("uint16", "lru:52 l0:8 ll:8 cidx:20 nbu:32 na:32 nl:20 qrep:26 adr:40 ul:20 ulb:6 lz:8 lab:8 lt:8")
+_declare("float8_e4m3fn_x4", "qw:512 qu:128 q0:128 qv:128 qe:512 qc:416 qm:320 qt:320 qr:224")
+_declare("uint8", "sw:512 su:128 s0:128 sv:128 se:512 sc:416 sm:320 st:320 sr:224")
+_declare("float32", "idn:516 iw:416 cs:96 dsc:320 dia:416 offc:64 c16:8 pf:8 ja:8 jb:8 jc:8")
+_declare("float32", "k0:8 k1:8 k2:8 k3:8 k4:8 k5:8 hs:8 q4:8 dn:832 aiw:416 bi:832 win:832 ts0:128 gt:128 tr:128")
+_declare("float32", "wv:64 nw:64 pt:8 nm:64 pn:64 nn:32 gf:512 tf:512 nlf:20 ss:416 s2:416 sn:832 nr:320 eq:320 scn:320")
+_declare("float32", "dq:20 ad:20 inv0:432 inv1:432 dg0:416 dg1:416 dm:26 xf:384 ysb:320")
+_declare("float32", "ps0:512 ps1:512 ps2:512 ps3:512 ps4:512 ps5:512 ps6:512 ps7:512")
+SEMAPHORES = "cv cs ct cg lx0 lx1 llr lu lv lw stc rl nd ob bl rtl ba0 ba1 ba2 ra0 ra1 ra2".split()
+
+
+def rank_program(g, core, T, topo):
+    rank = T.rank_of(core)
+    if rank is None:
+        return
+    nxt, prv = T.cores[(rank + 1) % 4], T.cores[(rank - 1) % 4]
+    eng = {"v": g.vector, "s": g.scalar, "t": g.tensor, "g": g, "y": g.sync}
+    csem = {"v": "cv", "s": "cs", "t": "ct", "g": "cg"}
+    cnt = {s: 0 for s in SEMAPHORES}
+    know = {q: {} for q in eng}
+    acc = {}
+    serial = [0]
+
+    def A(name, lo=0, hi=None, step=1, p=None, bits=None):
+        t = T[name]
+        hi = t.shape[1] if hi is None else hi
+        ps = slice(None) if p is None else slice(*p)
+        ap = t[ps, lo:hi] if step == 1 else t[ps, lo:hi:step]
+        if bits is not None:
+            ap = ap.bitcast(bits)
+        p0, p1 = (0, 128) if p is None else (p[0], p[1])
+        return {"ap": ap, "n": name, "lo": lo, "hi": hi, "st": step, "p0": p0, "p1": p1}
+
+    def meet(a, b):
+        if a["n"].startswith("ps"):
+            return True
+        if a["hi"] <= b["lo"] or b["hi"] <= a["lo"] or a["p1"] <= b["p0"] or b["p1"] <= a["p0"]:
+            return False
+        return not (a["st"] == b["st"] and a["st"] > 1 and (a["lo"] - b["lo"]) % a["st"])
+
+    def learn(q, rec, val):
+        k = know[q]
+        k[rec["sem"]] = max(k.get(rec["sem"], 0), val)
+        for s, c in rec["know"].items():
+            if k.get(s, 0) < c:
+                k[s] = c
+
+    def settle(q, reads, writes):
+        need = []
+        for kind, regs in ((0, reads), (1, writes)):
+            for r in regs:
+                for a in acc.get(r["n"], []):
+                    if not meet(r, a["reg"]):
+                        continue
+                    same = a["rec"]["q"] == q and not a["rec"]["late"]
+                    if kind == 0 and not a["w"] and (same or not r["n"].startswith("ps")):
+                        continue
+                    need.append(a["rec"])
+        need.sort(key=lambda rec: -rec["id"])
+        for rec in need:
+            if know[q].get(rec["sem"], 0) >= rec["val"]:
+                continue
+            val = cnt[rec["sem"]] if rec["late"] else rec["val"]
+            eng[q].wait_ge(T.sem[rec["sem"]], val)
+            learn(q, rec, val)
+
+    def note(rec, reads, writes):
+        for w, regs in ((False, reads), (True, writes)):
+            for r in regs:
+                old = acc.get(r["n"], [])
+                if w and r["st"] == 1:
+                    old = [a for a in old if not (a["reg"]["lo"] >= r["lo"] and a["reg"]["hi"] <= r["hi"] and a["reg"]["p0"] >= r["p0"] and a["reg"]["p1"] <= r["p1"])]
+                old.append({"reg": r, "rec": rec, "w": w})
+                acc[r["n"]] = old
+
+    def op(q, fn, writes, reads, sem=None, inc=1, self_inc=False):
+        settle(q, reads, writes)
+        s = sem or csem[q]
+        ins = fn()
+        if not self_inc:
+            ins.then_inc(T.sem[s], inc)
+        cnt[s] += inc
+        serial[0] += 1
+        note({"q": q, "sem": s, "val": cnt[s], "late": sem is not None, "know": dict(know[q]), "id": serial[0]}, reads, writes)
+
+    def arrive(sem, n, writes):
+        cnt[sem] += n
+        serial[0] += 1
+        note({"q": "far", "sem": sem, "val": cnt[sem], "late": True, "know": {}, "id": serial[0]}, [], writes)
+
+    def copy(out, i):
+        op("v", lambda: g.vector.tensor_copy(out["ap"], i["ap"]), [out], [i])
+
+    def pick(out, i, off):
+        op("v", lambda: g.vector.tensor_copy(out["ap"], i["ap"].indirect(off["ap"])), [out], [i, off])
+
+    def put(out, off, i):
+        op("v", lambda: g.vector.tensor_copy(out["ap"].indirect(off["ap"]), i["ap"]), [out], [off, i])
+
+    def tt(out, a, b, o, off=None):
+        ia = a["ap"] if off is None else a["ap"].indirect(off["ap"])
+        op("v", lambda: g.vector.tensor_tensor(out["ap"], ia, b["ap"], o), [out], [a, b] + ([off] if off else []))
+
+    def ts(out, a, s1, o1, s2=None, o2=None, off=None):
+        ia = a["ap"] if off is None else a["ap"].indirect(off["ap"])
+        rd = [a] + [s for s in (s1, s2, off) if isinstance(s, dict)]
+        v1 = s1["ap"] if isinstance(s1, dict) else s1
+        v2 = s2["ap"] if isinstance(s2, dict) else s2
+        if o2 is None:
+            op("v", lambda: g.vector.tensor_scalar(out["ap"], ia, v1, None, o1), [out], rd)
+        else:
+            op("v", lambda: g.vector.tensor_scalar(out["ap"], ia, v1, v2, o1, o2), [out], rd)
+
+    def scan(out, d0, d1, o0, o1):
+        op("v", lambda: g.vector.tensor_tensor_scan(out["ap"], d0["ap"], d1["ap"], 0.0, o0, o1), [out], [d0, d1])
+
+    def turn(out, i):
+        op("v", lambda: g.vector.transpose(out["ap"], i["ap"]), [out], [i])
+
+    def fill(out, c):
+        op("v", lambda: g.vector.memset(out["ap"], c), [out], [])
+
+    def act(out, i, func=AF.Copy, scale=1.0, off=None, bias=0.0):
+        ia = i["ap"] if off is None else i["ap"].indirect(off["ap"])
+        sv, bv = [s["ap"] if isinstance(s, dict) else s for s in (scale, bias)]
+        rd = [i] + [s for s in (off, scale, bias) if isinstance(s, dict)]
+        op("s", lambda: g.scalar.activation(out["ap"], ia, func, scale=sv, bias=bv), [out], rd)
+
+    def quant(k, lo, hi, src):
+        o, s = A("q" + k, lo, hi), A("s" + k, lo, hi)
+        op("v", lambda: g.vector.quantize_mx(o["ap"], s["ap"], src["ap"]), [o, s], [src])
+
+    def mm(bank, w, wlo, x, lo, hi):
+        o = A("ps%d" % bank, 0, hi - lo)
+        a, b, c, d = A("q" + w, wlo, wlo + 128), A("s" + w, wlo, wlo + 128), A("q" + x, lo, hi), A("s" + x, lo, hi)
+        op("t", lambda: g.tensor.matmul_mx(o["ap"], a["ap"], b["ap"], c["ap"], d["ap"], True, True), [o], [a, b, c, d])
+
+    def P(bank, lo, hi):
+        return A("ps%d" % bank, lo, hi)
+
+    def dma(q, sem, out, i):
+        w, rd = [[a] if isinstance(a, dict) else [] for a in (out, i)]
+        oa, ia = [a["ap"] if isinstance(a, dict) else a for a in (out, i)]
+        op(q, lambda: eng[q].dma_start(oa, ia), w, rd, sem=sem, inc=16)
+
+    def iota(o, pattern, cm, base=0):
+        op("g", lambda: g.iota(o["ap"], pattern, base, cm, allow_small_or_imprecise_dtypes=True), [o], [])
+
+    def send(dst, k, a, b, c, rsem, lsem):
+        rid, pid = topo.addr(dst)[:2]
+        mask, n = topo.mask(core, dst), len(topo.engines(core, dst))
+        for name, bits in (("q" + k, dt.uint8), ("s" + k, None)):
+            i, o = A(name, a, b, bits=bits), A(name, c, c + b - a, bits=bits)
+            op("g", lambda: g.remote_dma(o["ap"], i["ap"], T.sem[rsem], T.sem[lsem], pid, rid, mask), [], [i], sem=lsem, inc=n, self_inc=True)
+
+    def unpack(banks, lo, hi, who, skip=0):
+        for b in range(4):
+            mm(banks[b], "e", 128 * b, "c", lo, hi)
+        for b in range(4):
+            o, i = A("vt", E * b + lo + skip, E * b + hi), P(banks[b], skip, hi - lo)
+            copy(o, i) if who[b] == "v" else act(o, i)
+
+    def score(bank, bank2, lo, hi, skip=0, both=True):
+        mm(bank, "u", 0, "c", lo, hi)
+        mm(bank2, "0", 0, "c", lo, hi)
+        act(A("ss", lo + skip, hi), P(bank, skip, hi - lo), AF.Abs)
+        if both:
+            act(A("s2", lo + skip, hi), P(bank2, skip, hi - lo), AF.Abs)
+
+    def border_out(r):
+        send(prv, "c", 0, H, C, "ba%d" % r, "bl")
+
+    dma("y", "lx0", A("xt", 0, 512), T.x[:, 0:512])
+    dma("s", "llr", A("lri", 0, 26), T.lf[:, :])
+    dma("y", "lx1", A("xt", 512, 1280), T.x[:, 512:1280])
+    dma("s", "llr", A("lri", 26, 52), T.rt[:, :])
+    dma("y", "lu", A("ut"), T.u[:, :])
+    dma("s", "lw", A("qw", bits=dt.uint8), T.wc[:, :])
+    dma("s", "lw", A("sw"), T.ws[:, :])
+    dma("y", "lv", A("vin"), T.v[:, :])
+    pi = A("pi")
+    op("g", lambda: g.iota(pi["ap"], [[0, 8]], 0, 1), [pi], [])
+    iota(A("c16"), [[416, 2], [256, 2], [16, 2]], 0)
+    iota(A("iw"), [[1, 416]], 0)
+    iota(A("offc"), [[0, 8], [416, 2], [0, 4]], 0)
+    quant("c", 0, 128, A("xt", 0, 512))
+    border_out(0)
+    iota(A("idn"), [[1, 516]], -4)
+
+    z, q = A("k0", 0, 1), A("pf", 1, 2)
+    copy(A("pf", 0, 1), A("pi", 0, 1))
+    ts(A("pq", 0, 1), A("pi", 0, 1), 15, ALU.bitwise_and)
+    ts(z, A("pf", 0, 1), 0.0, ALU.is_equal)
+    ts(A("k1", 0, 1), A("pf", 0, 1), 112.0, ALU.is_equal)
+    copy(q, A("pq", 0, 1))
+    ts(A("k2", 0, 1), z, -1.0, ALU.mult, 1.0, ALU.add)
+    ts(A("k3", 0, 1), z, 2.0, ALU.mult, -1.0, ALU.add)
+    ts(A("k5", 0, 1), z, 416.0, ALU.mult)
+    tt(A("k4", 0, 1), A("k3", 0, 1), A("k1", 0, 1), ALU.add)
+    for lo in (0, 4):
+        ts(A("pa", lo, lo + 2), A("pi", lo, lo + 2), 7, ALU.bitwise_and)
+        ts(A("pb", lo, lo + 2), A("pi", lo, lo + 2), 3, ALU.logical_shift_right)
+        ts(A("pa", lo + 2, lo + 4), A("pi", lo + 2, lo + 4), 1, ALU.bitwise_and)
+        ts(A("pb", lo + 2, lo + 4), A("pi", lo + 2, lo + 4), 1, ALU.logical_shift_right)
+    ts(A("hs", 0, 1), q, 15.0, ALU.is_lt, 2000.0, ALU.mult)
+    ts(A("ja"), A("pa"), 32.0, ALU.mult)
+    ts(A("q4", 0, 1), q, 416.0, ALU.add)
+    tt(A("jb"), A("ja"), A("pb"), ALU.add)
+    fill(A("lz"), 0)
+    tt(A("jc"), A("jb"), A("c16"), ALU.add)
+    fill(A("ub", 384, 512), 0.0)
+    copy(A("l0"), A("jc"))
+    t16, d16 = A("iw", 0, 16), A("cs", 32, 48)
+    ts(d16, t16, q, ALU.subtract)
+    ts(A("cs", 80, 96), t16, 0.0, ALU.is_gt)
+    ts(A("qrep"), A("iw", 0, 26), 0.0, ALU.mult, q, ALU.add)
+    ts(A("cs", 48, 64), d16, 0.0, ALU.is_equal, -4000.0, ALU.mult)
+    ts(A("cs", 64, 80), d16, 1.0, ALU.is_equal, 2000.0, ALU.mult)
+    ts(d16, d16, 0.0, ALU.is_equal, 63.0, ALU.mult)
+    tt(A("cs", 16, 32), A("cs", 48, 64), A("cs", 64, 80), ALU.add)
+    ts(d16, d16, 1.0, ALU.add)
+    copy(A("cidx"), A("iw", 0, 20))
+    tt(A("cs", 0, 16), d16, A("cs", 80, 96), ALU.mult)
+    w16 = A("iw")
+    act(A("aiw"), w16, scale=A("k2", 0, 1))
+    act(A("bi", 0, 416), w16, scale=A("k4", 0, 1))
+    act(A("bi", 416, 832), w16, AF.Identity, scale=A("k4", 0, 1), bias=A("k5", 0, 1))
+    act(A("dsc"), A("cs", 0, 16), off=A("qrep", 0, 20))
+    act(A("dia"), A("cs", 16, 32), off=A("qrep", 0, 26))
+
+    copy(A("lru"), A("lri"))
+    tt(A("dn"), A("aiw"), A("bi"), ALU.add, off=A("lru"))
+    for h in range(8):
+        for k in range(2):
+            dma("y" if h < 5 else "s", "stc", A("win", p=(16 * h + 8 * k, 16 * h + 8 * k + 8)), A("dn", p=(1 - k, 128, 16)))
+    quant("u", 0, 128, A("ut"))
+    for n, w in (("q", dt.uint32), ("s", None)):
+        pick(A(n + "0", bits=w), A(n + "u", bits=w), A("lz"))
+    score(0, 1, 0, 128)
+    quant("c", 128, 320, A("xt", 512, 1280))
+    score(6, 7, 128, 320)
+    for b in range(4):
+        fill(A("tt", 336 * b + 320, 336 * b + 336), 0.0)
+    ts(A("eb"), A("idn"), 3.0, ALU.is_equal)
+    for b in range(4):
+        quant("e", 128 * b, 128 * b + 128, A("eb", 3 - b, 515 - b))
+    pick(A("gt"), A("win"), A("l0"))
+    turn(A("ts0"), A("gt"))
+    tt(A("pt"), A("ts0", 0, 128, 16), A("ts0", 8, 128, 16), ALU.add)
+    copy(A("lt"), A("pt"))
+    pick(A("gt"), A("win"), A("lt"))
+    turn(A("tr"), A("gt"))
+    tt(A("pt"), A("tr", 8, 128, 16), A("offc", 0, 8), ALU.subtract)
+    copy(A("lab"), A("pt"))
+
+    def to_list(gi, q="y"):
+        c, p = 4 * gi, (16 * gi, 16 * gi + 16)
+        dma(q, "nd", A("nl", 0, 16, p=p), A("na", c, c + 2))
+        dma(q, "nd", A("nl", 16, 20, p=p), A("na", c + 2, c + 4, p=(0, 32)))
+
+    def choices(s):
+        a, b = 8 * s, 8 * s + 16
+        m = 4 * s
+        yield lambda: tt(A("nm", a, b), A("nw", a, b), A("offc", a, b), ALU.subtract)
+        yield lambda: tt(A("pn", a, b), A("nm", a, b), A("wv", a, b), ALU.mult)
+        yield lambda: tt(A("nn", m, m + 4), A("pn", a, a + 4), A("pn", a + 4, a + 8), ALU.add)
+        yield lambda: tt(A("nn", m + 4, m + 8), A("pn", a + 8, a + 12), A("pn", a + 12, a + 16), ALU.add)
+
+        def out():
+            copy(A("nbu", m, m + 4), A("nn", m, m + 4))
+            act(A("gf", 16 * m, 16 * m + 64), A("win"), off=A("nbu", m, m + 4))
+        yield out
+
+        def out2():
+            copy(A("na", m + 4, m + 8), A("nn", m + 4, m + 8))
+            to_list(s + 1)
+        yield out2
+        yield None
+        yield lambda: turn(A("tf", 16 * m, 16 * m + 64), A("gf", 16 * m, 16 * m + 64))
+
+        def out3():
+            copy(A("na", m, m + 4), A("tf", 16 * m + 8, 16 * m + 64, 16))
+            to_list(s)
+        yield out3
+
+    def growth():
+        todo = []
+
+        def gap():
+            f = todo.pop(0) if todo else None
+            if f:
+                f()
+        for s in range(8):
+            a = 8 * s
+            if s == 0:
+                pick(A("gt"), A("s2"), A("lab"))
+            else:
+                pick(A("gt"), A("win"), A("ll"))
+            if s < 7:
+                gap()
+                turn(A("tr"), A("gt"))
+                gap()
+            else:
+                tt(A("nm", 48, 56), A("nw", 48, 56), A("offc", 48, 56), ALU.subtract)
+                tt(A("pn", 48, 56), A("nm", 48, 56), A("wv", 48, 56), ALU.mult)
+                turn(A("tr"), A("gt"))
+                tt(A("nn", 24, 28), A("pn", 48, 52), A("pn", 52, 56), ALU.add)
+            tt(A("wv", a, a + 4), A("tr", s, 64, 16), A("tr", 64 + s, 128, 16), ALU.is_le)
+            tt(A("wv", a + 4, a + 8), A("tr", s, 64, 16), A("tr", 64 + s, 128, 16), ALU.is_gt)
+            if s == 7:
+                copy(A("nbu", 24, 28), A("nn", 24, 28))
+                act(A("gf", 384, 448), A("win"), off=A("nbu", 24, 28))
+                tt(A("pn", 56, 64), A("wv", 56, 64), A("tr", 15, 128, 16), ALU.mult)
+                gap()
+                tt(A("nn", 28, 32), A("pn", 56, 60), A("pn", 60, 64), ALU.add)
+                gap()
+                copy(A("na", 28, 32), A("nn", 28, 32))
+                to_list(7)
+                turn(A("tf", 384, 448), A("gf", 384, 448))
+                gap()
+                copy(A("na", 24, 28), A("tf", 392, 448, 16))
+                to_list(6, "s")
+                while todo:
+                    gap()
+                break
+            gap()
+            dif = A("ts0", 0, 128, 16) if s == 0 else A("tr", 8 + s, 128, 16)
+            base = A("ts0", 8, 128, 16) if s == 0 else A("tr", 8, 128, 16)
+            tt(A("pt"), A("wv", a, a + 8), dif, ALU.mult)
+            gap()
+            tt(A("nw", a, a + 8), A("pt"), base, ALU.add)
+            gap()
+            copy(A("ll"), A("nw", a, a + 8))
+            if s in (1, 3, 5):
+                todo.extend(choices(s - 1))
+
+    n_in_b = 2 * len(topo.engines(nxt, core))
+    n_in_r = 2 * len(topo.engines(prv, core))
+    for r in range(ROUNDS):
+        last = r == ROUNDS - 1
+        arrive("ba%d" % r, n_in_b, [A("qc", C, E), A("sc", C, E)])
+        score(6, 7, 288, 416, 32, False)
+        pick(A("sn", 0, 480), A("ss"), A("lru", 0, 30))
+        act(A("sn", 480, 832), A("ss"), off=A("lru", 30, 52))
+        act(A("s2", C, E), P(7, 32, 128), AF.Abs)
+        for h in range(8):
+            dma("y" if h < 4 else "s", "rl", A("win", p=(16 * h, 16 * h + 8)), A("sn", p=(0, 128, 16)))
+        if r == 0:
+            unpack((2, 3, 4, 5), 0, 128, "ssss")
+            unpack((0, 1, 2, 3), 128, 320, "ssss")
+        unpack((2, 3, 4, 5), 288, 416, "ssss", 32)
+        for k in range(2):
+            iota(A("inv%d" % k), [[0, 432]], 0, base=320)
+        growth()
+        for t in (2, 3):
+            act(A("mt", t, 1280, 4), A("vt", E * t, E * t + E), off=A("nl"))
+        act(A("nr"), A("iw"), off=A("nl"))
+        for t in (0, 1):
+            pick(A("mt", t, 1280, 4), A("vt", E * t, E * t + E), A("nl"))
+        copy(A("nlf"), A("nl"))
+        quant("m", 0, 320, A("mt"))
+        hb = (0, 1, 6, 7)
+        for b in range(4):
+            mm(hb[b], "w", 128 * b, "m", 0, 320)
+        for b in range(4):
+            act(A("tb", b, 1280, 4), P(hb[b], 0, 320), scale=0.03125)
+        tt(A("eq"), A("nlf"), A("nr"), ALU.is_equal, off=A("cidx"))
+        if last:
+            dma("y", "ob", T.on[:, :], A("nr", p=(0, 128, 16)))
+        scan(A("scn"), A("dsc"), A("eq"), ALU.mult, ALU.add)
+        ts(A("dq"), A("scn", 15, 320, 16), 32.0, ALU.is_ge, A("q4", 0, 1), ALU.mult)
+        tt(A("ad"), A("nlf"), A("dq"), ALU.max)
+        copy(A("adr", 0, 40, 2), A("ad"))
+        for c in range(9, -1, -1):
+            if c == 6:
+                quant("t", 0, 320, A("tb"))
+                for b in range(4):
+                    mm(2 + b, "e", 128 * b, "t", 0, 320)
+                for b in range(4):
+                    act(A("tt", 336 * b, 336 * b + 320), P(2 + b, 0, 320), scale=-1.0)
+            for k in (1, 0):
+                d = 10 * k + c
+                put(A("inv%d" % k), A("adr", 2 * d, 2 * d + 1), A("iw", 16 * d, 16 * d + 16))
+
+        def lists(lo, hi, out):
+            for k in (1, 0):
+                scan(A("dg%d" % k, lo, hi), A("dia", lo, hi), A("inv%d" % k, lo, hi), ALU.add, ALU.max)
+            m = A("dm", lo // 16, hi // 16)
+            tt(m, A("dg0", lo + 15, hi, 16), A("dg1", lo + 15, hi, 16), ALU.min)
+            ts(A(out), m, A("hs", 0, 1), ALU.subtract)
+
+        def minus(t):
+            return A("tt", 336 * t, 336 * t + 336)
+        lists(C, E, "ulb")
+        for t in (2, 3):
+            act(A("ub", t, 384, 4), minus(t), scale=-1.0, off=A("ulb"))
+        for t in (0, 1):
+            ts(A("ub", t, 384, 4), minus(t), -1.0, ALU.mult, off=A("ulb"))
+        quant("r", 0, 128, A("ub"))
+        send(nxt, "r", 0, H, 128, "ra%d" % r, "rtl")
+        lists(0, C, "ul")
+        for t in range(4):
+            tt(A("xt", 384 + t, 1280, 4), minus(t), A("vt", E * t + H, E * t + C), ALU.add, off=A("ul", 6, 20))
+        quant("c", 128, 320, A("xt", 512, 1280))
+        for t in range(4):
+            tt(A("xf", H * t, H * t + H), minus(t), A("vt", E * t, E * t + H), ALU.add, off=A("ul", 0, 6))
+        if last:
+            quant("v", 0, 128, A("vin"))
+            mm(6, "v", 0, "c", 128, 320)
+            act(A("ysb", 128, 320), P(6, 0, 192))
+            dma("y", "ob", T.y[:, 128:320], A("ysb", 128, 320))
+        else:
+            score(6, 7, 128, 320)
+            unpack((2, 3, 4, 5), 128, 320, "ssss")
+        arrive("ra%d" % r, n_in_r, [A("qr", 128, 224), A("sr", 128, 224)])
+        bb = (0, 1, 7, 6)
+        for b in range(4):
+            mm(bb[b], "e", 128 * b, "r", 96, 224)
+        for b in range(4):
+            tt(A("xt", b, 384, 4), A("xf", H * b, H * b + H), P(bb[b], 32, 128), ALU.subtract)
+        quant("c", 0, 128, A("xt", 0, 512))
+        if last:
+            mm(0, "v", 0, "c", 0, 128)
+            act(A("ysb", 0, 128), P(0, 0, 128))
+            dma("y", "ob", T.oc[:, :], A("qc", 0, 320, bits=dt.uint8))
+            for k in range(4):
+                dma("y" if k % 2 else "s", "ob", T.osc[4 * k:4 * k + 4, 0:320], A("sc", 0, 320, p=(32 * k, 32 * k + 4)))
+            dma("s", "ob", T.y[:, 0:128], A("ysb", 0, 128))
+        else:
+            border_out(r + 1)
+            score(0, 1, 0, 128)
+            unpack((2, 3, 4, 5), 0, 128, "vvss")
+    for s in SEMAPHORES:
+        if know["g"].get(s, 0) < cnt[s]:
+            g.wait_ge(T.sem[s], cnt[s])

@@ -11,17 +11,18 @@ def _declare(kind, names):
         SCRATCH[n] = ("psum" if n.startswith("ps") else "sbuf", [128, int(c)], kind)
 
 
-_declare("bfloat16", "xt:1280 ut:512 vin:512 eb:516 vt:1664 mt:1280 tb:1280 tt:1344 ub:512")
-_declare("int32", "lri:52 pi:8 pa:8 pb:8 pq:8")
-_declare("uint16", "lru:52 l0:8 ll:8 cidx:20 nbu:32 na:32 nl:20 qrep:26 adr:40 ul:20 ulb:6 lz:8 lab:8 lt:8")
-_declare("float8_e4m3fn_x4", "qw:512 qu:128 q0:128 qv:128 qe:512 qc:416 qm:320 qt:320 qr:224")
-_declare("uint8", "sw:512 su:128 s0:128 sv:128 se:512 sc:416 sm:320 st:320 sr:224")
-_declare("float32", "idn:516 iw:416 cs:96 dsc:320 dia:416 offc:64 c16:8 pf:8 ja:8 jb:8 jc:8")
-_declare("float32", "k0:8 k1:8 k2:8 k3:8 k4:8 k5:8 hs:8 q4:8 dn:832 aiw:416 bi:832 win:832 ts0:128 gt:128 tr:128")
-_declare("float32", "wv:64 nw:64 pt:8 nm:64 pn:64 nn:32 gf:512 tf:512 nlf:20 ss:416 s2:416 sn:832 nr:320 eq:320 scn:320")
-_declare("float32", "dq:20 ad:20 inv0:432 inv1:432 dg0:416 dg1:416 dm:26 xf:384 ysb:320")
+_declare("bfloat16", "xt:1280 ut:512 vin:512 zb:516 eb:516 vt:1664 mt:1280 tb:1280 tt:1344 ub:512 wr:960 ra:640 rb:1152")
+_declare("int32", "lri:104 bli:78 cpi:26 pi:2 pa:10 ni:32 dg:128")
+_declare("uint16", "lru:52 bl:78 l0:16 ll:8 cidx:20 nl:20 qrep:26 adr:40 ul:20 ulb:6 lz:8 lab:24 rl:8")
+_declare("float8_e4m3fn_x4", "qw:512 qu:128 q0:128 qv:128 qe:512 qc:416 qm:320 qt:320 qr:352 qa:160 qb:288 qk:240")
+_declare("uint8", "sw:512 su:128 s0:128 sv:128 se:512 sc:416 sm:320 st:320 sr:352 sa:160 sb:288 sk:240")
+_declare("float32", "i32:32 iw:416 cs:96 dsc:320 dia:416 offs:8 pf:10 kk:64 cf:16 lsa:52 lsb:52 lsc:52")
+_declare("float32", "aiw:416 biw:416 base:416 gr2:416 r2:416 ur:416 rc:416 t1:416 t2:416 t3:416 win:1664 sums:24 pat:32")
+_declare("float32", "g0:384 tr0:384 ts0:256 gt:128 tr1:128 tr2:128 tr3:128 bt0:32 bt1:32 bt2:32 bt3:32 fo0:32 fo1:32 fo2:32 fo3:32")
+_declare("float32", "nd:32 ww:32 nlf:20 ss:416 sn:1248 nr:320 eq:320 scn:320")
+_declare("float32", "dq:20 ad:20 inv0:432 inv1:432 dg0:416 dg1:416 dm:26 xf:512 ysb:320")
 _declare("float32", "ps0:512 ps1:512 ps2:512 ps3:512 ps4:512 ps5:512 ps6:512 ps7:512")
-SEMAPHORES = "cv cs ct cg lx0 lx1 llr lu lv lw stc rl nd ob bl rtl ba0 ba1 ba2 ra0 ra1 ra2".split()
+SEMAPHORES = "cv cs ct cg lx0 lx1 llr lb lc lu lv lw ka kb ta tb ob bl rtl ba0 ba1 ba2 ra0 ra1 ra2".split()
 
 
 def rank_program(g, core, T, topo):
@@ -35,6 +36,7 @@ def rank_program(g, core, T, topo):
     know = {q: {} for q in eng}
     acc = {}
     serial = [0]
+    M, S, EQ = ALU.mult, ALU.add, ALU.is_equal
 
     def A(name, lo=0, hi=None, step=1, p=None, bits=None):
         t = T[name]
@@ -43,13 +45,18 @@ def rank_program(g, core, T, topo):
         ap = t[ps, lo:hi] if step == 1 else t[ps, lo:hi:step]
         if bits is not None:
             ap = ap.bitcast(bits)
-        p0, p1 = (0, 128) if p is None else (p[0], p[1])
-        return {"ap": ap, "n": name, "lo": lo, "hi": hi, "st": step, "p0": p0, "p1": p1}
+        return {"ap": ap, "n": name, "lo": lo, "hi": hi, "st": step, "p": set(range(*(p or (128,))))}
+
+    slots = {}
+
+    def K(name):
+        i = slots.setdefault(name, len(slots))
+        return A("kk", i, i + 1)
 
     def meet(a, b):
         if a["n"].startswith("ps"):
             return True
-        if a["hi"] <= b["lo"] or b["hi"] <= a["lo"] or a["p1"] <= b["p0"] or b["p1"] <= a["p0"]:
+        if a["hi"] <= b["lo"] or b["hi"] <= a["lo"] or not a["p"] & b["p"]:
             return False
         return not (a["st"] == b["st"] and a["st"] > 1 and (a["lo"] - b["lo"]) % a["st"])
 
@@ -60,7 +67,7 @@ def rank_program(g, core, T, topo):
             if k.get(s, 0) < c:
                 k[s] = c
 
-    def settle(q, reads, writes):
+    def settle(q, reads, writes, adds):
         need = []
         for kind, regs in ((0, reads), (1, writes)):
             for r in regs:
@@ -69,6 +76,8 @@ def rank_program(g, core, T, topo):
                         continue
                     same = a["rec"]["q"] == q and not a["rec"]["late"]
                     if kind == 0 and not a["w"] and (same or not r["n"].startswith("ps")):
+                        continue
+                    if kind == 1 and adds and same:
                         continue
                     need.append(a["rec"])
         need.sort(key=lambda rec: -rec["id"])
@@ -84,12 +93,12 @@ def rank_program(g, core, T, topo):
             for r in regs:
                 old = acc.get(r["n"], [])
                 if w and r["st"] == 1:
-                    old = [a for a in old if not (a["reg"]["lo"] >= r["lo"] and a["reg"]["hi"] <= r["hi"] and a["reg"]["p0"] >= r["p0"] and a["reg"]["p1"] <= r["p1"])]
+                    old = [a for a in old if not (a["reg"]["lo"] >= r["lo"] and a["reg"]["hi"] <= r["hi"] and a["reg"]["p"] <= r["p"])]
                 old.append({"reg": r, "rec": rec, "w": w})
                 acc[r["n"]] = old
 
-    def op(q, fn, writes, reads, sem=None, inc=1, self_inc=False):
-        settle(q, reads, writes)
+    def op(q, fn, writes, reads, sem=None, inc=1, self_inc=False, adds=False):
+        settle(q, reads, writes, adds)
         s = sem or csem[q]
         ins = fn()
         if not self_inc:
@@ -145,10 +154,10 @@ def rank_program(g, core, T, topo):
         o, s = A("q" + k, lo, hi), A("s" + k, lo, hi)
         op("v", lambda: g.vector.quantize_mx(o["ap"], s["ap"], src["ap"]), [o, s], [src])
 
-    def mm(bank, w, wlo, x, lo, hi):
+    def mm(bank, w, wlo, x, lo, hi, start=True, stop=True):
         o = A("ps%d" % bank, 0, hi - lo)
         a, b, c, d = A("q" + w, wlo, wlo + 128), A("s" + w, wlo, wlo + 128), A("q" + x, lo, hi), A("s" + x, lo, hi)
-        op("t", lambda: g.tensor.matmul_mx(o["ap"], a["ap"], b["ap"], c["ap"], d["ap"], True, True), [o], [a, b, c, d])
+        op("t", lambda: g.tensor.matmul_mx(o["ap"], a["ap"], b["ap"], c["ap"], d["ap"], start, stop), [o], [a, b, c, d], adds=not start)
 
     def P(bank, lo, hi):
         return A("ps%d" % bank, lo, hi)
@@ -158,7 +167,7 @@ def rank_program(g, core, T, topo):
         oa, ia = [a["ap"] if isinstance(a, dict) else a for a in (out, i)]
         op(q, lambda: eng[q].dma_start(oa, ia), w, rd, sem=sem, inc=16)
 
-    def iota(o, pattern, cm, base=0):
+    def iota(o, pattern, cm=0, base=0):
         op("g", lambda: g.iota(o["ap"], pattern, base, cm, allow_small_or_imprecise_dtypes=True), [o], [])
 
     def send(dst, k, a, b, c, rsem, lsem):
@@ -175,198 +184,301 @@ def rank_program(g, core, T, topo):
             o, i = A("vt", E * b + lo + skip, E * b + hi), P(banks[b], skip, hi - lo)
             copy(o, i) if who[b] == "v" else act(o, i)
 
-    def score(bank, bank2, lo, hi, skip=0, both=True):
-        mm(bank, "u", 0, "c", lo, hi)
-        mm(bank2, "0", 0, "c", lo, hi)
+    def score(bank, lo, hi, skip=0):
+        mm(bank, "0", 0, "c", lo, hi)
         act(A("ss", lo + skip, hi), P(bank, skip, hi - lo), AF.Abs)
-        if both:
-            act(A("s2", lo + skip, hi), P(bank2, skip, hi - lo), AF.Abs)
 
     def border_out(r):
         send(prv, "c", 0, H, C, "ba%d" % r, "bl")
 
+    def grp(gi):
+        return (16 * gi, 16 * gi + 16)
+
+    def rows(t, gi):
+        return t[16 * gi:16 * gi + 16, :]
+
     dma("y", "lx0", A("xt", 0, 512), T.x[:, 0:512])
     dma("s", "llr", A("lri", 0, 26), T.lf[:, :])
+    dma("y", "llr", A("lri", 26, 52, p=(0, 112)), T.lf[16:128, :])
+    dma("s", "llr", A("lri", 52, 78, p=(16, 128)), T.rt[0:112, :])
+    dma("y", "llr", A("lri", 78, 104), T.rt[:, :])
+    dma("s", "llr", A("lri", 26, 52, p=(112, 128)), rows(T.lf, 0))
+    dma("y", "llr", A("lri", 52, 78, p=(0, 16)), rows(T.rt, 0))
+    dma("s", "lu", A("ut"), T.u[:, :])
     dma("y", "lx1", A("xt", 512, 1280), T.x[:, 512:1280])
-    dma("s", "llr", A("lri", 26, 52), T.rt[:, :])
-    dma("y", "lu", A("ut"), T.u[:, :])
-    dma("s", "lw", A("qw", bits=dt.uint8), T.wc[:, :])
-    dma("s", "lw", A("sw"), T.ws[:, :])
-    dma("y", "lv", A("vin"), T.v[:, :])
     pi = A("pi")
-    op("g", lambda: g.iota(pi["ap"], [[0, 8]], 0, 1), [pi], [])
-    iota(A("c16"), [[416, 2], [256, 2], [16, 2]], 0)
-    iota(A("iw"), [[1, 416]], 0)
-    iota(A("offc"), [[0, 8], [416, 2], [0, 4]], 0)
+    op("g", lambda: g.iota(pi["ap"], [[0, 2]], 0, 1), [pi], [])
+    iota(A("i32"), [[1, 32]])
+    iota(A("iw"), [[1, 416]])
+    fill(A("bli"), 0)
+    for t, gi, h, k in ((T.rt, 3, 1, 0), (T.lf, 2, 2, 0), (T.rt, 2, 3, 0), (T.lf, 3, 4, 0), (T.rt, 5, 0, 2), (T.rt, 7, 1, 2),
+                        (T.lf, 4, 2, 1), (T.rt, 4, 2, 2), (T.lf, 6, 3, 1), (T.rt, 6, 3, 2), (T.lf, 5, 4, 1), (T.lf, 7, 5, 1)):
+        dma("y", "lb", A("bli", 26 * k, 26 * k + 26, p=grp(h)), rows(t, gi))
+    dma("y", "lw", A("qw", bits=dt.uint8), T.wc[:, :])
+    dma("y", "lw", A("sw"), T.ws[:, :])
+    dma("y", "lv", A("vin"), T.v[:, :])
+
+    for i, bits in enumerate((15, 16, 3, 96, 4, 8, 6, 1, 120, 24)):
+        ts(A("pa", i, i + 1), A("pi", 0, 1), bits, ALU.bitwise_and)
+    copy(K("p"), A("pi", 0, 1))
+    copy(A("pf"), A("pa"))
+    q, e16, m4, a32, g4, t8, p6, p1, p120, p24 = [A("pf", i, i + 1) for i in range(10)]
+
+    def few(n):
+        return A("i32", 0, n)
+    d16 = A("cs", 32, 48)
+    ts(K("nl"), K("p"), 96.0, ALU.is_lt)
+    ts(K("sg"), e16, -0.125, M, 1.0, S)
+    ts(K("od3"), e16, 0.1875, M)
+    ts(d16, few(16), q, ALU.subtract)
+    ts(K("e1"), m4, 3.0, EQ, e16, M)
+    ts(K("z"), m4, K("sg"), M, K("od3"), S)
+    ts(A("cs", 48, 64), d16, 0.0, EQ, -4000.0, M)
+    ts(A("cs", 64, 80), d16, 1.0, EQ, 2000.0, M)
+    ts(K("z2"), K("z"), K("sg"), S)
+    ts(A("cf", 0, 4), few(4), K("z"), EQ)
+    ts(A("qrep"), few(26), 0.0, M, q, S)
+    ts(A("cf", 4, 8), few(4), K("z2"), EQ)
+    tt(A("cs", 16, 32), A("cs", 48, 64), A("cs", 64, 80), S)
+    ts(K("eps"), K("e1"), 26.0, M, K("nl"), M)
+    tt(A("cf", 8, 12), A("cf", 0, 4), A("cf", 4, 8), ALU.subtract)
+    act(A("dia"), A("cs", 16, 32), off=A("qrep"))
+    ts(K("od"), e16, 0.0625, M)
+    ts(A("cf", 12, 16), A("cf", 8, 12), K("nl"), M)
+    ts(K("ev"), e16, -0.0625, M, 1.0, S)
+    ts(K("ub"), e16, -256.0, M, 4096.0, S)
+    act(A("aiw"), A("iw"), scale=A("cf", 13, 14))
+    act(A("base"), A("iw"), AF.Identity, scale=A("cf", 15, 16), bias=K("eps"))
+    act(A("biw"), A("iw"), scale=A("cf", 10, 11))
+    ts(K("r1"), p6, 2.0, ALU.not_equal, 16.0, M)
+    ts(K("r2"), p1, 32.0, M, 32.0, S)
+    ts(K("r3"), t8, 0.0, EQ)
+    ts(K("r5"), q, 14.0, EQ, -48.0, M)
+    ts(K("r6"), q, 15.0, EQ, -32.0, M)
+    ts(K("r4"), K("r2"), K("r3"), M, 32.0, S)
+    ts(K("r7"), K("r1"), K("r5"), S, K("r6"), S)
+    ts(K("hs"), q, 15.0, ALU.is_lt, 2000.0, M)
+    ts(K("r8"), K("r4"), K("r7"), S)
     quant("c", 0, 128, A("xt", 0, 512))
     border_out(0)
-    iota(A("idn"), [[1, 516]], -4)
-
-    z, q = A("k0", 0, 1), A("pf", 1, 2)
-    copy(A("pf", 0, 1), A("pi", 0, 1))
-    ts(A("pq", 0, 1), A("pi", 0, 1), 15, ALU.bitwise_and)
-    ts(z, A("pf", 0, 1), 0.0, ALU.is_equal)
-    ts(A("k1", 0, 1), A("pf", 0, 1), 112.0, ALU.is_equal)
-    copy(q, A("pq", 0, 1))
-    ts(A("k2", 0, 1), z, -1.0, ALU.mult, 1.0, ALU.add)
-    ts(A("k3", 0, 1), z, 2.0, ALU.mult, -1.0, ALU.add)
-    ts(A("k5", 0, 1), z, 416.0, ALU.mult)
-    tt(A("k4", 0, 1), A("k3", 0, 1), A("k1", 0, 1), ALU.add)
-    for lo in (0, 4):
-        ts(A("pa", lo, lo + 2), A("pi", lo, lo + 2), 7, ALU.bitwise_and)
-        ts(A("pb", lo, lo + 2), A("pi", lo, lo + 2), 3, ALU.logical_shift_right)
-        ts(A("pa", lo + 2, lo + 4), A("pi", lo + 2, lo + 4), 1, ALU.bitwise_and)
-        ts(A("pb", lo + 2, lo + 4), A("pi", lo + 2, lo + 4), 1, ALU.logical_shift_right)
-    ts(A("hs", 0, 1), q, 15.0, ALU.is_lt, 2000.0, ALU.mult)
-    ts(A("ja"), A("pa"), 32.0, ALU.mult)
-    ts(A("q4", 0, 1), q, 416.0, ALU.add)
-    tt(A("jb"), A("ja"), A("pb"), ALU.add)
-    fill(A("lz"), 0)
-    tt(A("jc"), A("jb"), A("c16"), ALU.add)
-    fill(A("ub", 384, 512), 0.0)
-    copy(A("l0"), A("jc"))
-    t16, d16 = A("iw", 0, 16), A("cs", 32, 48)
-    ts(d16, t16, q, ALU.subtract)
-    ts(A("cs", 80, 96), t16, 0.0, ALU.is_gt)
-    ts(A("qrep"), A("iw", 0, 26), 0.0, ALU.mult, q, ALU.add)
-    ts(A("cs", 48, 64), d16, 0.0, ALU.is_equal, -4000.0, ALU.mult)
-    ts(A("cs", 64, 80), d16, 1.0, ALU.is_equal, 2000.0, ALU.mult)
-    ts(d16, d16, 0.0, ALU.is_equal, 63.0, ALU.mult)
-    tt(A("cs", 16, 32), A("cs", 48, 64), A("cs", 64, 80), ALU.add)
-    ts(d16, d16, 1.0, ALU.add)
-    copy(A("cidx"), A("iw", 0, 20))
-    tt(A("cs", 0, 16), d16, A("cs", 80, 96), ALU.mult)
-    w16 = A("iw")
-    act(A("aiw"), w16, scale=A("k2", 0, 1))
-    act(A("bi", 0, 416), w16, scale=A("k4", 0, 1))
-    act(A("bi", 416, 832), w16, AF.Identity, scale=A("k4", 0, 1), bias=A("k5", 0, 1))
-    act(A("dsc"), A("cs", 0, 16), off=A("qrep", 0, 20))
-    act(A("dia"), A("cs", 16, 32), off=A("qrep", 0, 26))
-
-    copy(A("lru"), A("lri"))
-    tt(A("dn"), A("aiw"), A("bi"), ALU.add, off=A("lru"))
-    for h in range(8):
-        for k in range(2):
-            dma("y" if h < 5 else "s", "stc", A("win", p=(16 * h + 8 * k, 16 * h + 8 * k + 8)), A("dn", p=(1 - k, 128, 16)))
+    iota(A("offs"), [[416, 2], [0, 4]])
+    iota(A("zb"), [[0, 516]])
+    eb, zb = A("eb"), A("zb")
+    op("g", lambda: g.affine_select(eb["ap"], zb["ap"], [[1, 516]], ALU.not_equal, 1.0, -3, -4), [eb], [zb])
+    for n in ("ra", "rb", "ub"):
+        iota(A(n), [[0, T[n].shape[1]]])
+    ts(A("lsa"), A("lri", 0, 52), K("ev"), M)
+    ts(A("lsb"), A("lri", 52, 104), K("od"), M)
+    ts(A("lz"), few(8), 0.0, M, K("r8"), S)
+    tt(A("lsc"), A("lsa"), A("lsb"), S)
+    copy(A("lru"), A("lsc"))
+    l1, l2 = A("lru", 0, 26), A("lru", 26, 52)
+    act(A("r2"), A("iw"), off=l2)
+    tt(A("t1"), A("aiw"), A("base"), S, off=l1)
+    act(A("gr2"), A("r2"), scale=A("cf", 8, 9))
+    act(A("rc"), A("r2"), off=l1)
     quant("u", 0, 128, A("ut"))
-    for n, w in (("q", dt.uint32), ("s", None)):
-        pick(A(n + "0", bits=w), A(n + "u", bits=w), A("lz"))
-    score(0, 1, 0, 128)
+    tt(A("t2"), A("biw"), A("t1"), S, off=l2)
+    act(A("ur"), A("iw"), AF.Identity, bias=K("ub"), off=l1)
+    pick(A("q0", bits=dt.uint32), A("qu", bits=dt.uint32), A("lz"))
+    tt(A("t3"), A("gr2"), A("t2"), S, off=l1)
+    phase = (2, 0, 0, 2)
+
+    def lay(qs, src, s, cls, all16=True):
+        for side in (0, 1):
+            gi, lo = 2 * s + side, 832 * (s // 2) + 416 * side
+            for dst, p in ([((cls + 64 * z, 64 * z + 64, 4), grp(gi)) for z in (0, 1)] if all16 else [((cls, 128, 16), (16 * gi, 16 * gi + 8))]):
+                dma(qs[side], "ka" if s < 2 else "kb", A("win", lo, lo + 416, p=dst), A(src, p=p))
+    scan(A("dg0"), A("dia"), A("rc"), S, ALU.max)
+    for s in (0, 1):
+        lay("yy", "t3", s, phase[s])
+        lay("ss", "ur", s, phase[s] + 1)
+    s0, su, lz = A("s0"), A("su"), A("lz")
+    op("s", lambda: g.scalar.activation(s0["ap"], su["ap"].indirect(lz["ap"]), AF.Copy), [s0], [su, lz])
     quant("c", 128, 320, A("xt", 512, 1280))
-    score(6, 7, 128, 320)
-    for b in range(4):
-        fill(A("tt", 336 * b + 320, 336 * b + 336), 0.0)
-    ts(A("eb"), A("idn"), 3.0, ALU.is_equal)
-    for b in range(4):
-        quant("e", 128 * b, 128 * b + 128, A("eb", 3 - b, 515 - b))
-    pick(A("gt"), A("win"), A("l0"))
-    turn(A("ts0"), A("gt"))
-    tt(A("pt"), A("ts0", 0, 128, 16), A("ts0", 8, 128, 16), ALU.add)
-    copy(A("lt"), A("pt"))
-    pick(A("gt"), A("win"), A("lt"))
-    turn(A("tr"), A("gt"))
-    tt(A("pt"), A("tr", 8, 128, 16), A("offc", 0, 8), ALU.subtract)
-    copy(A("lab"), A("pt"))
+    ts(A("cpi"), A("dg0", 15, 416, 16), K("hs"), ALU.subtract)
+    for gi, h, k in ((2, 0, 0), (3, 5, 0), (4, 0, 1), (5, 4, 2), (6, 1, 1), (7, 5, 2)):
+        dma("y", "lc", A("bli", 26 * k, 26 * k + 26, p=grp(h)), A("cpi", p=grp(gi)))
+    for s in (2, 3):
+        lay("yy", "t3", s, phase[s])
+        lay("yy", "ur", s, phase[s] + 1, False)
+    score(0, 0, 128)
+    score(6, 128, 320)
+    ts(K("b0"), K("p"), 2.0, M, q, ALU.subtract)
+    ts(K("b2"), a32, 0.5, M, q, S)
+    ts(K("b4"), K("p"), a32, S)
+    ts(K("b1"), K("b0"), 16.0, S)
+    ts(K("b3"), K("b2"), 256.0, S)
+    ts(K("b5"), K("b4"), 32.0, S)
+    for i, b in enumerate(("b0", "b1", "b3", "b3", "b4", "b5", "b3", "b3")):
+        lo = 8 * (i // 4)
+        ts(A("l0", lo + i % 4, lo + 8, 4), few(2), 416.0, M, K(b), S)
+    ts(K("c0"), g4, 32.0, M, m4, S)
+    ts(K("c1"), e16, 0.25, M, t8, S)
+    ts(K("c2"), p24, 2.0, M, 64.0, S)
+    ts(K("c3"), p120, 0.5, M, K("c0"), S)
+    ts(K("c4"), a32, 0.5, M, K("c0"), S)
+    ts(K("c5"), a32, 0.125, M, K("c0"), S)
+    ts(K("c6"), K("c3"), 256.0, S)
+    ts(K("c7"), K("c4"), K("c1"), S)
+    ts(K("c8"), K("c5"), K("c2"), S)
+    ts(A("rl", 2, 8, 4), few(2), -256.0, M, K("c6"), S)
+    ts(A("rl", 0, 8, 4), few(2), 512.0, M, K("c7"), S)
+    ts(A("rl", 1, 6, 2), few(3), 256.0, M, K("c8"), S)
+    copy(A("rl", 7, 8), K("c8"))
+    fill(A("bt0", 0, 32, 4), 0.0)
+    fill(A("dg"), 0)
+    for lo, hi, st, c in ((0, 16, 2, 1.0), (16, 32, 2, -1.0), (1, 16, 4, -1.0), (17, 32, 2, 1.0), (3, 16, 4, 0.0)):
+        fill(A("pat", lo, hi, st), c)
+    ts(K("w0"), q, 112.0, S)
+    pick(A("g0", 0, 256), A("win", 0, 832), A("l0"))
+    ts(A("wr", 0, 960, 4), A("iw", 0, 240), K("w0"), EQ)
+    turn(A("ts0"), A("g0", 0, 256))
+    for t in (1, 2, 3):
+        act(A("wr", t, 960, 4), A("wr", 0, 960, 4))
+    v = [A("ts0", 128 + 14 - 4 * i, 256, 16) for i in range(4)]
+    copy(A("bl"), A("bli"))
+    tt(A("sums", 0, 8), v[0], v[1], S)
+    ts(A("lab", 20, 24), A("ts0", 192 + 14, 256, 16), 416.0, ALU.subtract)
+    tt(A("sums", 8, 16), A("sums", 0, 8), v[2], S)
+    copy(A("lab", 8, 12), A("sums", 0, 4))
+    ts(A("lab", 16, 20), A("sums", 4, 8), 416.0, ALU.subtract)
+    tt(A("sums", 16, 20), A("sums", 8, 12), A("ts0", 128 + 2, 192, 16), S)
+    copy(A("lab", 4, 8), A("sums", 8, 12))
+    ts(A("lab", 12, 16), A("sums", 12, 16), 416.0, ALU.subtract)
+    copy(A("lab", 0, 4), A("sums", 16, 20))
 
-    def to_list(gi, q="y"):
-        c, p = 4 * gi, (16 * gi, 16 * gi + 16)
-        dma(q, "nd", A("nl", 0, 16, p=p), A("na", c, c + 2))
-        dma(q, "nd", A("nl", 16, 20, p=p), A("na", c + 2, c + 4, p=(0, 32)))
+    def later_constants():
+        yield lambda: quant("k", 0, 240, A("wr"))
+        yield lambda: quant("b", 128, 288, A("rb", 512, 1152))
+        for b in range(4):
+            yield lambda b=b: quant("e", 128 * b, 128 * b + 128, A("eb", 3 - b, 515 - b))
+        yield lambda: quant("a", 32, 160, A("ra", 128, 640))
 
-    def choices(s):
-        a, b = 8 * s, 8 * s + 16
-        m = 4 * s
-        yield lambda: tt(A("nm", a, b), A("nw", a, b), A("offc", a, b), ALU.subtract)
-        yield lambda: tt(A("pn", a, b), A("nm", a, b), A("wv", a, b), ALU.mult)
-        yield lambda: tt(A("nn", m, m + 4), A("pn", a, a + 4), A("pn", a + 4, a + 8), ALU.add)
-        yield lambda: tt(A("nn", m + 4, m + 8), A("pn", a + 8, a + 12), A("pn", a + 12, a + 16), ALU.add)
+        def scans():
+            ts(A("cs", 80, 96), few(16), 0.0, ALU.is_gt)
+            ts(A("cs", 48, 64), d16, 0.0, EQ, 63.0, M)
+            copy(A("cidx"), few(20))
+            ts(A("cs", 64, 80), A("cs", 48, 64), 1.0, S)
+            ts(K("q4"), q, 416.0, S)
+            tt(A("cs", 0, 16), A("cs", 64, 80), A("cs", 80, 96), M)
+        yield scans
 
-        def out():
-            copy(A("nbu", m, m + 4), A("nn", m, m + 4))
-            act(A("gf", 16 * m, 16 * m + 64), A("win"), off=A("nbu", m, m + 4))
-        yield out
+        def rest():
+            unpack((2, 3, 4, 5), 0, 128, "ssss")
+            unpack((0, 7, 2, 3), 128, 320, "ssss")
+            unpack((2, 3, 4, 5), 288, 416, "ssss", 32)
+            act(A("dsc"), A("cs", 0, 16), off=A("qrep", 0, 20))
+            for b in range(4):
+                act(A("tt", 336 * b + 320, 336 * b + 336), few(16), scale=0.0)
+            quant("r", 224, 352, A("ub"))
+        yield rest
 
-        def out2():
-            copy(A("na", m + 4, m + 8), A("nn", m + 4, m + 8))
-            to_list(s + 1)
-        yield out2
-        yield None
-        yield lambda: turn(A("tf", 16 * m, 16 * m + 64), A("gf", 16 * m, 16 * m + 64))
+    def carry(gi):
+        x, lo = ("a", 32 * (gi - 6)) if gi > 5 else ("b", 32 * gi)
+        mm(1, "k", 112 - 16 * gi, x, lo, lo + 128, gi == 0, gi == 7)
 
-        def out3():
-            copy(A("na", m, m + 4), A("tf", 16 * m + 8, 16 * m + 64, 16))
-            to_list(s)
-        yield out3
+    def digits(s):
+        for i, bits in enumerate((15, 240, 256)):
+            yield lambda i=i, bits=bits: ts(A("dg", 32 * s + i, 32 * s + 32, 4), A("ni", 8 * s, 8 * s + 8), bits, ALU.bitwise_and)
+        yield lambda: put(A("ra" if s == 3 else "rb"), A("rl", 2 * s, 2 * s + 2), A("dg", 32 * s, 32 * s + 32))
 
-    def growth():
+    def first_choice(s, tr):
+        bt, u, n = "bt%d" % s, phase[s] + 1, 24 * (s == 3)
+        yield lambda: tt(A("nd", n, n + 4), A(tr, u, 64, 16), A(tr, 64 + u, 128, 16), ALU.subtract)
+        yield lambda: tt(A("nd", n + 4, n + 8), A("nd", n, n + 4), A(bt, 2, 16, 4), M)
+        yield lambda: tt(A("ni", 8 * s, 8 * s + 8, 2), A("nd", n + 4, n + 8), A(tr, 64 + u, 128, 16), S)
+
+    def choices(s, tr):
+        bt, fo = "bt%d" % s, "fo%d" % s
+        f = list(first_choice(s, tr))
+        yield f[0]
+        yield lambda: scan(A("ww"), A(bt), A("pat"), M, S)
+        yield lambda: tt(A("nd", 8, 16), A(fo, 3, 32, 4), A("offs"), ALU.subtract)
+        yield f[1]
+        yield lambda: tt(A("nd", 16, 24), A("nd", 8, 16), A("ww", 3, 32, 4), M)
+        yield f[2]
+        yield lambda: tt(A("ni", 8 * s + 1, 8 * s + 8, 2), A("nd", 16, 20), A("nd", 20, 24), S)
+        yield from digits(s)
+        if s:
+            def out():
+                quant("b", 128 * s - 128, 128 * s, A("rb", 512 * s - 512, 512 * s))
+                for gi in range(0, 4) if s == 1 else (4, 5):
+                    carry(gi)
+            yield out
+
+    def growth(r):
         todo = []
 
-        def gap():
-            f = todo.pop(0) if todo else None
-            if f:
-                f()
-        for s in range(8):
-            a = 8 * s
+        def gap(n=1):
+            for _ in range(n):
+                if todo:
+                    todo.pop(0)()
+        for s in range(4):
+            bt, fo, ph = "bt%d" % s, "fo%d" % s, phase[s]
             if s == 0:
-                pick(A("gt"), A("s2"), A("lab"))
+                tr = "ts0"
+                pick(A("g0"), A("ss"), A("lab"))
+                turn(A("tr0"), A("g0"))
+                for side in (0, 1):
+                    for k, cls in enumerate((15, 14, 15)):
+                        c = 64 * k + cls
+                        tt(A(bt, 16 * side + k + 1, 16 * side + 16, 4), A("tr0", c, 64 * k + 64, 16), A("tr0", 192 + c, 256 + 64 * k, 16), ALU.is_le)
             else:
-                pick(A("gt"), A("win"), A("ll"))
-            if s < 7:
-                gap()
-                turn(A("tr"), A("gt"))
+                tr = "tr%d" % s
+                lo = 832 * (s // 2)
+                pick(A("gt"), A("win", lo, lo + 832), A("ll"))
+                gap(2)
+                turn(A(tr), A("gt"))
+                gap(2)
+                for side in (0, 1):
+                    tt(A(bt, 16 * side, 16 * side + 16), A(tr, ph + 1, 64, 4), A(tr, 64 + ph + 1, 128, 4), ALU.is_le)
+            f = list(first_choice(3, tr)) if s == 3 else None
+            f[0]() if f else gap()
+            gap()
+            tt(A(bt, 3, 32, 4), A(bt, 2, 32, 4), A(bt, 3, 32, 4), ALU.max)
+            f[1]() if f else gap()
+            gap()
+            scan(A(fo), A(bt), A(tr, ph, 128, 4), M, S)
+            f[2]() if f else gap()
+            gap()
+            if s < 3:
+                copy(A("ll"), A(fo, 3, 32, 4))
+                todo.extend(choices(s, tr))
+                if s == 0:
+                    gap(len(todo))
+                    if r == 0:
+                        todo.extend(later_constants())
                 gap()
             else:
-                tt(A("nm", 48, 56), A("nw", 48, 56), A("offc", 48, 56), ALU.subtract)
-                tt(A("pn", 48, 56), A("nm", 48, 56), A("wv", 48, 56), ALU.mult)
-                turn(A("tr"), A("gt"))
-                tt(A("nn", 24, 28), A("pn", 48, 52), A("pn", 52, 56), ALU.add)
-            tt(A("wv", a, a + 4), A("tr", s, 64, 16), A("tr", 64 + s, 128, 16), ALU.is_le)
-            tt(A("wv", a + 4, a + 8), A("tr", s, 64, 16), A("tr", 64 + s, 128, 16), ALU.is_gt)
-            if s == 7:
-                copy(A("nbu", 24, 28), A("nn", 24, 28))
-                act(A("gf", 384, 448), A("win"), off=A("nbu", 24, 28))
-                tt(A("pn", 56, 64), A("wv", 56, 64), A("tr", 15, 128, 16), ALU.mult)
-                gap()
-                tt(A("nn", 28, 32), A("pn", 56, 60), A("pn", 60, 64), ALU.add)
-                gap()
-                copy(A("na", 28, 32), A("nn", 28, 32))
-                to_list(7)
-                turn(A("tf", 384, 448), A("gf", 384, 448))
-                gap()
-                copy(A("na", 24, 28), A("tf", 392, 448, 16))
-                to_list(6, "s")
-                while todo:
-                    gap()
-                break
-            gap()
-            dif = A("ts0", 0, 128, 16) if s == 0 else A("tr", 8 + s, 128, 16)
-            base = A("ts0", 8, 128, 16) if s == 0 else A("tr", 8, 128, 16)
-            tt(A("pt"), A("wv", a, a + 8), dif, ALU.mult)
-            gap()
-            tt(A("nw", a, a + 8), A("pt"), base, ALU.add)
-            gap()
-            copy(A("ll"), A("nw", a, a + 8))
-            if s in (1, 3, 5):
-                todo.extend(choices(s - 1))
+                tt(A("ni", 25, 32, 2), A(fo, 3, 16, 4), A(fo, 19, 32, 4), S)
+                gap(len(todo))
+                for f in digits(3):
+                    f()
+                quant("a", 0, 128, A("ra", 0, 512))
+                carry(6)
+                carry(7)
+                copy(A("nl"), P(1, 0, 20))
 
     n_in_b = 2 * len(topo.engines(nxt, core))
     n_in_r = 2 * len(topo.engines(prv, core))
     for r in range(ROUNDS):
         last = r == ROUNDS - 1
         arrive("ba%d" % r, n_in_b, [A("qc", C, E), A("sc", C, E)])
-        score(6, 7, 288, 416, 32, False)
-        pick(A("sn", 0, 480), A("ss"), A("lru", 0, 30))
-        act(A("sn", 480, 832), A("ss"), off=A("lru", 30, 52))
-        act(A("s2", C, E), P(7, 32, 128), AF.Abs)
+        score(6, 288, 416, 32)
+        pick(A("sn", 0, 416), A("ss"), A("bl", 0, 26))
+        act(A("sn", 416, 1248), A("ss"), off=A("bl", 26, 78))
         for h in range(8):
-            dma("y" if h < 4 else "s", "rl", A("win", p=(16 * h, 16 * h + 8)), A("sn", p=(0, 128, 16)))
-        if r == 0:
+            dma("y", "ta", A("win", 0, 832, p=(16 * h + 5, 16 * h + 14, 4)), A("sn", 0, 416, p=(8, 94, 17)))
+        for h in range(8):
+            dma("ys"[h % 2], "tb", A("win", 832, 1664, p=(16 * h + 5, 16 * h + 16, 2)), A("sn", 416, 1248, p=(0, 86, 17)))
+        if r:
             unpack((2, 3, 4, 5), 0, 128, "ssss")
-            unpack((0, 1, 2, 3), 128, 320, "ssss")
-        unpack((2, 3, 4, 5), 288, 416, "ssss", 32)
+            unpack((0, 7, 2, 3), 128, 320, "ssss")
+            unpack((2, 3, 4, 5), 288, 416, "ssss", 32)
         for k in range(2):
-            iota(A("inv%d" % k), [[0, 432]], 0, base=320)
-        growth()
+            iota(A("inv%d" % k), [[0, 432]], base=320)
+        growth(r)
         for t in (2, 3):
             act(A("mt", t, 1280, 4), A("vt", E * t, E * t + E), off=A("nl"))
         act(A("nr"), A("iw"), off=A("nl"))
@@ -379,11 +491,11 @@ def rank_program(g, core, T, topo):
             mm(hb[b], "w", 128 * b, "m", 0, 320)
         for b in range(4):
             act(A("tb", b, 1280, 4), P(hb[b], 0, 320), scale=0.03125)
-        tt(A("eq"), A("nlf"), A("nr"), ALU.is_equal, off=A("cidx"))
+        tt(A("eq"), A("nlf"), A("nr"), EQ, off=A("cidx"))
         if last:
             dma("y", "ob", T.on[:, :], A("nr", p=(0, 128, 16)))
-        scan(A("scn"), A("dsc"), A("eq"), ALU.mult, ALU.add)
-        ts(A("dq"), A("scn", 15, 320, 16), 32.0, ALU.is_ge, A("q4", 0, 1), ALU.mult)
+        scan(A("scn"), A("dsc"), A("eq"), M, S)
+        ts(A("dq"), A("scn", 15, 320, 16), 32.0, ALU.is_ge, K("q4"), M)
         tt(A("ad"), A("nlf"), A("dq"), ALU.max)
         copy(A("adr", 0, 40, 2), A("ad"))
         for c in range(9, -1, -1):
@@ -399,40 +511,40 @@ def rank_program(g, core, T, topo):
 
         def lists(lo, hi, out):
             for k in (1, 0):
-                scan(A("dg%d" % k, lo, hi), A("dia", lo, hi), A("inv%d" % k, lo, hi), ALU.add, ALU.max)
+                scan(A("dg%d" % k, lo, hi), A("dia", lo, hi), A("inv%d" % k, lo, hi), S, ALU.max)
             m = A("dm", lo // 16, hi // 16)
             tt(m, A("dg0", lo + 15, hi, 16), A("dg1", lo + 15, hi, 16), ALU.min)
-            ts(A(out), m, A("hs", 0, 1), ALU.subtract)
+            ts(out, m, K("hs"), ALU.subtract)
 
         def minus(t):
             return A("tt", 336 * t, 336 * t + 336)
-        lists(C, E, "ulb")
+        lists(C, E, A("ulb"))
         for t in (2, 3):
             act(A("ub", t, 384, 4), minus(t), scale=-1.0, off=A("ulb"))
         for t in (0, 1):
-            ts(A("ub", t, 384, 4), minus(t), -1.0, ALU.mult, off=A("ulb"))
+            ts(A("ub", t, 384, 4), minus(t), -1.0, M, off=A("ulb"))
         quant("r", 0, 128, A("ub"))
         send(nxt, "r", 0, H, 128, "ra%d" % r, "rtl")
-        lists(0, C, "ul")
+
+        def rest():
+            for t in range(4):
+                tt(A("xt", 512 + t, 1280, 4), minus(t), A("vt", E * t + 128, E * t + C), S, off=A("ul", 8, 20))
+            quant("c", 128, 320, A("xt", 512, 1280))
+        lists(0, C, A("ul"))
         for t in range(4):
-            tt(A("xt", 384 + t, 1280, 4), minus(t), A("vt", E * t + H, E * t + C), ALU.add, off=A("ul", 6, 20))
-        quant("c", 128, 320, A("xt", 512, 1280))
-        for t in range(4):
-            tt(A("xf", H * t, H * t + H), minus(t), A("vt", E * t, E * t + H), ALU.add, off=A("ul", 0, 6))
+            tt(A("xf", 128 * t, 128 * t + 128), minus(t), A("vt", E * t, E * t + 128), S, off=A("ul", 0, 8))
         if last:
+            rest()
             quant("v", 0, 128, A("vin"))
             mm(6, "v", 0, "c", 128, 320)
             act(A("ysb", 128, 320), P(6, 0, 192))
             dma("y", "ob", T.y[:, 128:320], A("ysb", 128, 320))
-        else:
-            score(6, 7, 128, 320)
-            unpack((2, 3, 4, 5), 128, 320, "ssss")
         arrive("ra%d" % r, n_in_r, [A("qr", 128, 224), A("sr", 128, 224)])
-        bb = (0, 1, 7, 6)
+        bb = (0, 1, 7, 2)
         for b in range(4):
-            mm(bb[b], "e", 128 * b, "r", 96, 224)
+            mm(bb[b], "e", 128 * b, "r", 128, 256)
         for b in range(4):
-            tt(A("xt", b, 384, 4), A("xf", H * b, H * b + H), P(bb[b], 32, 128), ALU.subtract)
+            tt(A("xt", b, 512, 4), A("xf", 128 * b, 128 * b + 128), P(bb[b], 0, 128), ALU.subtract)
         quant("c", 0, 128, A("xt", 0, 512))
         if last:
             mm(0, "v", 0, "c", 0, 128)
@@ -443,8 +555,9 @@ def rank_program(g, core, T, topo):
             dma("s", "ob", T.y[:, 0:128], A("ysb", 0, 128))
         else:
             border_out(r + 1)
-            score(0, 1, 0, 128)
-            unpack((2, 3, 4, 5), 0, 128, "vvss")
+            score(0, 0, 128)
+            rest()
+            score(6, 128, 320)
     for s in SEMAPHORES:
         if know["g"].get(s, 0) < cnt[s]:
             g.wait_ge(T.sem[s], cnt[s])

@@ -11,18 +11,18 @@ def _declare(kind, names):
         SCRATCH[n] = ("psum" if n.startswith("ps") else "sbuf", [128, int(c)], kind)
 
 
-_declare("bfloat16", "xt:1280 ut:512 vin:512 zb:516 eb:516 vt:1664 mt:1280 tb:1280 tt:1344 ub:512 wr:960 ra:640 rb:1152")
-_declare("int32", "lri:104 bli:78 cpi:26 pi:2 pa:10 ni:32 dg:128")
+_declare("bfloat16", "xt:1280 ut:512 vin:512 zb:516 eb:516 vt:1664 mt:1280 tb:1280 tt:1344 ub:512 wr:960 ra:640 rb:1152 dsc:320 eq:320 scn:320")
+_declare("int32", "lri:104 bli:78 cpi:26 pi:2 pa:8 ni:32 dg:128")
 _declare("uint16", "lru:52 bl:78 l0:16 ll:8 cidx:20 nl:20 qrep:26 adr:40 ul:20 ulb:6 lz:8 lab:24 rl:8")
 _declare("float8_e4m3fn_x4", "qw:512 qu:128 q0:128 qv:128 qe:512 qc:416 qm:320 qt:320 qr:352 qa:160 qb:288 qk:240")
 _declare("uint8", "sw:512 su:128 s0:128 sv:128 se:512 sc:416 sm:320 st:320 sr:352 sa:160 sb:288 sk:240")
-_declare("float32", "i32:32 iw:416 cs:96 dsc:320 dia:416 offs:8 pf:10 kk:64 cf:16 lsa:52 lsb:52 lsc:52")
+_declare("float32", "i32:32 iw:416 cs:96 dia:416 offs:8 pf:8 kk:64 cf:16 lsa:52 lsb:52 lsc:52 l0f:16 rlf:8")
 _declare("float32", "aiw:416 biw:416 base:416 gr2:416 r2:416 ur:416 rc:416 t1:416 t2:416 t3:416 win:1664 sums:24 pat:32")
 _declare("float32", "g0:384 tr0:384 ts0:256 gt:128 tr1:128 tr2:128 tr3:128 bt0:32 bt1:32 bt2:32 bt3:32 fo0:32 fo1:32 fo2:32 fo3:32")
-_declare("float32", "nd:32 ww:32 nlf:20 ss:416 sn:1248 nr:320 eq:320 scn:320")
+_declare("float32", "nd:80 ww:96 nlf:20 ss:416 sn:1248 nr:320")
 _declare("float32", "dq:20 ad:20 inv0:432 inv1:432 dg0:416 dg1:416 dm:26 xf:512 ysb:320")
 _declare("float32", "ps0:512 ps1:512 ps2:512 ps3:512 ps4:512 ps5:512 ps6:512 ps7:512")
-SEMAPHORES = "cv cs ct cg lx0 lx1 llr lb lc lu lv lw ka kb ta tb ob bl rtl ba0 ba1 ba2 ra0 ra1 ra2".split()
+SEMAPHORES = "cv cs ct cg lx0 lx1 llr lb lc lu lv lw ka kb t1 t2 t3 ob bl rtl ba0 ba1 ba2 ra0 ra1 ra2".split()
 
 
 def rank_program(g, core, T, topo):
@@ -150,6 +150,9 @@ def rank_program(g, core, T, topo):
         rd = [i] + [s for s in (off, scale, bias) if isinstance(s, dict)]
         op("s", lambda: g.scalar.activation(out["ap"], ia, func, scale=sv, bias=bv), [out], rd)
 
+    def lin(out, i, scale, bias):
+        act(out, i, AF.Identity, scale=scale, bias=bias)
+
     def quant(k, lo, hi, src):
         o, s = A("q" + k, lo, hi), A("s" + k, lo, hi)
         op("v", lambda: g.vector.quantize_mx(o["ap"], s["ap"], src["ap"]), [o, s], [src])
@@ -177,12 +180,16 @@ def rank_program(g, core, T, topo):
             i, o = A(name, a, b, bits=bits), A(name, c, c + b - a, bits=bits)
             op("g", lambda: g.remote_dma(o["ap"], i["ap"], T.sem[rsem], T.sem[lsem], pid, rid, mask), [], [i], sem=lsem, inc=n, self_inc=True)
 
-    def unpack(banks, lo, hi, who, skip=0):
+    def unpack(banks, lo, hi, skip=0):
         for b in range(4):
             mm(banks[b], "e", 128 * b, "c", lo, hi)
         for b in range(4):
-            o, i = A("vt", E * b + lo + skip, E * b + hi), P(banks[b], skip, hi - lo)
-            copy(o, i) if who[b] == "v" else act(o, i)
+            act(A("vt", E * b + lo + skip, E * b + hi), P(banks[b], skip, hi - lo))
+
+    def unpack_all():
+        unpack((2, 3, 4, 5), 0, 128)
+        unpack((0, 7, 2, 3), 128, 320)
+        unpack((2, 3, 4, 5), 288, 416, 32)
 
     def score(bank, lo, hi, skip=0):
         mm(bank, "0", 0, "c", lo, hi)
@@ -197,150 +204,159 @@ def rank_program(g, core, T, topo):
     def rows(t, gi):
         return t[16 * gi:16 * gi + 16, :]
 
+    def few(n):
+        return A("i32", 0, n)
+
     dma("y", "lx0", A("xt", 0, 512), T.x[:, 0:512])
     dma("s", "llr", A("lri", 0, 26), T.lf[:, :])
-    dma("y", "llr", A("lri", 26, 52, p=(0, 112)), T.lf[16:128, :])
     dma("s", "llr", A("lri", 52, 78, p=(16, 128)), T.rt[0:112, :])
-    dma("y", "llr", A("lri", 78, 104), T.rt[:, :])
-    dma("s", "llr", A("lri", 26, 52, p=(112, 128)), rows(T.lf, 0))
-    dma("y", "llr", A("lri", 52, 78, p=(0, 16)), rows(T.rt, 0))
-    dma("s", "lu", A("ut"), T.u[:, :])
+    dma("y", "llr", A("lri", 26, 52, p=(0, 112)), T.lf[16:128, :])
+    dma("s", "llr", A("lri", 78, 104), T.rt[:, :])
+    dma("y", "llr", A("lri", 26, 52, p=(112, 128)), rows(T.lf, 0))
+    dma("s", "llr", A("lri", 52, 78, p=(0, 16)), rows(T.rt, 0))
+    dma("y", "lu", A("ut"), T.u[:, :])
     dma("y", "lx1", A("xt", 512, 1280), T.x[:, 512:1280])
     pi = A("pi")
     op("g", lambda: g.iota(pi["ap"], [[0, 2]], 0, 1), [pi], [])
     iota(A("i32"), [[1, 32]])
     iota(A("iw"), [[1, 416]])
+    iota(A("win", 0, 832), [[0, 832]])
     fill(A("bli"), 0)
-    for t, gi, h, k in ((T.rt, 3, 1, 0), (T.lf, 2, 2, 0), (T.rt, 2, 3, 0), (T.lf, 3, 4, 0), (T.rt, 5, 0, 2), (T.rt, 7, 1, 2),
-                        (T.lf, 4, 2, 1), (T.rt, 4, 2, 2), (T.lf, 6, 3, 1), (T.rt, 6, 3, 2), (T.lf, 5, 4, 1), (T.lf, 7, 5, 1)):
-        dma("y", "lb", A("bli", 26 * k, 26 * k + 26, p=grp(h)), rows(t, gi))
-    dma("y", "lw", A("qw", bits=dt.uint8), T.wc[:, :])
-    dma("y", "lw", A("sw"), T.ws[:, :])
-    dma("y", "lv", A("vin"), T.v[:, :])
+    for s in (1, 2, 3):
+        for t, gi, h in ((T.rt, 2 * s + 1, 1), (T.lf, 2 * s, 2), (T.rt, 2 * s, 3), (T.lf, 2 * s + 1, 5)):
+            dma("y", "lb", A("bli", 26 * s - 26, 26 * s, p=grp(h)), rows(t, gi))
 
-    for i, bits in enumerate((15, 16, 3, 96, 4, 8, 6, 1, 120, 24)):
-        ts(A("pa", i, i + 1), A("pi", 0, 1), bits, ALU.bitwise_and)
+    def fields(lo, masks):
+        for i, bits in enumerate(masks):
+            ts(A("pa", lo + i, lo + i + 1), A("pi", 0, 1), bits, ALU.bitwise_and)
+    fields(0, (16, 3, 15))
     copy(K("p"), A("pi", 0, 1))
-    copy(A("pf"), A("pa"))
-    q, e16, m4, a32, g4, t8, p6, p1, p120, p24 = [A("pf", i, i + 1) for i in range(10)]
-
-    def few(n):
-        return A("i32", 0, n)
+    copy(A("pf", 0, 3), A("pa", 0, 3))
+    fields(3, (8, 96))
+    e16, m4, q, t8, a32, g4, p120, p24 = [A("pf", i, i + 1) for i in range(8)]
     d16 = A("cs", 32, 48)
-    ts(K("nl"), K("p"), 96.0, ALU.is_lt)
-    ts(K("sg"), e16, -0.125, M, 1.0, S)
-    ts(K("od3"), e16, 0.1875, M)
     ts(d16, few(16), q, ALU.subtract)
-    ts(K("e1"), m4, 3.0, EQ, e16, M)
-    ts(K("z"), m4, K("sg"), M, K("od3"), S)
+    ts(A("qrep"), few(26), 0.0, M, q, S)
     ts(A("cs", 48, 64), d16, 0.0, EQ, -4000.0, M)
     ts(A("cs", 64, 80), d16, 1.0, EQ, 2000.0, M)
+    ts(K("sg"), e16, -0.125, M, 1.0, S)
+    tt(A("cs", 16, 32), A("cs", 48, 64), A("cs", 64, 80), S)
+    act(A("dia"), A("cs", 16, 32), off=A("qrep"))
+    ts(K("od3"), e16, 0.1875, M)
+    ts(K("nl"), K("p"), 96.0, ALU.is_lt)
+    ts(K("z"), m4, K("sg"), M, K("od3"), S)
+    ts(K("e1"), m4, 3.0, EQ, e16, M)
     ts(K("z2"), K("z"), K("sg"), S)
     ts(A("cf", 0, 4), few(4), K("z"), EQ)
-    ts(A("qrep"), few(26), 0.0, M, q, S)
     ts(A("cf", 4, 8), few(4), K("z2"), EQ)
-    tt(A("cs", 16, 32), A("cs", 48, 64), A("cs", 64, 80), S)
     ts(K("eps"), K("e1"), 26.0, M, K("nl"), M)
     tt(A("cf", 8, 12), A("cf", 0, 4), A("cf", 4, 8), ALU.subtract)
-    act(A("dia"), A("cs", 16, 32), off=A("qrep"))
     ts(K("od"), e16, 0.0625, M)
     ts(A("cf", 12, 16), A("cf", 8, 12), K("nl"), M)
+    act(A("biw"), A("iw"), scale=A("cf", 10, 11))
+    act(A("aiw"), A("iw"), scale=A("cf", 13, 14))
+    lin(A("base"), A("iw"), A("cf", 15, 16), K("eps"))
     ts(K("ev"), e16, -0.0625, M, 1.0, S)
     ts(K("ub"), e16, -256.0, M, 4096.0, S)
-    act(A("aiw"), A("iw"), scale=A("cf", 13, 14))
-    act(A("base"), A("iw"), AF.Identity, scale=A("cf", 15, 16), bias=K("eps"))
-    act(A("biw"), A("iw"), scale=A("cf", 10, 11))
-    ts(K("r1"), p6, 2.0, ALU.not_equal, 16.0, M)
-    ts(K("r2"), p1, 32.0, M, 32.0, S)
-    ts(K("r3"), t8, 0.0, EQ)
-    ts(K("r5"), q, 14.0, EQ, -48.0, M)
-    ts(K("r6"), q, 15.0, EQ, -32.0, M)
-    ts(K("r4"), K("r2"), K("r3"), M, 32.0, S)
-    ts(K("r7"), K("r1"), K("r5"), S, K("r6"), S)
-    ts(K("hs"), q, 15.0, ALU.is_lt, 2000.0, M)
-    ts(K("r8"), K("r4"), K("r7"), S)
+    fields(5, (4, 120, 24))
+    copy(A("pf", 3, 8), A("pa", 3, 8))
     quant("c", 0, 128, A("xt", 0, 512))
     border_out(0)
-    iota(A("offs"), [[416, 2], [0, 4]])
+    ts(A("lsa"), A("lri", 0, 52), K("ev"), M)
+    ts(A("lsb"), A("lri", 52, 104), K("od"), M)
+    ts(K("r1"), m4, 32.0, M, 48.0, S)
+    tt(A("lsc"), A("lsa"), A("lsb"), S)
+    ts(K("r2"), m4, 3.0, EQ, -128.0, M)
+    copy(A("lru"), A("lsc"))
     iota(A("zb"), [[0, 516]])
     eb, zb = A("eb"), A("zb")
     op("g", lambda: g.affine_select(eb["ap"], zb["ap"], [[1, 516]], ALU.not_equal, 1.0, -3, -4), [eb], [zb])
-    for n in ("ra", "rb", "ub"):
+    iota(A("offs"), [[416, 2], [0, 4]])
+    for n in ("rb", "dg", "ra", "ub"):
         iota(A(n), [[0, T[n].shape[1]]])
-    ts(A("lsa"), A("lri", 0, 52), K("ev"), M)
-    ts(A("lsb"), A("lri", 52, 104), K("od"), M)
-    ts(A("lz"), few(8), 0.0, M, K("r8"), S)
-    tt(A("lsc"), A("lsa"), A("lsb"), S)
-    copy(A("lru"), A("lsc"))
     l1, l2 = A("lru", 0, 26), A("lru", 26, 52)
     act(A("r2"), A("iw"), off=l2)
     tt(A("t1"), A("aiw"), A("base"), S, off=l1)
     act(A("gr2"), A("r2"), scale=A("cf", 8, 9))
-    act(A("rc"), A("r2"), off=l1)
-    quant("u", 0, 128, A("ut"))
-    tt(A("t2"), A("biw"), A("t1"), S, off=l2)
     act(A("ur"), A("iw"), AF.Identity, bias=K("ub"), off=l1)
-    pick(A("q0", bits=dt.uint32), A("qu", bits=dt.uint32), A("lz"))
+    ts(K("r3"), t8, -2.0, M, K("r1"), S)
+    tt(A("t2"), A("biw"), A("t1"), S, off=l2)
+    act(A("rc"), A("r2"), off=l1)
+    ts(K("r4"), K("r3"), K("r2"), S)
     tt(A("t3"), A("gr2"), A("t2"), S, off=l1)
-    phase = (2, 0, 0, 2)
+    phase, region = (2, 0, 0, 2), (0, 0, 832, 832)
 
-    def lay(qs, src, s, cls, all16=True):
+    def lay(src, s, cls, all16=True):
         for side in (0, 1):
-            gi, lo = 2 * s + side, 832 * (s // 2) + 416 * side
+            gi, lo = 2 * s + side, region[s] + 416 * side
             for dst, p in ([((cls + 64 * z, 64 * z + 64, 4), grp(gi)) for z in (0, 1)] if all16 else [((cls, 128, 16), (16 * gi, 16 * gi + 8))]):
-                dma(qs[side], "ka" if s < 2 else "kb", A("win", lo, lo + 416, p=dst), A(src, p=p))
+                dma("y", "kb" if s else "ka", A("win", lo, lo + 416, p=dst), A(src, p=p))
+
+    def lay_stage(s):
+        lay("ur", s, phase[s] + 1, False)
+        lay("t3", s, phase[s])
+    lay_stage(0)
+    ts(K("hs"), q, 15.0, ALU.is_lt, 2000.0, M)
+    ts(A("lz"), few(8), 0.0, M, K("r4"), S)
+    quant("u", 0, 128, A("ut"))
     scan(A("dg0"), A("dia"), A("rc"), S, ALU.max)
-    for s in (0, 1):
-        lay("yy", "t3", s, phase[s])
-        lay("ss", "ur", s, phase[s] + 1)
+    ts(K("w0"), q, 112.0, S)
+    ts(A("cpi"), A("dg0", 15, 416, 16), K("hs"), ALU.subtract)
+    for s in (1, 2, 3):
+        for side in (0, 1):
+            dma("y", "lc", A("bli", 26 * s - 26, 26 * s, p=grp(6 * side)), A("cpi", p=grp(2 * s + side)))
+    for s in (2, 3):
+        lay_stage(s)
+    dma("y", "lw", A("qw", bits=dt.uint8), T.wc[:, :])
+    dma("y", "lw", A("sw"), T.ws[:, :])
+    dma("y", "lv", A("vin"), T.v[:, :])
+    lin(K("b0"), K("p"), 2.0, 0.0)
+    lin(K("b2"), a32, 0.5, q)
+    lin(K("b4"), a32, 1.0, K("p"))
+    lin(K("b0"), q, -1.0, K("b0"))
+    lin(K("b3"), K("b2"), 1.0, 256.0)
+    lin(K("b5"), K("b4"), 1.0, 32.0)
+    lin(K("b1"), K("b0"), 1.0, 16.0)
+    for i, b in enumerate(("b0", "b1", "b3", "b3", "b4", "b5", "b3", "b3")):
+        lo = 8 * (i // 4)
+        lin(A("l0f", lo + i % 4, lo + 8, 4), few(2), 416.0, K(b))
+    ts(A("wr", 0, 960, 4), A("iw", 0, 240), K("w0"), EQ)
+    pick(A("q0", bits=dt.uint32), A("qu", bits=dt.uint32), A("lz"))
     s0, su, lz = A("s0"), A("su"), A("lz")
     op("s", lambda: g.scalar.activation(s0["ap"], su["ap"].indirect(lz["ap"]), AF.Copy), [s0], [su, lz])
     quant("c", 128, 320, A("xt", 512, 1280))
-    ts(A("cpi"), A("dg0", 15, 416, 16), K("hs"), ALU.subtract)
-    for gi, h, k in ((2, 0, 0), (3, 5, 0), (4, 0, 1), (5, 4, 2), (6, 1, 1), (7, 5, 2)):
-        dma("y", "lc", A("bli", 26 * k, 26 * k + 26, p=grp(h)), A("cpi", p=grp(gi)))
-    for s in (2, 3):
-        lay("yy", "t3", s, phase[s])
-        lay("yy", "ur", s, phase[s] + 1, False)
     score(0, 0, 128)
     score(6, 128, 320)
-    ts(K("b0"), K("p"), 2.0, M, q, ALU.subtract)
-    ts(K("b2"), a32, 0.5, M, q, S)
-    ts(K("b4"), K("p"), a32, S)
-    ts(K("b1"), K("b0"), 16.0, S)
-    ts(K("b3"), K("b2"), 256.0, S)
-    ts(K("b5"), K("b4"), 32.0, S)
-    for i, b in enumerate(("b0", "b1", "b3", "b3", "b4", "b5", "b3", "b3")):
-        lo = 8 * (i // 4)
-        ts(A("l0", lo + i % 4, lo + 8, 4), few(2), 416.0, M, K(b), S)
-    ts(K("c0"), g4, 32.0, M, m4, S)
-    ts(K("c1"), e16, 0.25, M, t8, S)
-    ts(K("c2"), p24, 2.0, M, 64.0, S)
-    ts(K("c3"), p120, 0.5, M, K("c0"), S)
-    ts(K("c4"), a32, 0.5, M, K("c0"), S)
-    ts(K("c5"), a32, 0.125, M, K("c0"), S)
-    ts(K("c6"), K("c3"), 256.0, S)
-    ts(K("c7"), K("c4"), K("c1"), S)
-    ts(K("c8"), K("c5"), K("c2"), S)
-    ts(A("rl", 2, 8, 4), few(2), -256.0, M, K("c6"), S)
-    ts(A("rl", 0, 8, 4), few(2), 512.0, M, K("c7"), S)
-    ts(A("rl", 1, 6, 2), few(3), 256.0, M, K("c8"), S)
-    copy(A("rl", 7, 8), K("c8"))
-    fill(A("bt0", 0, 32, 4), 0.0)
-    fill(A("dg"), 0)
-    for lo, hi, st, c in ((0, 16, 2, 1.0), (16, 32, 2, -1.0), (1, 16, 4, -1.0), (17, 32, 2, 1.0), (3, 16, 4, 0.0)):
-        fill(A("pat", lo, hi, st), c)
-    ts(K("w0"), q, 112.0, S)
-    pick(A("g0", 0, 256), A("win", 0, 832), A("l0"))
-    ts(A("wr", 0, 960, 4), A("iw", 0, 240), K("w0"), EQ)
-    turn(A("ts0"), A("g0", 0, 256))
     for t in (1, 2, 3):
         act(A("wr", t, 960, 4), A("wr", 0, 960, 4))
+    lin(A("bt0", 0, 32, 4), few(8), 0.0, 0.0)
+    for lo, hi, st, c in ((0, 16, 2, 1.0), (16, 32, 2, -1.0), (1, 16, 4, -1.0), (17, 32, 2, 1.0), (3, 16, 4, 0.0)):
+        lin(A("pat", lo, hi, st), few(16 // st), 0.0, c)
+
+    def digit_places():
+        lin(K("c0"), g4, 32.0, m4)
+        lin(K("c1"), e16, 0.25, t8)
+        lin(K("c2"), p24, 2.0, 64.0)
+        lin(K("c3"), p120, 0.5, K("c0"))
+        lin(K("c4"), a32, 0.5, K("c0"))
+        lin(K("c5"), a32, 0.125, K("c0"))
+        lin(K("c6"), K("c3"), 1.0, 256.0)
+        lin(K("c7"), K("c4"), 1.0, K("c1"))
+        lin(A("rlf", 7, 8), K("c5"), 1.0, K("c2"))
+        lin(A("rlf", 2, 8, 4), few(2), -256.0, K("c6"))
+        lin(A("rlf", 0, 8, 4), few(2), 512.0, K("c7"))
+        lin(A("rlf", 1, 6, 2), few(3), 256.0, A("rlf", 7, 8))
+    copy(A("l0"), A("l0f"))
+    for b in range(4):
+        quant("e", 128 * b, 128 * b + 128, A("eb", 3 - b, 515 - b))
+    pick(A("g0", 0, 256), A("win", 0, 832), A("l0"))
+    lay_stage(1)
+    turn(A("ts0"), A("g0", 0, 256))
     v = [A("ts0", 128 + 14 - 4 * i, 256, 16) for i in range(4)]
-    copy(A("bl"), A("bli"))
     tt(A("sums", 0, 8), v[0], v[1], S)
     ts(A("lab", 20, 24), A("ts0", 192 + 14, 256, 16), 416.0, ALU.subtract)
     tt(A("sums", 8, 16), A("sums", 0, 8), v[2], S)
+    copy(A("bl"), A("bli"))
     copy(A("lab", 8, 12), A("sums", 0, 4))
     ts(A("lab", 16, 20), A("sums", 4, 8), 416.0, ALU.subtract)
     tt(A("sums", 16, 20), A("sums", 8, 12), A("ts0", 128 + 2, 192, 16), S)
@@ -349,61 +365,54 @@ def rank_program(g, core, T, topo):
     copy(A("lab", 0, 4), A("sums", 16, 20))
 
     def later_constants():
-        yield lambda: quant("k", 0, 240, A("wr"))
-        yield lambda: quant("b", 128, 288, A("rb", 512, 1152))
-        for b in range(4):
-            yield lambda b=b: quant("e", 128 * b, 128 * b + 128, A("eb", 3 - b, 515 - b))
         yield lambda: quant("a", 32, 160, A("ra", 128, 640))
-
-        def scans():
-            ts(A("cs", 80, 96), few(16), 0.0, ALU.is_gt)
-            ts(A("cs", 48, 64), d16, 0.0, EQ, 63.0, M)
-            copy(A("cidx"), few(20))
-            ts(A("cs", 64, 80), A("cs", 48, 64), 1.0, S)
-            ts(K("q4"), q, 416.0, S)
-            tt(A("cs", 0, 16), A("cs", 64, 80), A("cs", 80, 96), M)
-        yield scans
+        yield lambda: ts(A("cs", 80, 96), few(16), 0.0, ALU.is_gt)
+        yield lambda: ts(A("cs", 48, 64), d16, 0.0, EQ, 63.0, M)
+        yield lambda: copy(A("cidx"), few(20))
+        yield lambda: ts(A("cs", 64, 80), A("cs", 48, 64), 1.0, S)
+        yield lambda: ts(K("q4"), q, 416.0, S)
+        yield lambda: tt(A("cs", 0, 16), A("cs", 64, 80), A("cs", 80, 96), M)
 
         def rest():
-            unpack((2, 3, 4, 5), 0, 128, "ssss")
-            unpack((0, 7, 2, 3), 128, 320, "ssss")
-            unpack((2, 3, 4, 5), 288, 416, "ssss", 32)
             act(A("dsc"), A("cs", 0, 16), off=A("qrep", 0, 20))
             for b in range(4):
                 act(A("tt", 336 * b + 320, 336 * b + 336), few(16), scale=0.0)
             quant("r", 224, 352, A("ub"))
         yield rest
 
+    def tables(s):
+        act(A("sn", 416 * s - 416, 416 * s), A("ss"), off=A("bl", 26 * s - 26, 26 * s))
+        for h in range(8):
+            c = 16 * h + phase[s] + 5
+            dma("y", "t%d" % s, A("win", region[s], region[s] + 832, p=(c, c + 9, 4)), A("sn", 416 * s - 416, 416 * s, p=(s - 1, s + 100, 20)))
+
     def carry(gi):
         x, lo = ("a", 32 * (gi - 6)) if gi > 5 else ("b", 32 * gi)
         mm(1, "k", 112 - 16 * gi, x, lo, lo + 128, gi == 0, gi == 7)
 
-    def digits(s):
+    def digits(lo, s):
         for i, bits in enumerate((15, 240, 256)):
-            yield lambda i=i, bits=bits: ts(A("dg", 32 * s + i, 32 * s + 32, 4), A("ni", 8 * s, 8 * s + 8), bits, ALU.bitwise_and)
-        yield lambda: put(A("ra" if s == 3 else "rb"), A("rl", 2 * s, 2 * s + 2), A("dg", 32 * s, 32 * s + 32))
+            yield lambda i=i, bits=bits: ts(A("dg", 32 * lo + i, 32 * s + 32, 4), A("ni", 8 * lo, 8 * s + 8), bits, ALU.bitwise_and)
+        yield lambda: put(A("ra" if s == 3 else "rb"), A("rl", 2 * lo, 2 * s + 2), A("dg", 32 * lo, 32 * s + 32))
 
     def first_choice(s, tr):
-        bt, u, n = "bt%d" % s, phase[s] + 1, 24 * (s == 3)
+        bt, u, n = "bt%d" % s, phase[s] + 1, 8 * s
         yield lambda: tt(A("nd", n, n + 4), A(tr, u, 64, 16), A(tr, 64 + u, 128, 16), ALU.subtract)
         yield lambda: tt(A("nd", n + 4, n + 8), A("nd", n, n + 4), A(bt, 2, 16, 4), M)
         yield lambda: tt(A("ni", 8 * s, 8 * s + 8, 2), A("nd", n + 4, n + 8), A(tr, 64 + u, 128, 16), S)
 
-    def choices(s, tr):
-        bt, fo = "bt%d" % s, "fo%d" % s
-        f = list(first_choice(s, tr))
-        yield f[0]
-        yield lambda: scan(A("ww"), A(bt), A("pat"), M, S)
-        yield lambda: tt(A("nd", 8, 16), A(fo, 3, 32, 4), A("offs"), ALU.subtract)
-        yield f[1]
-        yield lambda: tt(A("nd", 16, 24), A("nd", 8, 16), A("ww", 3, 32, 4), M)
-        yield f[2]
-        yield lambda: tt(A("ni", 8 * s + 1, 8 * s + 8, 2), A("nd", 16, 20), A("nd", 20, 24), S)
-        yield from digits(s)
-        if s:
+    def second_choice(s):
+        bt, fo, n = "bt%d" % s, "fo%d" % s, 32 + 16 * s
+        yield lambda: scan(A("ww", 32 * s, 32 * s + 32), A(bt), A("pat"), M, S)
+        yield lambda: tt(A("nd", n, n + 8), A(fo, 3, 32, 4), A("offs"), ALU.subtract)
+        yield lambda: tt(A("nd", n + 8, n + 16), A("nd", n, n + 8), A("ww", 32 * s + 3, 32 * s + 32, 4), M)
+        yield lambda: tt(A("ni", 8 * s + 1, 8 * s + 8, 2), A("nd", n + 8, n + 12), A("nd", n + 12, n + 16), S)
+        if s != 1:
+            yield from digits(s // 2, s)
+
             def out():
-                quant("b", 128 * s - 128, 128 * s, A("rb", 512 * s - 512, 512 * s))
-                for gi in range(0, 4) if s == 1 else (4, 5):
+                quant("b", 32 * s, 32 * s + 128, A("rb", 128 * s, 128 * s + 512))
+                for gi in range(2, 6) if s else (0, 1):
                     carry(gi)
             yield out
 
@@ -421,44 +430,82 @@ def rank_program(g, core, T, topo):
                 pick(A("g0"), A("ss"), A("lab"))
                 turn(A("tr0"), A("g0"))
                 for side in (0, 1):
-                    for k, cls in enumerate((15, 14, 15)):
+                    for k, cls in enumerate((3, 11, 3)):
                         c = 64 * k + cls
                         tt(A(bt, 16 * side + k + 1, 16 * side + 16, 4), A("tr0", c, 64 * k + 64, 16), A("tr0", 192 + c, 256 + 64 * k, 16), ALU.is_le)
             else:
                 tr = "tr%d" % s
-                lo = 832 * (s // 2)
-                pick(A("gt"), A("win", lo, lo + 832), A("ll"))
+                pick(A("gt"), A("win", region[s], region[s] + 832), A("ll"))
                 gap(2)
                 turn(A(tr), A("gt"))
                 gap(2)
                 for side in (0, 1):
                     tt(A(bt, 16 * side, 16 * side + 16), A(tr, ph + 1, 64, 4), A(tr, 64 + ph + 1, 128, 4), ALU.is_le)
-            f = list(first_choice(3, tr)) if s == 3 else None
-            f[0]() if f else gap()
+            f = list(first_choice(s, tr))
+            f[0]()
             gap()
             tt(A(bt, 3, 32, 4), A(bt, 2, 32, 4), A(bt, 3, 32, 4), ALU.max)
-            f[1]() if f else gap()
+            f[1]()
             gap()
             scan(A(fo), A(bt), A(tr, ph, 128, 4), M, S)
-            f[2]() if f else gap()
-            gap()
+            f[2]()
             if s < 3:
                 copy(A("ll"), A(fo, 3, 32, 4))
-                todo.extend(choices(s, tr))
+                if s == 0 and r == 0:
+                    quant("k", 0, 240, A("wr"))
+                    quant("b", 128, 288, A("rb", 512, 1152))
+                todo.extend(second_choice(s))
+                if s == 0 and r == 0:
+                    todo.insert(7, lambda: copy(A("rl"), A("rlf")))
                 if s == 0:
-                    gap(len(todo))
+                    gap(8)
                     if r == 0:
                         todo.extend(later_constants())
+                    if r == 1:
+                        quant("v", 0, 128, A("vin"))
                 gap()
             else:
                 tt(A("ni", 25, 32, 2), A(fo, 3, 16, 4), A(fo, 19, 32, 4), S)
                 gap(len(todo))
-                for f in digits(3):
+                for f in digits(3, 3):
                     f()
                 quant("a", 0, 128, A("ra", 0, 512))
                 carry(6)
                 carry(7)
                 copy(A("nl"), P(1, 0, 20))
+
+    def take(t, z):
+        o, i, l = A("mt", 640 * z + t, 640 * z + 640, 4), A("vt", E * t, E * t + E), A("nl", 10 * z, 10 * z + 10)
+        pick(o, i, l) if t < 2 else act(o, i, off=l)
+
+    def layer(z):
+        quant("m", 160 * z, 160 * z + 160, A("mt", 640 * z, 640 * z + 640))
+        for b in range(4):
+            mm(4 * z + b, "w", 128 * b, "m", 160 * z, 160 * z + 160)
+        for b in range(4):
+            act(A("tb", 640 * z + b, 640 * z + 640, 4), P(4 * z + b, 0, 160), scale=0.03125)
+
+    def unpack_t(z):
+        quant("t", 160 * z, 160 * z + 160, A("tb", 640 * z, 640 * z + 640))
+        for b in range(4):
+            mm(4 * z + b, "e", 128 * b, "t", 160 * z, 160 * z + 160)
+        for b in range(4):
+            act(A("tt", 336 * b + 160 * z, 336 * b + 160 * z + 160), P(4 * z + b, 0, 160), scale=-1.0)
+
+    def lists(lo, hi, out):
+        for k in (1, 0):
+            scan(A("dg%d" % k, lo, hi), A("dia", lo, hi), A("inv%d" % k, lo, hi), S, ALU.max)
+        m = A("dm", lo // 16, hi // 16)
+        tt(m, A("dg0", lo + 15, hi, 16), A("dg1", lo + 15, hi, 16), ALU.min)
+        ts(out, m, K("hs"), ALU.subtract)
+
+    def minus(t):
+        return A("tt", 336 * t, 336 * t + 336)
+
+    def rest():
+        for t in range(4):
+            tt(A("xt", 512 + t, 1280, 4), minus(t), A("vt", E * t + 128, E * t + C), S, off=A("ul", 8, 20))
+        quant("c", 128, 320, A("xt", 512, 1280))
 
     n_in_b = 2 * len(topo.engines(nxt, core))
     n_in_r = 2 * len(topo.engines(prv, core))
@@ -466,58 +513,35 @@ def rank_program(g, core, T, topo):
         last = r == ROUNDS - 1
         arrive("ba%d" % r, n_in_b, [A("qc", C, E), A("sc", C, E)])
         score(6, 288, 416, 32)
-        pick(A("sn", 0, 416), A("ss"), A("bl", 0, 26))
-        act(A("sn", 416, 1248), A("ss"), off=A("bl", 26, 78))
-        for h in range(8):
-            dma("y", "ta", A("win", 0, 832, p=(16 * h + 5, 16 * h + 14, 4)), A("sn", 0, 416, p=(8, 94, 17)))
-        for h in range(8):
-            dma("ys"[h % 2], "tb", A("win", 832, 1664, p=(16 * h + 5, 16 * h + 16, 2)), A("sn", 416, 1248, p=(0, 86, 17)))
-        if r:
-            unpack((2, 3, 4, 5), 0, 128, "ssss")
-            unpack((0, 7, 2, 3), 128, 320, "ssss")
-            unpack((2, 3, 4, 5), 288, 416, "ssss", 32)
+        for s in (1, 2, 3):
+            tables(s)
+        if r == 0:
+            digit_places()
+        unpack_all()
         for k in range(2):
             iota(A("inv%d" % k), [[0, 432]], base=320)
         growth(r)
-        for t in (2, 3):
-            act(A("mt", t, 1280, 4), A("vt", E * t, E * t + E), off=A("nl"))
         act(A("nr"), A("iw"), off=A("nl"))
-        for t in (0, 1):
-            pick(A("mt", t, 1280, 4), A("vt", E * t, E * t + E), A("nl"))
-        copy(A("nlf"), A("nl"))
-        quant("m", 0, 320, A("mt"))
-        hb = (0, 1, 6, 7)
-        for b in range(4):
-            mm(hb[b], "w", 128 * b, "m", 0, 320)
-        for b in range(4):
-            act(A("tb", b, 1280, 4), P(hb[b], 0, 320), scale=0.03125)
+        for z in (0, 1):
+            for t in (2, 3, 0, 1):
+                take(t, z)
+            if z == 0:
+                copy(A("nlf"), A("nl"))
         tt(A("eq"), A("nlf"), A("nr"), EQ, off=A("cidx"))
+        layer(0)
         if last:
             dma("y", "ob", T.on[:, :], A("nr", p=(0, 128, 16)))
         scan(A("scn"), A("dsc"), A("eq"), M, S)
+        layer(1)
         ts(A("dq"), A("scn", 15, 320, 16), 32.0, ALU.is_ge, K("q4"), M)
         tt(A("ad"), A("nlf"), A("dq"), ALU.max)
         copy(A("adr", 0, 40, 2), A("ad"))
         for c in range(9, -1, -1):
-            if c == 6:
-                quant("t", 0, 320, A("tb"))
-                for b in range(4):
-                    mm(2 + b, "e", 128 * b, "t", 0, 320)
-                for b in range(4):
-                    act(A("tt", 336 * b, 336 * b + 320), P(2 + b, 0, 320), scale=-1.0)
+            if c in (6, 3):
+                unpack_t(c == 3)
             for k in (1, 0):
                 d = 10 * k + c
                 put(A("inv%d" % k), A("adr", 2 * d, 2 * d + 1), A("iw", 16 * d, 16 * d + 16))
-
-        def lists(lo, hi, out):
-            for k in (1, 0):
-                scan(A("dg%d" % k, lo, hi), A("dia", lo, hi), A("inv%d" % k, lo, hi), S, ALU.max)
-            m = A("dm", lo // 16, hi // 16)
-            tt(m, A("dg0", lo + 15, hi, 16), A("dg1", lo + 15, hi, 16), ALU.min)
-            ts(out, m, K("hs"), ALU.subtract)
-
-        def minus(t):
-            return A("tt", 336 * t, 336 * t + 336)
         lists(C, E, A("ulb"))
         for t in (2, 3):
             act(A("ub", t, 384, 4), minus(t), scale=-1.0, off=A("ulb"))
@@ -525,24 +549,19 @@ def rank_program(g, core, T, topo):
             ts(A("ub", t, 384, 4), minus(t), -1.0, M, off=A("ulb"))
         quant("r", 0, 128, A("ub"))
         send(nxt, "r", 0, H, 128, "ra%d" % r, "rtl")
-
-        def rest():
-            for t in range(4):
-                tt(A("xt", 512 + t, 1280, 4), minus(t), A("vt", E * t + 128, E * t + C), S, off=A("ul", 8, 20))
-            quant("c", 128, 320, A("xt", 512, 1280))
         lists(0, C, A("ul"))
         for t in range(4):
             tt(A("xf", 128 * t, 128 * t + 128), minus(t), A("vt", E * t, E * t + 128), S, off=A("ul", 0, 8))
         if last:
             rest()
-            quant("v", 0, 128, A("vin"))
-            mm(6, "v", 0, "c", 128, 320)
-            act(A("ysb", 128, 320), P(6, 0, 192))
-            dma("y", "ob", T.y[:, 128:320], A("ysb", 128, 320))
         arrive("ra%d" % r, n_in_r, [A("qr", 128, 224), A("sr", 128, 224)])
         bb = (0, 1, 7, 2)
         for b in range(4):
             mm(bb[b], "e", 128 * b, "r", 128, 256)
+        if last:
+            mm(6, "v", 0, "c", 128, 320)
+            act(A("ysb", 128, 320), P(6, 0, 192))
+            dma("y", "ob", T.y[:, 128:320], A("ysb", 128, 320))
         for b in range(4):
             tt(A("xt", b, 512, 4), A("xf", 128 * b, 128 * b + 128), P(bb[b], 0, 128), ALU.subtract)
         quant("c", 0, 128, A("xt", 0, 512))

@@ -11,18 +11,18 @@ def _declare(kind, names):
         SCRATCH[n] = ("psum" if n.startswith("ps") else "sbuf", [128, int(c)], kind)
 
 
-_declare("bfloat16", "xt:1280 ut:512 vin:512 zb:516 eb:516 vt:1664 mt:1280 tb:1280 tt:1344 ub:512 wr:960 ra:640 rb:1152 dsc:320 eq:320 scn:320")
-_declare("int32", "lri:104 bli:78 cpi:26 pi:2 pa:8 ni:32 dg:128")
-_declare("uint16", "lru:52 bl:78 l0:16 ll:8 cidx:20 nl:20 qrep:26 adr:40 ul:20 ulb:6 lz:8 lab:24 rl:8")
-_declare("float8_e4m3fn_x4", "qw:512 qu:128 q0:128 qv:128 qe:512 qc:416 qm:320 qt:320 qr:352 qa:160 qb:288 qk:240")
-_declare("uint8", "sw:512 su:128 s0:128 sv:128 se:512 sc:416 sm:320 st:320 sr:352 sa:160 sb:288 sk:240")
-_declare("float32", "i32:32 iw:416 cs:96 dia:416 offs:8 pf:8 kk:64 cf:16 lsa:52 lsb:52 lsc:52 l0f:16 rlf:8")
-_declare("float32", "aiw:416 biw:416 base:416 gr2:416 r2:416 ur:416 rc:416 t1:416 t2:416 t3:416 win:1664 sums:24 pat:32")
+_declare("bfloat16", "xt:1280 ut:512 vin:512 zb:516 eb:516 vt:1664 mt:1280 tb:1280 tt:1344 ub:512 wr:896 ra:640 rb:640 dsc:320 eq:320 scn:320")
+_declare("int32", "lri:104 bli:78 cpi:26 pi:2 pa:6 ni:32 lo5:32 dg:64")
+_declare("uint16", "lru:52 bl:78 l0:16 ll:8 cidx:20 nl:20 qrep:26 qrep2:52 adr:20 ul:20 ulb:6 lz:8 lab:24 rl:4")
+_declare("float8_e4m3fn_x4", "qw:512 qu:128 q0:128 qv:128 qe:512 qc:416 qm:320 qt:320 qr:352 qa:160 qb:160 qk:224")
+_declare("uint8", "sw:512 su:128 s0:128 sv:128 se:512 sc:416 sm:320 st:320 sr:352 sa:160 sb:160 sk:224")
+_declare("float32", "i32:32 iw:416 cs:96 cs2:32 dia:416 dia2:832 back:320 offs:8 pf:6 kk:64 cf:16 ls:156 l0f:16 rlf:4")
+_declare("float32", "aiw:416 biw:416 base:416 gr2:416 r2:416 ur:416 rc:416 t1:416 t2:416 t3:416 win:2496 sums:24 pat:32")
 _declare("float32", "g0:384 tr0:384 ts0:256 gt:128 tr1:128 tr2:128 tr3:128 bt0:32 bt1:32 bt2:32 bt3:32 fo0:32 fo1:32 fo2:32 fo3:32")
 _declare("float32", "nd:80 ww:96 nlf:20 ss:416 sn:1248 nr:320")
-_declare("float32", "dq:20 ad:20 inv0:432 inv1:432 dg0:416 dg1:416 dm:26 xf:512 ysb:320")
+_declare("float32", "dq:20 ad:20 inv0:864 inv1:864 dg0:832 dg1:832 dm:26 xf:512 ysb:320")
 _declare("float32", "ps0:512 ps1:512 ps2:512 ps3:512 ps4:512 ps5:512 ps6:512 ps7:512")
-SEMAPHORES = "cv cs ct cg lx0 lx1 llr lb lc lu lv lw ka kb t1 t2 t3 ob bl rtl ba0 ba1 ba2 ra0 ra1 ra2".split()
+SEMAPHORES = "cv cs ct cg lx0 lx1 llr lb lc lu lv lw k0 k1 k2 k3 t1 t2 t3 ob bl rtl ba0 ba1 ba2 ra0 ra1 ra2".split()
 
 
 def rank_program(g, core, T, topo):
@@ -186,11 +186,6 @@ def rank_program(g, core, T, topo):
         for b in range(4):
             act(A("vt", E * b + lo + skip, E * b + hi), P(banks[b], skip, hi - lo))
 
-    def unpack_all():
-        unpack((2, 3, 4, 5), 0, 128)
-        unpack((0, 7, 2, 3), 128, 320)
-        unpack((2, 3, 4, 5), 288, 416, 32)
-
     def score(bank, lo, hi, skip=0):
         mm(bank, "0", 0, "c", lo, hi)
         act(A("ss", lo + skip, hi), P(bank, skip, hi - lo), AF.Abs)
@@ -226,6 +221,10 @@ def rank_program(g, core, T, topo):
         for t, gi, h in ((T.rt, 2 * s + 1, 1), (T.lf, 2 * s, 2), (T.rt, 2 * s, 3), (T.lf, 2 * s + 1, 5)):
             dma("y", "lb", A("bli", 26 * s - 26, 26 * s, p=grp(h)), rows(t, gi))
 
+    lin(A("bt0", 0, 32, 4), few(8), 0.0, 0.0)
+    for lo, hi, st, c in ((0, 16, 2, 1.0), (16, 32, 2, -1.0), (1, 16, 4, -1.0), (17, 32, 2, 1.0), (3, 16, 4, 0.0)):
+        lin(A("pat", lo, hi, st), few(16 // st), 0.0, c)
+
     def fields(lo, masks):
         for i, bits in enumerate(masks):
             ts(A("pa", lo + i, lo + i + 1), A("pi", 0, 1), bits, ALU.bitwise_and)
@@ -233,7 +232,7 @@ def rank_program(g, core, T, topo):
     copy(K("p"), A("pi", 0, 1))
     copy(A("pf", 0, 3), A("pa", 0, 3))
     fields(3, (8, 96))
-    e16, m4, q, t8, a32, g4, p120, p24 = [A("pf", i, i + 1) for i in range(8)]
+    e16, m4, q, t8, a32, g4 = [A("pf", i, i + 1) for i in range(6)]
     d16 = A("cs", 32, 48)
     ts(d16, few(16), q, ALU.subtract)
     ts(A("qrep"), few(26), 0.0, M, q, S)
@@ -249,67 +248,20 @@ def rank_program(g, core, T, topo):
     ts(K("z2"), K("z"), K("sg"), S)
     ts(A("cf", 0, 4), few(4), K("z"), EQ)
     ts(A("cf", 4, 8), few(4), K("z2"), EQ)
-    ts(K("eps"), K("e1"), 26.0, M, K("nl"), M)
+    ts(K("e2"), K("e1"), 26.0, M, K("nl"), M)
+    ts(K("e3"), K("p"), 96.0, ALU.is_ge, K("z"), M)
     tt(A("cf", 8, 12), A("cf", 0, 4), A("cf", 4, 8), ALU.subtract)
+    ts(K("e4"), K("e3"), 3.0, EQ, 16.0, M)
     ts(K("od"), e16, 0.0625, M)
+    ts(K("ev"), e16, -0.0625, M, 1.0, S)
     ts(A("cf", 12, 16), A("cf", 8, 12), K("nl"), M)
+    ts(K("eps"), K("e4"), K("ev"), M, K("e2"), S)
     act(A("biw"), A("iw"), scale=A("cf", 10, 11))
     act(A("aiw"), A("iw"), scale=A("cf", 13, 14))
     lin(A("base"), A("iw"), A("cf", 15, 16), K("eps"))
-    ts(K("ev"), e16, -0.0625, M, 1.0, S)
-    ts(K("ub"), e16, -256.0, M, 4096.0, S)
-    fields(5, (4, 120, 24))
-    copy(A("pf", 3, 8), A("pa", 3, 8))
-    quant("c", 0, 128, A("xt", 0, 512))
-    border_out(0)
-    ts(A("lsa"), A("lri", 0, 52), K("ev"), M)
-    ts(A("lsb"), A("lri", 52, 104), K("od"), M)
-    ts(K("r1"), m4, 32.0, M, 48.0, S)
-    tt(A("lsc"), A("lsa"), A("lsb"), S)
-    ts(K("r2"), m4, 3.0, EQ, -128.0, M)
-    copy(A("lru"), A("lsc"))
-    iota(A("zb"), [[0, 516]])
-    eb, zb = A("eb"), A("zb")
-    op("g", lambda: g.affine_select(eb["ap"], zb["ap"], [[1, 516]], ALU.not_equal, 1.0, -3, -4), [eb], [zb])
-    iota(A("offs"), [[416, 2], [0, 4]])
-    for n in ("rb", "dg", "ra", "ub"):
-        iota(A(n), [[0, T[n].shape[1]]])
-    l1, l2 = A("lru", 0, 26), A("lru", 26, 52)
-    act(A("r2"), A("iw"), off=l2)
-    tt(A("t1"), A("aiw"), A("base"), S, off=l1)
-    act(A("gr2"), A("r2"), scale=A("cf", 8, 9))
-    act(A("ur"), A("iw"), AF.Identity, bias=K("ub"), off=l1)
-    ts(K("r3"), t8, -2.0, M, K("r1"), S)
-    tt(A("t2"), A("biw"), A("t1"), S, off=l2)
-    act(A("rc"), A("r2"), off=l1)
-    ts(K("r4"), K("r3"), K("r2"), S)
-    tt(A("t3"), A("gr2"), A("t2"), S, off=l1)
-    phase, region = (2, 0, 0, 2), (0, 0, 832, 832)
-
-    def lay(src, s, cls, all16=True):
-        for side in (0, 1):
-            gi, lo = 2 * s + side, region[s] + 416 * side
-            for dst, p in ([((cls + 64 * z, 64 * z + 64, 4), grp(gi)) for z in (0, 1)] if all16 else [((cls, 128, 16), (16 * gi, 16 * gi + 8))]):
-                dma("y", "kb" if s else "ka", A("win", lo, lo + 416, p=dst), A(src, p=p))
-
-    def lay_stage(s):
-        lay("ur", s, phase[s] + 1, False)
-        lay("t3", s, phase[s])
-    lay_stage(0)
-    ts(K("hs"), q, 15.0, ALU.is_lt, 2000.0, M)
-    ts(A("lz"), few(8), 0.0, M, K("r4"), S)
-    quant("u", 0, 128, A("ut"))
-    scan(A("dg0"), A("dia"), A("rc"), S, ALU.max)
-    ts(K("w0"), q, 112.0, S)
-    ts(A("cpi"), A("dg0", 15, 416, 16), K("hs"), ALU.subtract)
-    for s in (1, 2, 3):
-        for side in (0, 1):
-            dma("y", "lc", A("bli", 26 * s - 26, 26 * s, p=grp(6 * side)), A("cpi", p=grp(2 * s + side)))
-    for s in (2, 3):
-        lay_stage(s)
-    dma("y", "lw", A("qw", bits=dt.uint8), T.wc[:, :])
-    dma("y", "lw", A("sw"), T.ws[:, :])
-    dma("y", "lv", A("vin"), T.v[:, :])
+    ts(K("ub"), e16, -256.0, M, 4112.0, S)
+    fields(5, (4,))
+    copy(A("pf", 3, 6), A("pa", 3, 6))
     lin(K("b0"), K("p"), 2.0, 0.0)
     lin(K("b2"), a32, 0.5, q)
     lin(K("b4"), a32, 1.0, K("p"))
@@ -317,41 +269,95 @@ def rank_program(g, core, T, topo):
     lin(K("b3"), K("b2"), 1.0, 256.0)
     lin(K("b5"), K("b4"), 1.0, 32.0)
     lin(K("b1"), K("b0"), 1.0, 16.0)
+    quant("c", 0, 128, A("xt", 0, 512))
+    border_out(0)
+    ts(A("cs", 80, 96), few(16), 0.0, ALU.is_gt)
+    ts(A("cs", 48, 64), d16, 0.0, EQ, 63.0, M)
+    copy(A("cidx"), few(20))
+    copy(A("qrep2", 0, 52, 2), A("qrep"))
+    ts(A("ls", 0, 52), A("lri", 0, 52), K("ev"), M)
+    ts(A("ls", 52, 104), A("lri", 52, 104), K("od"), M)
+    ts(K("r1"), m4, 32.0, M, 48.0, S)
+    tt(A("ls", 104, 156), A("ls", 0, 52), A("ls", 52, 104), S)
+    ts(K("r2"), m4, 3.0, EQ, -128.0, M)
+    copy(A("lru"), A("ls", 104, 156))
+    iota(A("zb"), [[0, 516]])
+    eb, zb = A("eb"), A("zb")
+    op("g", lambda: g.affine_select(eb["ap"], zb["ap"], [[1, 516]], ALU.not_equal, 1.0, -3, -4), [eb], [zb])
+    iota(A("offs"), [[416, 2], [0, 4]], base=-16)
+    iota(A("win", 832, 2496), [[0, 1664]])
+    for n in ("rb", "ra", "ub"):
+        iota(A(n), [[0, T[n].shape[1]]])
+    l1, l2 = A("lru", 0, 26), A("lru", 26, 52)
+    ts(A("cs", 64, 80), A("cs", 48, 64), 1.0, S)
+    act(A("r2"), A("iw"), off=l2)
+    tt(A("t1"), A("aiw"), A("base"), S, off=l1)
+    act(A("gr2"), A("r2"), scale=A("cf", 8, 9))
+    act(A("ur"), A("iw"), AF.Identity, bias=K("ub"), off=l1)
+    ts(K("r3"), t8, -2.0, M, K("r1"), S)
+    tt(A("cs", 0, 16), A("cs", 64, 80), A("cs", 80, 96), M)
+    tt(A("t2"), A("biw"), A("t1"), S, off=l2)
+    act(A("rc"), A("r2"), off=l1)
+    ts(K("r4"), K("r3"), K("r2"), S)
+    ts(A("qrep2", 1, 52, 2), A("qrep"), 16.0, S)
+    tt(A("t3"), A("gr2"), A("t2"), S, off=l1)
+    phase, region = (2, 0, 0, 0), (0, 0, 832, 1664)
+
+    def lay_stage(s):
+        c = phase[s]
+        for side in (0, 1):
+            gi, lo = 2 * s + side, region[s] + 416 * side
+            for src, dst, p in (("ur", (c + 1, 128, 16), (16 * gi, 16 * gi + 8)), ("t3", (c, 64, 4), grp(gi)), ("t3", (c + 64, 128, 4), grp(gi))):
+                dma("y", "k%d" % s, A("win", lo, lo + 416, p=dst), A(src, p=p))
+    lay_stage(0)
+    ts(K("hs"), q, 15.0, ALU.is_lt, 2000.0, M)
+    ts(A("lz"), few(8), 0.0, M, K("r4"), S)
+    quant("u", 0, 128, A("ut"))
+    scan(A("dg0", 0, 416), A("dia"), A("rc"), S, ALU.max)
+    ts(K("w0"), q, 96.0, S)
+    ts(A("cpi"), A("dg0", 15, 416, 16), K("hs"), ALU.subtract)
+    for s in (1, 2, 3):
+        for side in (0, 1):
+            dma("y", "lc", A("bli", 26 * s - 26, 26 * s, p=grp(6 * side)), A("cpi", p=grp(2 * s + side)))
+    dma("y", "lw", A("qw", bits=dt.uint8), T.wc[:, :])
+    dma("y", "lw", A("sw"), T.ws[:, :])
+    dma("y", "lv", A("vin"), T.v[:, :])
     for i, b in enumerate(("b0", "b1", "b3", "b3", "b4", "b5", "b3", "b3")):
         lo = 8 * (i // 4)
         lin(A("l0f", lo + i % 4, lo + 8, 4), few(2), 416.0, K(b))
-    ts(A("wr", 0, 960, 4), A("iw", 0, 240), K("w0"), EQ)
+    ts(A("wr", 0, 896, 4), A("iw", 0, 224), K("w0"), EQ)
     pick(A("q0", bits=dt.uint32), A("qu", bits=dt.uint32), A("lz"))
     s0, su, lz = A("s0"), A("su"), A("lz")
     op("s", lambda: g.scalar.activation(s0["ap"], su["ap"].indirect(lz["ap"]), AF.Copy), [s0], [su, lz])
+    lin(K("c0"), a32, 0.375, -64.0)
+    lin(K("c3"), a32, 0.125, m4)
+    lin(K("c7"), t8, -0.125, 1.0)
+    lin(K("c1"), g4, -3.0, K("c0"))
+    lin(K("c2"), g4, -2.0, K("c0"))
+    lin(K("c6"), g4, 4.0, K("c3"))
+    lin(K("c4"), e16, -1.5, K("c1"))
+    lin(K("c8"), e16, 2.0, K("c6"))
+    lin(K("c5"), e16, -1.75, K("c2"))
+    lin(K("c9"), K("c8"), 1.0, 64.0)
     quant("c", 128, 320, A("xt", 512, 1280))
     score(0, 0, 128)
+    lin(K("d0"), K("c4"), K("c7"), K("c9"))
+    lin(A("rlf", 0, 1), K("c5"), K("c7"), K("c9"))
+    lin(K("d1"), K("d0"), 1.0, 128.0)
     score(6, 128, 320)
-    for t in (1, 2, 3):
-        act(A("wr", t, 960, 4), A("wr", 0, 960, 4))
-    lin(A("bt0", 0, 32, 4), few(8), 0.0, 0.0)
-    for lo, hi, st, c in ((0, 16, 2, 1.0), (16, 32, 2, -1.0), (1, 16, 4, -1.0), (17, 32, 2, 1.0), (3, 16, 4, 0.0)):
-        lin(A("pat", lo, hi, st), few(16 // st), 0.0, c)
-
-    def digit_places():
-        lin(K("c0"), g4, 32.0, m4)
-        lin(K("c1"), e16, 0.25, t8)
-        lin(K("c2"), p24, 2.0, 64.0)
-        lin(K("c3"), p120, 0.5, K("c0"))
-        lin(K("c4"), a32, 0.5, K("c0"))
-        lin(K("c5"), a32, 0.125, K("c0"))
-        lin(K("c6"), K("c3"), 1.0, 256.0)
-        lin(K("c7"), K("c4"), 1.0, K("c1"))
-        lin(A("rlf", 7, 8), K("c5"), 1.0, K("c2"))
-        lin(A("rlf", 2, 8, 4), few(2), -256.0, K("c6"))
-        lin(A("rlf", 0, 8, 4), few(2), 512.0, K("c7"))
-        lin(A("rlf", 1, 6, 2), few(3), 256.0, A("rlf", 7, 8))
+    lin(A("rlf", 1, 4), few(3), 0.0, K("d1"))
+    act(A("wr", 1, 896, 4), A("wr", 0, 896, 4))
+    for t in (2, 3):
+        act(A("wr", t, 64, 4), A("wr", 0, 64, 4))
+        act(A("wr", 64 + t, 896, 4), A("wr", 0, 832, 4))
     copy(A("l0"), A("l0f"))
     for b in range(4):
         quant("e", 128 * b, 128 * b + 128, A("eb", 3 - b, 515 - b))
-    pick(A("g0", 0, 256), A("win", 0, 832), A("l0"))
+    pick(A("g0", 128, 256), A("win", 0, 832), A("l0", 8, 16))
+    pick(A("g0", 0, 128), A("win", 0, 832), A("l0", 0, 8))
     lay_stage(1)
-    turn(A("ts0"), A("g0", 0, 256))
+    turn(A("ts0", 128, 256), A("g0", 128, 256))
+    turn(A("ts0", 0, 128), A("g0", 0, 128))
     v = [A("ts0", 128 + 14 - 4 * i, 256, 16) for i in range(4)]
     tt(A("sums", 0, 8), v[0], v[1], S)
     ts(A("lab", 20, 24), A("ts0", 192 + 14, 256, 16), 416.0, ALU.subtract)
@@ -365,35 +371,33 @@ def rank_program(g, core, T, topo):
     copy(A("lab", 0, 4), A("sums", 16, 20))
 
     def later_constants():
-        yield lambda: quant("a", 32, 160, A("ra", 128, 640))
-        yield lambda: ts(A("cs", 80, 96), few(16), 0.0, ALU.is_gt)
-        yield lambda: ts(A("cs", 48, 64), d16, 0.0, EQ, 63.0, M)
-        yield lambda: copy(A("cidx"), few(20))
-        yield lambda: ts(A("cs", 64, 80), A("cs", 48, 64), 1.0, S)
-        yield lambda: ts(K("q4"), q, 416.0, S)
-        yield lambda: tt(A("cs", 0, 16), A("cs", 64, 80), A("cs", 80, 96), M)
-
-        def rest():
-            act(A("dsc"), A("cs", 0, 16), off=A("qrep", 0, 20))
-            for b in range(4):
-                act(A("tt", 336 * b + 320, 336 * b + 336), few(16), scale=0.0)
-            quant("r", 224, 352, A("ub"))
-        yield rest
+        act(A("dsc"), A("cs", 0, 16), off=A("qrep", 0, 20))
+        lin(A("cs2", 0, 32, 2), A("cs", 16, 32), 1.0, 0.0)
+        lin(A("cs2", 1, 32, 2), few(16), 0.0, 0.0)
+        lin(K("q4"), q, 1.0, 416.0)
+        lin(K("h3"), K("hs"), 1.0, 320.0)
+        lin(A("back"), A("iw", 0, 320), -1.0, 320.0)
+        act(A("dia2"), A("cs2", 0, 32), off=A("qrep2"))
+        for b in range(4):
+            act(A("tt", 336 * b + 320, 336 * b + 336), few(16), scale=0.0)
+        quant("r", 224, 352, A("ub"))
 
     def tables(s):
         act(A("sn", 416 * s - 416, 416 * s), A("ss"), off=A("bl", 26 * s - 26, 26 * s))
         for h in range(8):
             c = 16 * h + phase[s] + 5
-            dma("y", "t%d" % s, A("win", region[s], region[s] + 832, p=(c, c + 9, 4)), A("sn", 416 * s - 416, 416 * s, p=(s - 1, s + 100, 20)))
+            dma("s" if s == 1 and h % 2 else "y", "t%d" % s, A("win", region[s], region[s] + 832, p=(c, c + 9, 4)), A("sn", 416 * s - 416, 416 * s, p=(s - 1, s + 100, 20)))
 
-    def carry(gi):
-        x, lo = ("a", 32 * (gi - 6)) if gi > 5 else ("b", 32 * gi)
-        mm(1, "k", 112 - 16 * gi, x, lo, lo + 128, gi == 0, gi == 7)
+    def carry(s):
+        x, lo = "ba"[s // 2], 32 * (s % 2)
+        mm(1, "k", 96 - 32 * s, x, lo, lo + 128, s == 0, s == 3)
 
     def digits(lo, s):
-        for i, bits in enumerate((15, 240, 256)):
-            yield lambda i=i, bits=bits: ts(A("dg", 32 * lo + i, 32 * s + 32, 4), A("ni", 8 * lo, 8 * s + 8), bits, ALU.bitwise_and)
-        yield lambda: put(A("ra" if s == 3 else "rb"), A("rl", 2 * lo, 2 * s + 2), A("dg", 32 * lo, 32 * s + 32))
+        n, low, c = A("ni", 8 * lo, 8 * s + 8), A("lo5", 8 * lo, 8 * s + 8), 2 * (lo % 2)
+        yield lambda: ts(low, n, 31, ALU.bitwise_and)
+        yield lambda: ts(A("dg", 16 * lo, 16 * s + 16, 2), n, 480, ALU.bitwise_and)
+        yield lambda: ts(A("dg", 16 * lo + 1, 16 * s + 16, 2), low, 16.0, ALU.subtract)
+        yield lambda: put(A("ra" if s == 3 else "rb"), A("rl", c, c + s - lo + 1), A("dg", 16 * lo, 16 * s + 16))
 
     def first_choice(s, tr):
         bt, u, n = "bt%d" % s, phase[s] + 1, 8 * s
@@ -402,18 +406,17 @@ def rank_program(g, core, T, topo):
         yield lambda: tt(A("ni", 8 * s, 8 * s + 8, 2), A("nd", n + 4, n + 8), A(tr, 64 + u, 128, 16), S)
 
     def second_choice(s):
-        bt, fo, n = "bt%d" % s, "fo%d" % s, 32 + 16 * s
-        yield lambda: scan(A("ww", 32 * s, 32 * s + 32), A(bt), A("pat"), M, S)
+        fo, n = "fo%d" % s, 32 + 16 * s
         yield lambda: tt(A("nd", n, n + 8), A(fo, 3, 32, 4), A("offs"), ALU.subtract)
         yield lambda: tt(A("nd", n + 8, n + 16), A("nd", n, n + 8), A("ww", 32 * s + 3, 32 * s + 32, 4), M)
         yield lambda: tt(A("ni", 8 * s + 1, 8 * s + 8, 2), A("nd", n + 8, n + 12), A("nd", n + 12, n + 16), S)
-        if s != 1:
-            yield from digits(s // 2, s)
-
+        if s < 2:
+            yield from digits(s, s)
+        if s == 1:
             def out():
-                quant("b", 32 * s, 32 * s + 128, A("rb", 128 * s, 128 * s + 512))
-                for gi in range(2, 6) if s else (0, 1):
-                    carry(gi)
+                quant("b", 0, 160, A("rb"))
+                carry(0)
+                carry(1)
             yield out
 
     def growth(r):
@@ -436,9 +439,9 @@ def rank_program(g, core, T, topo):
             else:
                 tr = "tr%d" % s
                 pick(A("gt"), A("win", region[s], region[s] + 832), A("ll"))
-                gap(2)
+                gap()
                 turn(A(tr), A("gt"))
-                gap(2)
+                gap()
                 for side in (0, 1):
                     tt(A(bt, 16 * side, 16 * side + 16), A(tr, ph + 1, 64, 4), A(tr, 64 + ph + 1, 128, 4), ALU.is_le)
             f = list(first_choice(s, tr))
@@ -451,32 +454,30 @@ def rank_program(g, core, T, topo):
             f[2]()
             if s < 3:
                 copy(A("ll"), A(fo, 3, 32, 4))
-                if s == 0 and r == 0:
-                    quant("k", 0, 240, A("wr"))
-                    quant("b", 128, 288, A("rb", 512, 1152))
+                scan(A("ww", 32 * s, 32 * s + 32), A(bt), A("pat"), M, S)
                 todo.extend(second_choice(s))
-                if s == 0 and r == 0:
-                    todo.insert(7, lambda: copy(A("rl"), A("rlf")))
                 if s == 0:
-                    gap(8)
                     if r == 0:
-                        todo.extend(later_constants())
+                        quant("k", 0, 224, A("wr"))
+                        todo.insert(6, lambda: copy(A("rl"), A("rlf")))
+                        todo.append(later_constants)
+                    gap(5)
                     if r == 1:
                         quant("v", 0, 128, A("vin"))
-                gap()
+                else:
+                    gap()
             else:
                 tt(A("ni", 25, 32, 2), A(fo, 3, 16, 4), A(fo, 19, 32, 4), S)
                 gap(len(todo))
-                for f in digits(3, 3):
+                for f in digits(2, 3):
                     f()
-                quant("a", 0, 128, A("ra", 0, 512))
-                carry(6)
-                carry(7)
+                quant("a", 0, 160, A("ra"))
+                carry(2)
+                carry(3)
                 copy(A("nl"), P(1, 0, 20))
 
-    def take(t, z):
-        o, i, l = A("mt", 640 * z + t, 640 * z + 640, 4), A("vt", E * t, E * t + E), A("nl", 10 * z, 10 * z + 10)
-        pick(o, i, l) if t < 2 else act(o, i, off=l)
+    def take(t, z, how):
+        how(A("mt", 640 * z + t, 640 * z + 640, 4), A("vt", E * t, E * t + E), off=A("nl", 10 * z, 10 * z + 10))
 
     def layer(z):
         quant("m", 160 * z, 160 * z + 160, A("mt", 640 * z, 640 * z + 640))
@@ -494,10 +495,10 @@ def rank_program(g, core, T, topo):
 
     def lists(lo, hi, out):
         for k in (1, 0):
-            scan(A("dg%d" % k, lo, hi), A("dia", lo, hi), A("inv%d" % k, lo, hi), S, ALU.max)
+            scan(A("dg%d" % k, 2 * lo, 2 * hi), A("dia2", 2 * lo, 2 * hi), A("inv%d" % k, 2 * lo, 2 * hi), S, ALU.max)
         m = A("dm", lo // 16, hi // 16)
-        tt(m, A("dg0", lo + 15, hi, 16), A("dg1", lo + 15, hi, 16), ALU.min)
-        ts(out, m, K("hs"), ALU.subtract)
+        tt(m, A("dg0", 2 * lo + 31, 2 * hi, 32), A("dg1", 2 * lo + 31, 2 * hi, 32), ALU.max)
+        ts(out, m, -1.0, M, K("h3"), S)
 
     def minus(t):
         return A("tt", 336 * t, 336 * t + 336)
@@ -507,6 +508,14 @@ def rank_program(g, core, T, topo):
             tt(A("xt", 512 + t, 1280, 4), minus(t), A("vt", E * t + 128, E * t + C), S, off=A("ul", 8, 20))
         quant("c", 128, 320, A("xt", 512, 1280))
 
+    def store(lo, hi):
+        dma("y", "ob", T.oc[:, 4 * lo:4 * hi], A("qc", lo, hi, bits=dt.uint8))
+        for k in range(4):
+            dma("y", "ob", T.osc[4 * k:4 * k + 4, lo:hi], A("sc", lo, hi, p=(32 * k, 32 * k + 4)))
+        mm(6, "v", 0, "c", lo, hi)
+        act(A("ysb", lo, hi), P(6, 0, hi - lo))
+        dma("s", "ob", T.y[:, lo:hi], A("ysb", lo, hi))
+
     n_in_b = 2 * len(topo.engines(nxt, core))
     n_in_r = 2 * len(topo.engines(prv, core))
     for r in range(ROUNDS):
@@ -514,34 +523,36 @@ def rank_program(g, core, T, topo):
         arrive("ba%d" % r, n_in_b, [A("qc", C, E), A("sc", C, E)])
         score(6, 288, 416, 32)
         for s in (1, 2, 3):
+            if r == 0 and s > 1:
+                lay_stage(s)
             tables(s)
         if r == 0:
-            digit_places()
-        unpack_all()
+            unpack((2, 3, 4, 5), 0, 128)
+        unpack((0, 7, 2, 3), 128, 320)
+        unpack((2, 3, 4, 5), 288, 416, 32)
         for k in range(2):
-            iota(A("inv%d" % k), [[0, 432]], base=320)
+            iota(A("inv%d" % k), [[0, 864]])
         growth(r)
-        act(A("nr"), A("iw"), off=A("nl"))
-        for z in (0, 1):
-            for t in (2, 3, 0, 1):
-                take(t, z)
-            if z == 0:
-                copy(A("nlf"), A("nl"))
+        act(A("nlf"), P(1, 0, 20))
+        for t, z in ((1, 0), (2, 0), (3, 0), (0, 1), (1, 1), (2, 1), (3, 1)):
+            take(t, z, act)
+        pick(A("nr"), A("iw"), A("nl"))
+        take(0, 0, pick)
         tt(A("eq"), A("nlf"), A("nr"), EQ, off=A("cidx"))
         layer(0)
-        if last:
-            dma("y", "ob", T.on[:, :], A("nr", p=(0, 128, 16)))
         scan(A("scn"), A("dsc"), A("eq"), M, S)
-        layer(1)
         ts(A("dq"), A("scn", 15, 320, 16), 32.0, ALU.is_ge, K("q4"), M)
         tt(A("ad"), A("nlf"), A("dq"), ALU.max)
-        copy(A("adr", 0, 40, 2), A("ad"))
-        for c in range(9, -1, -1):
-            if c in (6, 3):
-                unpack_t(c == 3)
-            for k in (1, 0):
-                d = 10 * k + c
-                put(A("inv%d" % k), A("adr", 2 * d, 2 * d + 1), A("iw", 16 * d, 16 * d + 16))
+        for k in (0, 1):
+            ts(A("adr", k, 20, 2), A("ad", k, 20, 2), 2.0, M, float(k), S)
+        if last:
+            dma("y", "ob", T.on[:, :], A("nr", p=(0, 128, 16)))
+        between = {0: lambda: layer(1), 4: lambda: unpack_t(0), 8: lambda: unpack_t(1)}
+        for i in range(10):
+            if i in between:
+                between[i]()
+            d = 18 - 10 * (i % 2) - 2 * (i // 2)
+            put(A("inv%d" % (d // 10)), A("adr", d, d + 2), A("back", 16 * d, 16 * d + 32))
         lists(C, E, A("ulb"))
         for t in (2, 3):
             act(A("ub", t, 384, 4), minus(t), scale=-1.0, off=A("ulb"))
@@ -550,31 +561,24 @@ def rank_program(g, core, T, topo):
         quant("r", 0, 128, A("ub"))
         send(nxt, "r", 0, H, 128, "ra%d" % r, "rtl")
         lists(0, C, A("ul"))
-        for t in range(4):
-            tt(A("xf", 128 * t, 128 * t + 128), minus(t), A("vt", E * t, E * t + 128), S, off=A("ul", 0, 8))
         if last:
             rest()
+            store(128, 320)
+        for t in range(4):
+            tt(A("xf", 128 * t, 128 * t + 128), minus(t), A("vt", E * t, E * t + 128), S, off=A("ul", 0, 8))
         arrive("ra%d" % r, n_in_r, [A("qr", 128, 224), A("sr", 128, 224)])
         bb = (0, 1, 7, 2)
         for b in range(4):
             mm(bb[b], "e", 128 * b, "r", 128, 256)
-        if last:
-            mm(6, "v", 0, "c", 128, 320)
-            act(A("ysb", 128, 320), P(6, 0, 192))
-            dma("y", "ob", T.y[:, 128:320], A("ysb", 128, 320))
         for b in range(4):
             tt(A("xt", b, 512, 4), A("xf", 128 * b, 128 * b + 128), P(bb[b], 0, 128), ALU.subtract)
         quant("c", 0, 128, A("xt", 0, 512))
         if last:
-            mm(0, "v", 0, "c", 0, 128)
-            act(A("ysb", 0, 128), P(0, 0, 128))
-            dma("y", "ob", T.oc[:, :], A("qc", 0, 320, bits=dt.uint8))
-            for k in range(4):
-                dma("y" if k % 2 else "s", "ob", T.osc[4 * k:4 * k + 4, 0:320], A("sc", 0, 320, p=(32 * k, 32 * k + 4)))
-            dma("s", "ob", T.y[:, 0:128], A("ysb", 0, 128))
+            store(0, 128)
         else:
             border_out(r + 1)
             score(0, 0, 128)
+            unpack((2, 3, 4, 5), 0, 128)
             rest()
             score(6, 128, 320)
     for s in SEMAPHORES:

@@ -12,15 +12,17 @@ def _declare(kind, names):
 
 
 _declare("bfloat16", "xt:1280 ut:512 vin:512 zb:516 eb:516 vt:1664 mt:1280 tb:1280 tt:1344 ub:512 wr:896 ra:640 rb:640 dsc:320 eq:320 scn:320")
+_declare("bfloat16", "inv0:864 inv1:864 dia2:832 back:320")
+_declare("float16", "dg0:832 dg1:832")
 _declare("int32", "lri:104 bli:78 cpi:26 pi:2 pa:6 ni:32 lo5:32 dg:64")
 _declare("uint16", "lru:52 bl:78 l0:16 ll:8 cidx:20 nl:20 qrep:26 qrep2:52 adr:20 ul:20 ulb:6 lz:8 lab:24 rl:4")
 _declare("float8_e4m3fn_x4", "qw:512 qu:128 q0:128 qv:128 qe:512 qc:416 qm:320 qt:320 qr:352 qa:160 qb:160 qk:224")
 _declare("uint8", "sw:512 su:128 s0:128 sv:128 se:512 sc:416 sm:320 st:320 sr:352 sa:160 sb:160 sk:224")
-_declare("float32", "i32:32 iw:416 cs:96 cs2:32 dia:416 dia2:832 back:320 offs:8 pf:6 kk:64 cf:16 ls:156 l0f:16 rlf:4")
+_declare("float32", "i32:32 iw:416 cs:96 cs2:32 dia:416 offs:8 pf:6 kk:64 cf:16 ls:156 l0f:16 rlf:4")
 _declare("float32", "aiw:416 biw:416 base:416 gr2:416 r2:416 ur:416 rc:416 t1:416 t2:416 t3:416 win:2496 sums:24 pat:32")
 _declare("float32", "g0:384 tr0:384 ts0:256 gt:128 tr1:128 tr2:128 tr3:128 bt0:32 bt1:32 bt2:32 bt3:32 fo0:32 fo1:32 fo2:32 fo3:32")
-_declare("float32", "nd:80 ww:96 nlf:20 ss:416 sn:1248 nr:320")
-_declare("float32", "dq:20 ad:20 inv0:864 inv1:864 dg0:832 dg1:832 dm:26 xf:512 ysb:320")
+_declare("float32", "nd:80 ww:96 nlf:40 late:320 ss:416 sn:1248 nr:320")
+_declare("float32", "ad:20 dm:26 xf:512 ysb:320")
 _declare("float32", "ps0:512 ps1:512 ps2:512 ps3:512 ps4:512 ps5:512 ps6:512 ps7:512")
 SEMAPHORES = "cv cs ct cg lx0 lx1 llr lb lc lu lv lw k0 k1 k2 k3 t1 t2 t3 ob bl rtl ba0 ba1 ba2 ra0 ra1 ra2".split()
 
@@ -271,8 +273,7 @@ def rank_program(g, core, T, topo):
     lin(K("b1"), K("b0"), 1.0, 16.0)
     quant("c", 0, 128, A("xt", 0, 512))
     border_out(0)
-    ts(A("cs", 80, 96), few(16), 0.0, ALU.is_gt)
-    ts(A("cs", 48, 64), d16, 0.0, EQ, 63.0, M)
+    ts(A("cs", 0, 16), d16, 0.0, ALU.is_ge, 1000.0, M)
     copy(A("cidx"), few(20))
     copy(A("qrep2", 0, 52, 2), A("qrep"))
     ts(A("ls", 0, 52), A("lri", 0, 52), K("ev"), M)
@@ -289,13 +290,11 @@ def rank_program(g, core, T, topo):
     for n in ("rb", "ra", "ub"):
         iota(A(n), [[0, T[n].shape[1]]])
     l1, l2 = A("lru", 0, 26), A("lru", 26, 52)
-    ts(A("cs", 64, 80), A("cs", 48, 64), 1.0, S)
     act(A("r2"), A("iw"), off=l2)
     tt(A("t1"), A("aiw"), A("base"), S, off=l1)
     act(A("gr2"), A("r2"), scale=A("cf", 8, 9))
     act(A("ur"), A("iw"), AF.Identity, bias=K("ub"), off=l1)
     ts(K("r3"), t8, -2.0, M, K("r1"), S)
-    tt(A("cs", 0, 16), A("cs", 64, 80), A("cs", 80, 96), M)
     tt(A("t2"), A("biw"), A("t1"), S, off=l2)
     act(A("rc"), A("r2"), off=l1)
     ts(K("r4"), K("r3"), K("r2"), S)
@@ -313,9 +312,9 @@ def rank_program(g, core, T, topo):
     ts(K("hs"), q, 15.0, ALU.is_lt, 2000.0, M)
     ts(A("lz"), few(8), 0.0, M, K("r4"), S)
     quant("u", 0, 128, A("ut"))
-    scan(A("dg0", 0, 416), A("dia"), A("rc"), S, ALU.max)
+    scan(A("t1"), A("dia"), A("rc"), S, ALU.max)
     ts(K("w0"), q, 96.0, S)
-    ts(A("cpi"), A("dg0", 15, 416, 16), K("hs"), ALU.subtract)
+    ts(A("cpi"), A("t1", 15, 416, 16), K("hs"), ALU.subtract)
     for s in (1, 2, 3):
         for side in (0, 1):
             dma("y", "lc", A("bli", 26 * s - 26, 26 * s, p=grp(6 * side)), A("cpi", p=grp(2 * s + side)))
@@ -371,12 +370,16 @@ def rank_program(g, core, T, topo):
     copy(A("lab", 0, 4), A("sums", 16, 20))
 
     def later_constants():
-        act(A("dsc"), A("cs", 0, 16), off=A("qrep", 0, 20))
-        lin(A("cs2", 0, 32, 2), A("cs", 16, 32), 1.0, 0.0)
+        act(A("late"), A("cs", 0, 16), off=A("qrep", 0, 20))
+        lin(A("dsc"), A("iw", 0, 320), 0.0, 1.0)
+        lin(A("cs2", 0, 32, 2), A("cs", 16, 32), 0.5, 0.0)
         lin(A("cs2", 1, 32, 2), few(16), 0.0, 0.0)
-        lin(K("q4"), q, 1.0, 416.0)
-        lin(K("h3"), K("hs"), 1.0, 320.0)
-        lin(A("back"), A("iw", 0, 320), -1.0, 320.0)
+        lin(A("dsc", 0, 320, 16), few(20), 0.0, 0.0)
+        lin(A("dsc", 15, 320, 16), few(20), 0.0, 1000.0)
+        for k in (0, 1):
+            lin(K("q%d" % k), q, 2.0, 832.0 + k)
+        lin(K("h3"), K("hs"), 0.5, 256.0)
+        lin(A("back"), A("iw", 0, 320), -1.0, 256.0)
         act(A("dia2"), A("cs2", 0, 32), off=A("qrep2"))
         for b in range(4):
             act(A("tt", 336 * b + 320, 336 * b + 336), few(16), scale=0.0)
@@ -386,7 +389,7 @@ def rank_program(g, core, T, topo):
         act(A("sn", 416 * s - 416, 416 * s), A("ss"), off=A("bl", 26 * s - 26, 26 * s))
         for h in range(8):
             c = 16 * h + phase[s] + 5
-            dma("s" if s == 1 and h % 2 else "y", "t%d" % s, A("win", region[s], region[s] + 832, p=(c, c + 9, 4)), A("sn", 416 * s - 416, 416 * s, p=(s - 1, s + 100, 20)))
+            dma("ys"[h % 2], "t%d" % s, A("win", region[s], region[s] + 832, p=(c, c + 9, 4)), A("sn", 416 * s - 416, 416 * s, p=(s - 1, s + 100, 20)))
 
     def carry(s):
         x, lo = "ba"[s // 2], 32 * (s % 2)
@@ -410,9 +413,9 @@ def rank_program(g, core, T, topo):
         yield lambda: tt(A("nd", n, n + 8), A(fo, 3, 32, 4), A("offs"), ALU.subtract)
         yield lambda: tt(A("nd", n + 8, n + 16), A("nd", n, n + 8), A("ww", 32 * s + 3, 32 * s + 32, 4), M)
         yield lambda: tt(A("ni", 8 * s + 1, 8 * s + 8, 2), A("nd", n + 8, n + 12), A("nd", n + 12, n + 16), S)
-        if s < 2:
-            yield from digits(s, s)
         if s == 1:
+            yield from digits(0, 1)
+
             def out():
                 quant("b", 0, 160, A("rb"))
                 carry(0)
@@ -432,10 +435,9 @@ def rank_program(g, core, T, topo):
                 tr = "ts0"
                 pick(A("g0"), A("ss"), A("lab"))
                 turn(A("tr0"), A("g0"))
-                for side in (0, 1):
-                    for k, cls in enumerate((3, 11, 3)):
-                        c = 64 * k + cls
-                        tt(A(bt, 16 * side + k + 1, 16 * side + 16, 4), A("tr0", c, 64 * k + 64, 16), A("tr0", 192 + c, 256 + 64 * k, 16), ALU.is_le)
+                for k, cls in ((1, 11), (2, 3), (0, 3)):
+                    c = 64 * k + cls
+                    tt(A(bt, k + 1, 16, 4), A("tr0", c, 64 * k + 64, 16), A("tr0", 192 + c, 256 + 64 * k, 16), ALU.is_le)
             else:
                 tr = "tr%d" % s
                 pick(A("gt"), A("win", region[s], region[s] + 832), A("ll"))
@@ -445,12 +447,19 @@ def rank_program(g, core, T, topo):
                 for side in (0, 1):
                     tt(A(bt, 16 * side, 16 * side + 16), A(tr, ph + 1, 64, 4), A(tr, 64 + ph + 1, 128, 4), ALU.is_le)
             f = list(first_choice(s, tr))
-            f[0]()
+            if s or not r:
+                f[0]()
             gap()
-            tt(A(bt, 3, 32, 4), A(bt, 2, 32, 4), A(bt, 3, 32, 4), ALU.max)
+            n = 32 if s else 16
+            tt(A(bt, 3, n, 4), A(bt, 2, n, 4), A(bt, 3, n, 4), ALU.max)
             f[1]()
             gap()
-            scan(A(fo), A(bt), A(tr, ph, 128, 4), M, S)
+            if s:
+                scan(A(fo), A(bt), A(tr, ph, 128, 4), M, S)
+            else:
+                for o in (0, 16):
+                    scan(A(fo, o, o + 16), A(bt, 0, 16), A(tr, 4 * o + ph, 4 * o + 64, 4), M, S)
+                copy(A(bt, 16, 32), A(bt, 0, 16))
             f[2]()
             if s < 3:
                 copy(A("ll"), A(fo, 3, 32, 4))
@@ -459,13 +468,9 @@ def rank_program(g, core, T, topo):
                 if s == 0:
                     if r == 0:
                         quant("k", 0, 224, A("wr"))
-                        todo.insert(6, lambda: copy(A("rl"), A("rlf")))
+                        todo.append(lambda: copy(A("rl"), A("rlf")))
                         todo.append(later_constants)
-                    gap(5)
-                    if r == 1:
-                        quant("v", 0, 128, A("vin"))
-                else:
-                    gap()
+                gap()
             else:
                 tt(A("ni", 25, 32, 2), A(fo, 3, 16, 4), A(fo, 19, 32, 4), S)
                 gap(len(todo))
@@ -531,23 +536,22 @@ def rank_program(g, core, T, topo):
         unpack((0, 7, 2, 3), 128, 320)
         unpack((2, 3, 4, 5), 288, 416, 32)
         for k in range(2):
-            iota(A("inv%d" % k), [[0, 864]])
+            iota(A("inv%d" % k), [[0, 864]], base=-64)
         growth(r)
-        act(A("nlf"), P(1, 0, 20))
         for t, z in ((1, 0), (2, 0), (3, 0), (0, 1), (1, 1), (2, 1), (3, 1)):
             take(t, z, act)
-        pick(A("nr"), A("iw"), A("nl"))
+        tt(A("nr"), A("iw"), A("late"), S, off=A("nl"))
+        copy(A("nlf", 0, 20), A("nl"))
         take(0, 0, pick)
-        tt(A("eq"), A("nlf"), A("nr"), EQ, off=A("cidx"))
+        tt(A("eq"), A("nlf", 0, 20), A("nr"), EQ, off=A("cidx"))
         layer(0)
         scan(A("scn"), A("dsc"), A("eq"), M, S)
-        ts(A("dq"), A("scn", 15, 320, 16), 32.0, ALU.is_ge, K("q4"), M)
-        tt(A("ad"), A("nlf"), A("dq"), ALU.max)
         for k in (0, 1):
-            ts(A("adr", k, 20, 2), A("ad", k, 20, 2), 2.0, M, float(k), S)
-        if last:
-            dma("y", "ob", T.on[:, :], A("nr", p=(0, 128, 16)))
-        between = {0: lambda: layer(1), 4: lambda: unpack_t(0), 8: lambda: unpack_t(1)}
+            ts(A("nlf", 20 + k, 40, 2), A("nl", k, 20, 2), 2.0, M, float(k), S)
+        tt(A("ad"), A("nlf", 20, 40), A("scn", 15, 320, 16), S)
+        for k in (0, 1):
+            ts(A("adr", k, 20, 2), A("ad", k, 20, 2), K("q%d" % k), ALU.min)
+        between = {0: lambda: layer(1), 3: lambda: unpack_t(0), 6: lambda: unpack_t(1)}
         for i in range(10):
             if i in between:
                 between[i]()
@@ -562,6 +566,8 @@ def rank_program(g, core, T, topo):
         send(nxt, "r", 0, H, 128, "ra%d" % r, "rtl")
         lists(0, C, A("ul"))
         if last:
+            act(A("nr"), A("iw"), off=A("nl"))
+            dma("y", "ob", T.on[:, :], A("nr", p=(0, 128, 16)))
             rest()
             store(128, 320)
         for t in range(4):
@@ -581,6 +587,8 @@ def rank_program(g, core, T, topo):
             unpack((2, 3, 4, 5), 0, 128)
             rest()
             score(6, 128, 320)
+            if r == 0:
+                quant("v", 0, 128, A("vin"))
     for s in SEMAPHORES:
         if know["g"].get(s, 0) < cnt[s]:
             g.wait_ge(T.sem[s], cnt[s])

@@ -11,20 +11,20 @@ def _declare(kind, names):
         SCRATCH[n] = ("psum" if n.startswith("ps") else "sbuf", [128, int(c)], kind)
 
 
-_declare("bfloat16", "xt:1280 ut:512 vin:512 zb:516 eb:516 vt:1664 mt:1280 tb:1280 tt:1344 ub:512 wr:896 ra:640 rb:640 dsc:320 eq:320 scn:320")
+_declare("bfloat16", "xt:1280 ut:512 vin:512 zb:516 eb:516 vt:1664 mt:1280 tb:1280 tt:1344 ub:512 wr:896 ra:640 rb:640 gone:768 dsc:320 eq:320 scn:320")
 _declare("bfloat16", "inv0:864 inv1:864 dia2:832 back:320")
 _declare("float16", "dg0:832 dg1:832")
 _declare("int32", "lri:104 bli:78 cpi:26 pi:2 pa:6 ni:32 lo5:32 dg:64")
-_declare("uint16", "lru:52 bl:78 l0:16 ll:8 cidx:20 nl:20 qrep:26 qrep2:52 adr:20 ul:20 ulb:6 lz:8 lab:24 rl:4")
+_declare("uint16", "lru:52 bl:78 l0:16 ll:8 cidx:20 nl:20 adr:20 ul:20 ulb:6 lz:8 lab:24 rl:2")
 _declare("float8_e4m3fn_x4", "qw:512 qu:128 q0:128 qv:128 qe:512 qc:416 qm:320 qt:320 qr:352 qa:160 qb:160 qk:224")
 _declare("uint8", "sw:512 su:128 s0:128 sv:128 se:512 sc:416 sm:320 st:320 sr:352 sa:160 sb:160 sk:224")
-_declare("float32", "i32:32 iw:416 cs:96 cs2:32 dia:416 offs:8 pf:6 kk:64 cf:16 ls:156 l0f:16 rlf:4")
+_declare("float32", "i32:96 iw:416 cs:208 dia:416 offs:8 pf:5 kk:32 cf:16 ls:156 l0f:16 rlf:128")
 _declare("float32", "aiw:416 biw:416 base:416 gr2:416 r2:416 ur:416 rc:416 t1:416 t2:416 t3:416 win:2496 sums:24 pat:32")
 _declare("float32", "g0:384 tr0:384 ts0:256 gt:128 tr1:128 tr2:128 tr3:128 bt0:32 bt1:32 bt2:32 bt3:32 fo0:32 fo1:32 fo2:32 fo3:32")
-_declare("float32", "nd:80 ww:96 nlf:40 late:320 ss:416 sn:1248 nr:320")
+_declare("float32", "nd:64 nf:24 ww:96 nlf:20 iw2:416 late:320 ss:416 sn:1248 nr:320")
 _declare("float32", "ad:20 dm:26 xf:512 ysb:320")
 _declare("float32", "ps0:512 ps1:512 ps2:512 ps3:512 ps4:512 ps5:512 ps6:512 ps7:512")
-SEMAPHORES = "cv cs ct cg lx0 lx1 llr lb lc lu lv lw k0 k1 k2 k3 t1 t2 t3 ob bl rtl ba0 ba1 ba2 ra0 ra1 ra2".split()
+SEMAPHORES = "cv cs ct cg lx0 lx1 llr lb lc lu lv lw k0 k1 k2 k3 t1 t2 t3 rp ob bl rtl ba0 ba1 ba2 ra0 ra1 ra2".split()
 
 
 def rank_program(g, core, T, topo):
@@ -215,7 +215,8 @@ def rank_program(g, core, T, topo):
     dma("y", "lx1", A("xt", 512, 1280), T.x[:, 512:1280])
     pi = A("pi")
     op("g", lambda: g.iota(pi["ap"], [[0, 2]], 0, 1), [pi], [])
-    iota(A("i32"), [[1, 32]])
+    iota(A("i32", 0, 32), [[1, 32]])
+    iota(A("i32", 32, 96), [[0, 4], [1, 16]])
     iota(A("iw"), [[1, 416]])
     iota(A("win", 0, 832), [[0, 832]])
     fill(A("bli"), 0)
@@ -223,83 +224,90 @@ def rank_program(g, core, T, topo):
         for t, gi, h in ((T.rt, 2 * s + 1, 1), (T.lf, 2 * s, 2), (T.rt, 2 * s, 3), (T.lf, 2 * s + 1, 5)):
             dma("y", "lb", A("bli", 26 * s - 26, 26 * s, p=grp(h)), rows(t, gi))
 
-    lin(A("bt0", 0, 32, 4), few(8), 0.0, 0.0)
+    lin(A("bt0", 0, 16, 4), few(4), 0.0, 0.0)
+    lin(A("nf"), few(24), 0.0, 16.0)
     for lo, hi, st, c in ((0, 16, 2, 1.0), (16, 32, 2, -1.0), (1, 16, 4, -1.0), (17, 32, 2, 1.0), (3, 16, 4, 0.0)):
         lin(A("pat", lo, hi, st), few(16 // st), 0.0, c)
 
     def fields(lo, masks):
         for i, bits in enumerate(masks):
             ts(A("pa", lo + i, lo + i + 1), A("pi", 0, 1), bits, ALU.bitwise_and)
+
+    def repeat(names, steps):
+        for w, n in steps:
+            for name in names:
+                for lo in range(w, min(n, T[name].shape[1]), w):
+                    hi = min(lo + w, n)
+                    dma("y", "rp", A(name, lo, hi), A(name, 0, hi - lo))
     fields(0, (16, 3, 15))
-    copy(K("p"), A("pi", 0, 1))
+    e16, m4, q, t8, a32 = [A("pf", i, i + 1) for i in range(5)]
+    ei, mi = A("pa", 0, 1), A("pa", 1, 2)
+    d16, d64 = A("cs", 16, 32), A("cs", 16, 80)
+    ts(K("sg"), ei, -0.125, M, 1.0, S)
+    ts(K("o1"), ei, 0.1875, M)
+    ts(K("o2"), ei, 0.0625, M, 1.0, S)
     copy(A("pf", 0, 3), A("pa", 0, 3))
-    fields(3, (8, 96))
-    e16, m4, q, t8, a32, g4 = [A("pf", i, i + 1) for i in range(6)]
-    d16 = A("cs", 32, 48)
-    ts(d16, few(16), q, ALU.subtract)
-    ts(A("qrep"), few(26), 0.0, M, q, S)
-    ts(A("cs", 48, 64), d16, 0.0, EQ, -4000.0, M)
-    ts(A("cs", 64, 80), d16, 1.0, EQ, 2000.0, M)
-    ts(K("sg"), e16, -0.125, M, 1.0, S)
-    tt(A("cs", 16, 32), A("cs", 48, 64), A("cs", 64, 80), S)
-    act(A("dia"), A("cs", 16, 32), off=A("qrep"))
-    ts(K("od3"), e16, 0.1875, M)
-    ts(K("nl"), K("p"), 96.0, ALU.is_lt)
-    ts(K("z"), m4, K("sg"), M, K("od3"), S)
-    ts(K("e1"), m4, 3.0, EQ, e16, M)
-    ts(K("z2"), K("z"), K("sg"), S)
+    ts(K("z"), mi, K("sg"), M, K("o1"), S)
+    ts(K("z2"), mi, K("sg"), M, K("o2"), S)
+    ts(K("nl"), A("pi", 0, 1), 96.0, ALU.is_lt)
+    ts(d64, A("i32", 32, 96), q, ALU.subtract)
     ts(A("cf", 0, 4), few(4), K("z"), EQ)
     ts(A("cf", 4, 8), few(4), K("z2"), EQ)
-    ts(K("e2"), K("e1"), 26.0, M, K("nl"), M)
-    ts(K("e3"), K("p"), 96.0, ALU.is_ge, K("z"), M)
+    ts(K("e1"), mi, 3.0, EQ, e16, M)
+    ts(K("e3"), A("pi", 0, 1), 96.0, ALU.is_ge, K("z"), M)
     tt(A("cf", 8, 12), A("cf", 0, 4), A("cf", 4, 8), ALU.subtract)
-    ts(K("e4"), K("e3"), 3.0, EQ, 16.0, M)
-    ts(K("od"), e16, 0.0625, M)
-    ts(K("ev"), e16, -0.0625, M, 1.0, S)
+    ts(K("od"), ei, 0.0625, M)
+    ts(K("ev"), ei, -0.0625, M, 1.0, S)
     ts(A("cf", 12, 16), A("cf", 8, 12), K("nl"), M)
-    ts(K("eps"), K("e4"), K("ev"), M, K("e2"), S)
     act(A("biw"), A("iw"), scale=A("cf", 10, 11))
     act(A("aiw"), A("iw"), scale=A("cf", 13, 14))
+    ts(A("cs", 80, 144), d64, 0.0, EQ, -4000.0, M)
+    ts(A("cs", 144, 208), d64, 1.0, EQ, 2000.0, M)
+    ts(K("e2"), K("e1"), 26.0, M, K("nl"), M)
+    ts(K("e4"), K("e3"), 3.0, EQ, 16.0, M)
+    tt(A("dia", 0, 64), A("cs", 80, 144), A("cs", 144, 208), S)
+    repeat(["dia"], ((64, 416),))
+    ts(A("ls", 0, 52), A("lri", 0, 52), K("ev"), M)
+    ts(K("eps"), K("e4"), K("ev"), M, K("e2"), S)
     lin(A("base"), A("iw"), A("cf", 15, 16), K("eps"))
-    ts(K("ub"), e16, -256.0, M, 4112.0, S)
-    fields(5, (4,))
-    copy(A("pf", 3, 6), A("pa", 3, 6))
-    lin(K("b0"), K("p"), 2.0, 0.0)
-    lin(K("b2"), a32, 0.5, q)
-    lin(K("b4"), a32, 1.0, K("p"))
-    lin(K("b0"), q, -1.0, K("b0"))
-    lin(K("b3"), K("b2"), 1.0, 256.0)
-    lin(K("b5"), K("b4"), 1.0, 32.0)
-    lin(K("b1"), K("b0"), 1.0, 16.0)
+    ts(A("ls", 52, 104), A("lri", 52, 104), K("od"), M)
+    ts(K("ub"), ei, -256.0, M, 4112.0, S)
+    fields(3, (8,))
+    tt(A("ls", 104, 156), A("ls", 0, 52), A("ls", 52, 104), S)
     quant("c", 0, 128, A("xt", 0, 512))
     border_out(0)
-    ts(A("cs", 0, 16), d16, 0.0, ALU.is_ge, 1000.0, M)
-    copy(A("cidx"), few(20))
-    copy(A("qrep2", 0, 52, 2), A("qrep"))
-    ts(A("ls", 0, 52), A("lri", 0, 52), K("ev"), M)
-    ts(A("ls", 52, 104), A("lri", 52, 104), K("od"), M)
-    ts(K("r1"), m4, 32.0, M, 48.0, S)
-    tt(A("ls", 104, 156), A("ls", 0, 52), A("ls", 52, 104), S)
-    ts(K("r2"), m4, 3.0, EQ, -128.0, M)
     copy(A("lru"), A("ls", 104, 156))
+    fields(4, (96,))
     iota(A("zb"), [[0, 516]])
     eb, zb = A("eb"), A("zb")
     op("g", lambda: g.affine_select(eb["ap"], zb["ap"], [[1, 516]], ALU.not_equal, 1.0, -3, -4), [eb], [zb])
     iota(A("offs"), [[416, 2], [0, 4]], base=-16)
     iota(A("win", 832, 2496), [[0, 1664]])
-    for n in ("rb", "ra", "ub"):
+    for e in (0, 1):
+        for lo, first, step in ((0, 32 * e, 64), (32, 1024 + 64 * e, 32)):
+            iota(A("rlf", lo + 16 * e, lo + 16 * e + 8), [[step, 2], [8, 4]], 4, first)
+            iota(A("rlf", lo + 16 * e + 8, lo + 16 * e + 16), [[128, 2], [8, 4]], 1, 512 + 256 * e + 32 * lo)
+    for n in ("rb", "ra"):
         iota(A(n), [[0, T[n].shape[1]]])
+    iota(A("iw2"), [[2, 416]])
+    iota(A("dsc"), [[0, 320]], base=1)
+    iota(A("dsc", 0, 320, 16), [[0, 20]])
+    iota(A("dsc", 15, 320, 16), [[0, 20]], base=1000)
+    iota(A("back"), [[-1, 320]], base=256)
     l1, l2 = A("lru", 0, 26), A("lru", 26, 52)
     act(A("r2"), A("iw"), off=l2)
     tt(A("t1"), A("aiw"), A("base"), S, off=l1)
     act(A("gr2"), A("r2"), scale=A("cf", 8, 9))
     act(A("ur"), A("iw"), AF.Identity, bias=K("ub"), off=l1)
-    ts(K("r3"), t8, -2.0, M, K("r1"), S)
+    copy(K("p"), A("pi", 0, 1))
+    ts(K("r2"), mi, 3.0, EQ, -128.0, M)
     tt(A("t2"), A("biw"), A("t1"), S, off=l2)
     act(A("rc"), A("r2"), off=l1)
-    ts(K("r4"), K("r3"), K("r2"), S)
-    ts(A("qrep2", 1, 52, 2), A("qrep"), 16.0, S)
+    copy(A("pf", 3, 5), A("pa", 3, 5))
+    ts(K("r1"), mi, 32.0, M, K("r2"), S)
     tt(A("t3"), A("gr2"), A("t2"), S, off=l1)
+    ts(K("r3"), t8, -2.0, M, K("r1"), S)
+    quant("u", 0, 128, A("ut"))
     phase, region = (2, 0, 0, 0), (0, 0, 832, 1664)
 
     def lay_stage(s):
@@ -310,10 +318,10 @@ def rank_program(g, core, T, topo):
                 dma("y", "k%d" % s, A("win", lo, lo + 416, p=dst), A(src, p=p))
     lay_stage(0)
     ts(K("hs"), q, 15.0, ALU.is_lt, 2000.0, M)
-    ts(A("lz"), few(8), 0.0, M, K("r4"), S)
-    quant("u", 0, 128, A("ut"))
+    ts(A("lz"), A("zb", 0, 8), 48.0, S, K("r3"), S)
     scan(A("t1"), A("dia"), A("rc"), S, ALU.max)
     ts(K("w0"), q, 96.0, S)
+    ts(A("cs", 0, 16), d16, 0.0, ALU.is_ge, 1000.0, M)
     ts(A("cpi"), A("t1", 15, 416, 16), K("hs"), ALU.subtract)
     for s in (1, 2, 3):
         for side in (0, 1):
@@ -321,6 +329,13 @@ def rank_program(g, core, T, topo):
     dma("y", "lw", A("qw", bits=dt.uint8), T.wc[:, :])
     dma("y", "lw", A("sw"), T.ws[:, :])
     dma("y", "lv", A("vin"), T.v[:, :])
+    lin(K("b0"), K("p"), 2.0, 0.0)
+    lin(K("b2"), a32, 0.5, q)
+    lin(K("b4"), a32, 1.0, K("p"))
+    lin(K("b0"), q, -1.0, K("b0"))
+    lin(K("b3"), K("b2"), 1.0, 256.0)
+    lin(K("b5"), K("b4"), 1.0, 32.0)
+    lin(K("b1"), K("b0"), 1.0, 16.0)
     for i, b in enumerate(("b0", "b1", "b3", "b3", "b4", "b5", "b3", "b3")):
         lo = 8 * (i // 4)
         lin(A("l0f", lo + i % 4, lo + 8, 4), few(2), 416.0, K(b))
@@ -328,30 +343,14 @@ def rank_program(g, core, T, topo):
     pick(A("q0", bits=dt.uint32), A("qu", bits=dt.uint32), A("lz"))
     s0, su, lz = A("s0"), A("su"), A("lz")
     op("s", lambda: g.scalar.activation(s0["ap"], su["ap"].indirect(lz["ap"]), AF.Copy), [s0], [su, lz])
-    lin(K("c0"), a32, 0.375, -64.0)
-    lin(K("c3"), a32, 0.125, m4)
-    lin(K("c7"), t8, -0.125, 1.0)
-    lin(K("c1"), g4, -3.0, K("c0"))
-    lin(K("c2"), g4, -2.0, K("c0"))
-    lin(K("c6"), g4, 4.0, K("c3"))
-    lin(K("c4"), e16, -1.5, K("c1"))
-    lin(K("c8"), e16, 2.0, K("c6"))
-    lin(K("c5"), e16, -1.75, K("c2"))
-    lin(K("c9"), K("c8"), 1.0, 64.0)
     quant("c", 128, 320, A("xt", 512, 1280))
     score(0, 0, 128)
-    lin(K("d0"), K("c4"), K("c7"), K("c9"))
-    lin(A("rlf", 0, 1), K("c5"), K("c7"), K("c9"))
-    lin(K("d1"), K("d0"), 1.0, 128.0)
     score(6, 128, 320)
-    lin(A("rlf", 1, 4), few(3), 0.0, K("d1"))
     act(A("wr", 1, 896, 4), A("wr", 0, 896, 4))
     for t in (2, 3):
         act(A("wr", t, 64, 4), A("wr", 0, 64, 4))
         act(A("wr", 64 + t, 896, 4), A("wr", 0, 832, 4))
     copy(A("l0"), A("l0f"))
-    for b in range(4):
-        quant("e", 128 * b, 128 * b + 128, A("eb", 3 - b, 515 - b))
     pick(A("g0", 128, 256), A("win", 0, 832), A("l0", 8, 16))
     pick(A("g0", 0, 128), A("win", 0, 832), A("l0", 0, 8))
     lay_stage(1)
@@ -359,37 +358,32 @@ def rank_program(g, core, T, topo):
     turn(A("ts0", 0, 128), A("g0", 0, 128))
     v = [A("ts0", 128 + 14 - 4 * i, 256, 16) for i in range(4)]
     tt(A("sums", 0, 8), v[0], v[1], S)
-    ts(A("lab", 20, 24), A("ts0", 192 + 14, 256, 16), 416.0, ALU.subtract)
+    ts(A("lab", 12, 16), A("ts0", 192 + 14, 256, 16), 416.0, ALU.subtract)
+    copy(A("cidx"), few(20))
     tt(A("sums", 8, 16), A("sums", 0, 8), v[2], S)
     copy(A("bl"), A("bli"))
     copy(A("lab", 8, 12), A("sums", 0, 4))
-    ts(A("lab", 16, 20), A("sums", 4, 8), 416.0, ALU.subtract)
+    ts(A("lab", 4, 8), A("sums", 4, 8), 416.0, ALU.subtract)
     tt(A("sums", 16, 20), A("sums", 8, 12), A("ts0", 128 + 2, 192, 16), S)
-    copy(A("lab", 4, 8), A("sums", 8, 12))
-    ts(A("lab", 12, 16), A("sums", 12, 16), 416.0, ALU.subtract)
-    copy(A("lab", 0, 4), A("sums", 16, 20))
+    copy(A("lab", 0, 4), A("sums", 8, 12))
+    ts(A("lab", 20, 24), A("sums", 12, 16), 416.0, ALU.subtract)
+    copy(A("lab", 16, 20), A("sums", 16, 20))
 
     def later_constants():
-        act(A("late"), A("cs", 0, 16), off=A("qrep", 0, 20))
-        lin(A("dsc"), A("iw", 0, 320), 0.0, 1.0)
-        lin(A("cs2", 0, 32, 2), A("cs", 16, 32), 0.5, 0.0)
-        lin(A("cs2", 1, 32, 2), few(16), 0.0, 0.0)
-        lin(A("dsc", 0, 320, 16), few(20), 0.0, 0.0)
-        lin(A("dsc", 15, 320, 16), few(20), 0.0, 1000.0)
+        lin(A("late", 0, 16), A("cs", 0, 16), 1.0, 0.0)
+        lin(A("late", 16, 32), A("cs", 0, 16), 1.0, 1.0)
+        lin(A("dia2", 0, 32, 2), A("dia", 0, 16), 0.5, 0.0)
+        lin(A("dia2", 1, 32, 2), few(16), 0.0, 0.0)
         for k in (0, 1):
             lin(K("q%d" % k), q, 2.0, 832.0 + k)
         lin(K("h3"), K("hs"), 0.5, 256.0)
-        lin(A("back"), A("iw", 0, 320), -1.0, 256.0)
-        act(A("dia2"), A("cs2", 0, 32), off=A("qrep2"))
-        for b in range(4):
-            act(A("tt", 336 * b + 320, 336 * b + 336), few(16), scale=0.0)
-        quant("r", 224, 352, A("ub"))
+        repeat(["late", "dia2"], ((32, 160), (160, 832)))
 
     def tables(s):
         act(A("sn", 416 * s - 416, 416 * s), A("ss"), off=A("bl", 26 * s - 26, 26 * s))
         for h in range(8):
             c = 16 * h + phase[s] + 5
-            dma("ys"[h % 2], "t%d" % s, A("win", region[s], region[s] + 832, p=(c, c + 9, 4)), A("sn", 416 * s - 416, 416 * s, p=(s - 1, s + 100, 20)))
+            dma("s" if s == 1 and h % 2 else "y", "t%d" % s, A("win", region[s], region[s] + 832, p=(c, c + 9, 4)), A("sn", 416 * s - 416, 416 * s, p=(s - 1, s + 100, 20)))
 
     def carry(s):
         x, lo = "ba"[s // 2], 32 * (s % 2)
@@ -403,24 +397,43 @@ def rank_program(g, core, T, topo):
         yield lambda: put(A("ra" if s == 3 else "rb"), A("rl", c, c + s - lo + 1), A("dg", 16 * lo, 16 * s + 16))
 
     def first_choice(s, tr):
-        bt, u, n = "bt%d" % s, phase[s] + 1, 8 * s
+        bt, u, n = "bt%d" % s, phase[s] + 1, 16 + 8 * (s // 2)
         yield lambda: tt(A("nd", n, n + 4), A(tr, u, 64, 16), A(tr, 64 + u, 128, 16), ALU.subtract)
         yield lambda: tt(A("nd", n + 4, n + 8), A("nd", n, n + 4), A(bt, 2, 16, 4), M)
         yield lambda: tt(A("ni", 8 * s, 8 * s + 8, 2), A("nd", n + 4, n + 8), A(tr, 64 + u, 128, 16), S)
 
     def second_choice(s):
-        fo, n = "fo%d" % s, 32 + 16 * s
-        yield lambda: tt(A("nd", n, n + 8), A(fo, 3, 32, 4), A("offs"), ALU.subtract)
-        yield lambda: tt(A("nd", n + 8, n + 16), A("nd", n, n + 8), A("ww", 32 * s + 3, 32 * s + 32, 4), M)
-        yield lambda: tt(A("ni", 8 * s + 1, 8 * s + 8, 2), A("nd", n + 8, n + 12), A("nd", n + 12, n + 16), S)
-        if s == 1:
-            yield from digits(0, 1)
+        fo = "fo%d" % s
+        yield lambda: tt(A("nd", 48, 56), A(fo, 3, 32, 4), A("offs"), ALU.subtract)
+        yield lambda: tt(A("nd", 56, 64), A("nd", 48, 56), A("ww", 32 * s + 3, 32 * s + 32, 4), M)
+        yield lambda: tt(A("ni", 8 * s + 1, 8 * s + 8, 2), A("nd", 56, 60), A("nd", 60, 64), S)
 
-            def out():
-                quant("b", 0, 160, A("rb"))
-                carry(0)
-                carry(1)
-            yield out
+    def choices(s, tr, r):
+        bt, fo, u, n = "bt%d" % s, "fo%d" % s, phase[s] + 1, 16 * s
+
+        def one(name, i):
+            return A(name, i, i + 1)
+        lin(A("nd", n, n + 4), A(fo, 19, 32, 4), 1.0, -400.0)
+        lin(A("nd", n + 12, n + 16), A(fo, 3, 16, 4), 1.0, 16.0)
+        for m in range(3):
+            if s or not r:
+                lin(one("nd", n + 4 + m), one(tr, 64 + u + 16 * m), -1.0, one(tr, u + 16 * m))
+        for m in range(3):
+            lin(one("nd", n + 8 + m), one("nd", n + m), -1.0, one("nd", n + 12 + m))
+        for m in range(3):
+            lin(one("nf", 8 * s + 2 * m), one("nd", n + 4 + m), one(bt, 2 + 4 * m), one(tr, 64 + u + 16 * m))
+        for m in range(3):
+            lin(one("nf", 8 * s + 2 * m + 1), one("nd", n + 8 + m), one("ww", 32 * s + 3 + 4 * m), one("nd", n + m))
+
+    def carry_first(r):
+        yield lambda: copy(A("ni", 0, 8), A("nf", 0, 8))
+        yield from digits(0, 1)
+
+        def out():
+            quant("b", 0, 128 if r else 160, A("rb", 0, 512 if r else 640))
+            carry(0)
+            carry(1)
+        yield out
 
     def growth(r):
         todo = []
@@ -433,11 +446,16 @@ def rank_program(g, core, T, topo):
             bt, fo, ph = "bt%d" % s, "fo%d" % s, phase[s]
             if s == 0:
                 tr = "ts0"
-                pick(A("g0"), A("ss"), A("lab"))
-                turn(A("tr0"), A("g0"))
-                for k, cls in ((1, 11), (2, 3), (0, 3)):
-                    c = 64 * k + cls
-                    tt(A(bt, k + 1, 16, 4), A("tr0", c, 64 * k + 64, 16), A("tr0", 192 + c, 256 + 64 * k, 16), ALU.is_le)
+                if r == 0:
+                    todo.extend(lambda b=b: quant("e", 128 * b, 128 * b + 128, A("eb", 3 - b, 515 - b)) for b in range(4))
+                for k in range(3):
+                    pick(A("g0", 128 * k, 128 * k + 128), A("ss"), A("lab", 8 * k, 8 * k + 8))
+                for k in range(3):
+                    turn(A("tr0", 128 * k, 128 * k + 128), A("g0", 128 * k, 128 * k + 128))
+                gap()
+                for k, (bit, cls) in enumerate(((2, 11), (3, 3), (1, 3))):
+                    c = 128 * k + cls
+                    tt(A(bt, bit, 16, 4), A("tr0", c, 128 * k + 64, 16), A("tr0", c + 64, 128 * k + 128, 16), ALU.is_le)
             else:
                 tr = "tr%d" % s
                 pick(A("gt"), A("win", region[s], region[s] + 832), A("ll"))
@@ -446,37 +464,47 @@ def rank_program(g, core, T, topo):
                 gap()
                 for side in (0, 1):
                     tt(A(bt, 16 * side, 16 * side + 16), A(tr, ph + 1, 64, 4), A(tr, 64 + ph + 1, 128, 4), ALU.is_le)
-            f = list(first_choice(s, tr))
-            if s or not r:
-                f[0]()
-            gap()
+            f = list(first_choice(s, tr)) if s % 2 else [gap] * 3
+            f[0]()
             n = 32 if s else 16
             tt(A(bt, 3, n, 4), A(bt, 2, n, 4), A(bt, 3, n, 4), ALU.max)
             f[1]()
-            gap()
             if s:
                 scan(A(fo), A(bt), A(tr, ph, 128, 4), M, S)
             else:
                 for o in (0, 16):
                     scan(A(fo, o, o + 16), A(bt, 0, 16), A(tr, 4 * o + ph, 4 * o + 64, 4), M, S)
-                copy(A(bt, 16, 32), A(bt, 0, 16))
             f[2]()
             if s < 3:
                 copy(A("ll"), A(fo, 3, 32, 4))
-                scan(A("ww", 32 * s, 32 * s + 32), A(bt), A("pat"), M, S)
-                todo.extend(second_choice(s))
-                if s == 0:
+                k = 32 if s == 1 else 16
+                scan(A("ww", 32 * s, 32 * s + k), A(bt, 0, k), A("pat", 0, k), M, S)
+                if s == 1:
+                    todo.extend(second_choice(s))
                     if r == 0:
-                        quant("k", 0, 224, A("wr"))
-                        todo.append(lambda: copy(A("rl"), A("rlf")))
-                        todo.append(later_constants)
-                gap()
+                        ts(A("rl", 0, 2), A("rlf", 64, 128, 32), 0.125, M)
+                    todo.extend(carry_first(r))
+                else:
+                    choices(s, tr, r)
+                if s == 0:
+                    unpack((2, 3, 4, 5), 288, 416, 32)
+                if s == (0 if r else 2):
+                    if r == 0:
+                        unpack((2, 3, 4, 5), 0, 128)
+                    unpack((0, 7, 2, 3), 128, 320)
+                if s == 0 and r == 0:
+                    later_constants()
+                    todo.append(lambda: quant("k", 0, 224, A("wr")))
+                    todo.append(lambda: turn(A("rlf", 64, 128), A("rlf", 0, 64)))
+                else:
+                    gap()
             else:
                 tt(A("ni", 25, 32, 2), A(fo, 3, 16, 4), A(fo, 19, 32, 4), S)
                 gap(len(todo))
+                copy(A("ni", 16, 24), A("nf", 16, 24))
                 for f in digits(2, 3):
                     f()
-                quant("a", 0, 160, A("ra"))
+                quant("a", 0, 128 if r else 160, A("ra", 0, 512 if r else 640))
                 carry(2)
                 carry(3)
                 copy(A("nl"), P(1, 0, 20))
@@ -496,7 +524,8 @@ def rank_program(g, core, T, topo):
         for b in range(4):
             mm(4 * z + b, "e", 128 * b, "t", 160 * z, 160 * z + 160)
         for b in range(4):
-            act(A("tt", 336 * b + 160 * z, 336 * b + 160 * z + 160), P(4 * z + b, 0, 160), scale=-1.0)
+            if z == 0 or b < 3:
+                act(A("tt", 336 * b + 160 * z, 336 * b + 160 * z + 160), P(4 * z + b, 0, 160), scale=-1.0)
 
     def lists(lo, hi, out):
         for k in (1, 0):
@@ -508,9 +537,14 @@ def rank_program(g, core, T, topo):
     def minus(t):
         return A("tt", 336 * t, 336 * t + 336)
 
+    def rest_picks():
+        for t in range(4):
+            act(A("gone", 192 * t, 192 * t + 192), minus(t), off=A("ul", 8, 20))
+            mm(3 + t, "e", 128 * t, "c", 128, 320)
+
     def rest():
         for t in range(4):
-            tt(A("xt", 512 + t, 1280, 4), minus(t), A("vt", E * t + 128, E * t + C), S, off=A("ul", 8, 20))
+            tt(A("xt", 512 + t, 1280, 4), P(3 + t, 0, 192), A("gone", 192 * t, 192 * t + 192), S)
         quant("c", 128, 320, A("xt", 512, 1280))
 
     def store(lo, hi):
@@ -531,51 +565,56 @@ def rank_program(g, core, T, topo):
             if r == 0 and s > 1:
                 lay_stage(s)
             tables(s)
-        if r == 0:
-            unpack((2, 3, 4, 5), 0, 128)
-        unpack((0, 7, 2, 3), 128, 320)
-        unpack((2, 3, 4, 5), 288, 416, 32)
         for k in range(2):
             iota(A("inv%d" % k), [[0, 864]], base=-64)
+        if r == 0:
+            iota(A("ub", 384, 512), [[0, 128]])
+            for b in range(4):
+                iota(A("tt", 336 * b + 320, 336 * b + 336), [[0, 16]])
         growth(r)
         for t, z in ((1, 0), (2, 0), (3, 0), (0, 1), (1, 1), (2, 1), (3, 1)):
             take(t, z, act)
-        tt(A("nr"), A("iw"), A("late"), S, off=A("nl"))
-        copy(A("nlf", 0, 20), A("nl"))
+        tt(A("nr"), A("iw2"), A("late"), S, off=A("nl"))
+        for k in (0, 1):
+            ts(A("nlf", k, 20, 2), A("nl", k, 20, 2), 2.0, M, float(k), S)
         take(0, 0, pick)
-        tt(A("eq"), A("nlf", 0, 20), A("nr"), EQ, off=A("cidx"))
+        tt(A("eq"), A("nlf"), A("nr"), EQ, off=A("cidx"))
         layer(0)
         scan(A("scn"), A("dsc"), A("eq"), M, S)
-        for k in (0, 1):
-            ts(A("nlf", 20 + k, 40, 2), A("nl", k, 20, 2), 2.0, M, float(k), S)
-        tt(A("ad"), A("nlf", 20, 40), A("scn", 15, 320, 16), S)
+        tt(A("ad"), A("nlf"), A("scn", 15, 320, 16), S)
         for k in (0, 1):
             ts(A("adr", k, 20, 2), A("ad", k, 20, 2), K("q%d" % k), ALU.min)
-        between = {0: lambda: layer(1), 3: lambda: unpack_t(0), 6: lambda: unpack_t(1)}
+        between = {0: lambda: layer(1), 4: lambda: unpack_t(0), 7: lambda: unpack_t(1)}
         for i in range(10):
             if i in between:
                 between[i]()
             d = 18 - 10 * (i % 2) - 2 * (i // 2)
             put(A("inv%d" % (d // 10)), A("adr", d, d + 2), A("back", 16 * d, 16 * d + 32))
         lists(C, E, A("ulb"))
+        ts(A("tt", 336 * 3 + 160, 336 * 3 + 320), P(7, 0, 160), -1.0, M)
         for t in (2, 3):
             act(A("ub", t, 384, 4), minus(t), scale=-1.0, off=A("ulb"))
         for t in (0, 1):
             ts(A("ub", t, 384, 4), minus(t), -1.0, M, off=A("ulb"))
         quant("r", 0, 128, A("ub"))
         send(nxt, "r", 0, H, 128, "ra%d" % r, "rtl")
+        if r == 0:
+            quant("r", 224, 352, A("zb", 0, 512))
         lists(0, C, A("ul"))
         if last:
             act(A("nr"), A("iw"), off=A("nl"))
             dma("y", "ob", T.on[:, :], A("nr", p=(0, 128, 16)))
-            rest()
-            store(128, 320)
+        rest_picks()
         for t in range(4):
             tt(A("xf", 128 * t, 128 * t + 128), minus(t), A("vt", E * t, E * t + 128), S, off=A("ul", 0, 8))
+        if last:
+            rest()
         arrive("ra%d" % r, n_in_r, [A("qr", 128, 224), A("sr", 128, 224)])
         bb = (0, 1, 7, 2)
         for b in range(4):
             mm(bb[b], "e", 128 * b, "r", 128, 256)
+        if last:
+            store(128, 320)
         for b in range(4):
             tt(A("xt", b, 512, 4), A("xf", 128 * b, 128 * b + 128), P(bb[b], 0, 128), ALU.subtract)
         quant("c", 0, 128, A("xt", 0, 512))
@@ -584,9 +623,9 @@ def rank_program(g, core, T, topo):
         else:
             border_out(r + 1)
             score(0, 0, 128)
-            unpack((2, 3, 4, 5), 0, 128)
             rest()
             score(6, 128, 320)
+            unpack((2, 3, 4, 5), 0, 128)
             if r == 0:
                 quant("v", 0, 128, A("vin"))
     for s in SEMAPHORES:

@@ -2,6 +2,8 @@ from concourse.mybir import dt, AluOpType as ALU, ActivationFunctionType as AF
 
 ROUNDS = 3
 C, H, E = 320, 96, 416
+BIG = 1.5 * 2.0 ** 28
+FLUX = "ns1 ms02 ns0 ms03 ms10 ms11 ms12 mv00 mv01 ev1 kv sv1 ev0 av1 lv0 sv0 bv1 mv13 pv4 lv1 ts00 ts01 ts02 ts03 ts10 ts11 ts12 ts13 av0 pv3 bv0 pv2 uv0 pv1 uv1 pv0 is00 is01 is02 is03 iv10 is11 is12 is13"
 SCRATCH = {}
 
 
@@ -11,20 +13,20 @@ def _declare(kind, names):
         SCRATCH[n] = ("psum" if n.startswith("ps") else "sbuf", [128, int(c)], kind)
 
 
-_declare("bfloat16", "xt:1280 ut:512 vin:512 zb:516 eb:516 vt:1664 mt:1280 tb:1280 tt:1344 ub:512 wr:896 ra:640 rb:640 gone:768 dsc:320 eq:320 scn:320")
-_declare("bfloat16", "inv0:864 inv1:864 dia2:832 back:320")
-_declare("float16", "dg0:832 dg1:832")
-_declare("int32", "lri:104 bli:78 cpi:26 pi:2 pa:6 ni:32 lo5:32 dg:64")
-_declare("uint16", "lru:52 bl:78 l0:16 ll:8 cidx:20 nl:20 adr:20 ul:20 ulb:6 lz:8 lab:24 rl:2")
+_declare("bfloat16", "xt:1280 ut:512 vin:512 zb:640 eb:516 vt:1664 mt:1280 tb:1280 tt:1344 ub:512 wr:896 ra:640 rb:640 gone:896 dsc:320 eq:320 scn:320")
+_declare("bfloat16", "inv:3072 dia:416 dia4:384 back:320")
+_declare("float16", "dgb:384 dgo:1280")
+_declare("int32", "lri:128 bli:78 cpi:26 pi:2 pa:7")
+_declare("uint16", "lru:64 lo16:4 bl:78 l0:16 ll:8 cidx:20 nl:20 adr:20 ul:20 ulb:6 lz:8 lab:24 rl:2")
 _declare("float8_e4m3fn_x4", "qw:512 qu:128 q0:128 qv:128 qe:512 qc:416 qm:320 qt:320 qr:352 qa:160 qb:160 qk:224")
 _declare("uint8", "sw:512 su:128 s0:128 sv:128 se:512 sc:416 sm:320 st:320 sr:352 sa:160 sb:160 sk:224")
-_declare("float32", "i32:96 iw:416 cs:208 dia:416 offs:8 pf:5 kk:32 cf:16 ls:156 l0f:16 rlf:128")
-_declare("float32", "aiw:416 biw:416 base:416 gr2:416 r2:416 ur:416 rc:416 t1:416 t2:416 t3:416 win:2496 sums:24 pat:32")
+_declare("float32", "i32:96 iw:416 cs:208 offs:8 lzf:8 pf:7 kk:32 dgf:64 df0:32 l0f:16 rlf:128")
+_declare("float32", "aiw:416 giw:416 one:416 two:416 both:416 dx:416 dy:416 dz:416 win:2496 pat:32")
 _declare("float32", "g0:384 tr0:384 ts0:256 gt:128 tr1:128 tr2:128 tr3:128 bt0:32 bt1:32 bt2:32 bt3:32 fo0:32 fo1:32 fo2:32 fo3:32")
-_declare("float32", "nd:64 nf:24 ww:96 nlf:20 iw2:416 late:320 ss:416 sn:1248 nr:320")
-_declare("float32", "ad:20 dm:26 xf:512 ysb:320")
+_declare("float32", "nd:64 nf:28 ww:96 nlf:20 nlk:20 kpat:20 ss:416 sn:1248 nr:320")
+_declare("float32", "ad:20 xf:384 ysb:320 nr4:320")
 _declare("float32", "ps0:512 ps1:512 ps2:512 ps3:512 ps4:512 ps5:512 ps6:512 ps7:512")
-SEMAPHORES = "cv cs ct cg lx0 lx1 llr lb lc lu lv lw k0 k1 k2 k3 t1 t2 t3 rp ob bl rtl ba0 ba1 ba2 ra0 ra1 ra2".split()
+SEMAPHORES = "cv cs ct cg lx0 lx1 llr lb lc lu lv lw lz ka k0 k1 k2 k3 t1 t2 t3 rp bl rtl ba0 ba1 ba2 ra0 ra1 ra2 ob".split()
 
 
 def rank_program(g, core, T, topo):
@@ -188,9 +190,9 @@ def rank_program(g, core, T, topo):
         for b in range(4):
             act(A("vt", E * b + lo + skip, E * b + hi), P(banks[b], skip, hi - lo))
 
-    def score(bank, lo, hi, skip=0):
+    def score(bank, lo, hi, skip=0, cut=0):
         mm(bank, "0", 0, "c", lo, hi)
-        act(A("ss", lo + skip, hi), P(bank, skip, hi - lo), AF.Abs)
+        act(A("ss", lo + skip, hi - cut), P(bank, skip, hi - lo - cut), AF.Abs)
 
     def border_out(r):
         send(prv, "c", 0, H, C, "ba%d" % r, "bl")
@@ -204,13 +206,13 @@ def rank_program(g, core, T, topo):
     def few(n):
         return A("i32", 0, n)
 
-    dma("y", "lx0", A("xt", 0, 512), T.x[:, 0:512])
     dma("s", "llr", A("lri", 0, 26), T.lf[:, :])
-    dma("s", "llr", A("lri", 52, 78, p=(16, 128)), T.rt[0:112, :])
     dma("y", "llr", A("lri", 26, 52, p=(0, 112)), T.lf[16:128, :])
-    dma("s", "llr", A("lri", 78, 104), T.rt[:, :])
-    dma("y", "llr", A("lri", 26, 52, p=(112, 128)), rows(T.lf, 0))
+    dma("s", "llr", A("lri", 52, 78, p=(16, 128)), T.rt[0:112, :])
+    dma("y", "llr", A("lri", 78, 104), T.rt[:, :])
     dma("s", "llr", A("lri", 52, 78, p=(0, 16)), rows(T.rt, 0))
+    dma("y", "llr", A("lri", 26, 52, p=(112, 128)), rows(T.lf, 0))
+    dma("s", "lx0", A("xt", 0, 512), T.x[:, 0:512])
     dma("y", "lu", A("ut"), T.u[:, :])
     dma("y", "lx1", A("xt", 512, 1280), T.x[:, 512:1280])
     pi = A("pi")
@@ -218,14 +220,16 @@ def rank_program(g, core, T, topo):
     iota(A("i32", 0, 32), [[1, 32]])
     iota(A("i32", 32, 96), [[0, 4], [1, 16]])
     iota(A("iw"), [[1, 416]])
-    iota(A("win", 0, 832), [[0, 832]])
+    iota(A("win", 0, 416), [[0, 416]], base=1)
     fill(A("bli"), 0)
+    fill(A("win", 416, 832), 0.0)
     for s in (1, 2, 3):
-        for t, gi, h in ((T.rt, 2 * s + 1, 1), (T.lf, 2 * s, 2), (T.rt, 2 * s, 3), (T.lf, 2 * s + 1, 5)):
+        for t, gi, h in ((T.rt, 2 * s + 1, 1), (T.lf, 2 * s, 2), (T.rt, 2 * s, 3), (T.lf, 2 * s + 1, 4)):
             dma("y", "lb", A("bli", 26 * s - 26, 26 * s, p=grp(h)), rows(t, gi))
 
     lin(A("bt0", 0, 16, 4), few(4), 0.0, 0.0)
-    lin(A("nf"), few(24), 0.0, 16.0)
+    lin(A("nf"), few(28), 0.0, 0.0)
+    lin(A("df0", 0, 2), few(2), 0.0, 16.0)
     for lo, hi, st, c in ((0, 16, 2, 1.0), (16, 32, 2, -1.0), (1, 16, 4, -1.0), (17, 32, 2, 1.0), (3, 16, 4, 0.0)):
         lin(A("pat", lo, hi, st), few(16 // st), 0.0, c)
 
@@ -239,195 +243,211 @@ def rank_program(g, core, T, topo):
                 for lo in range(w, min(n, T[name].shape[1]), w):
                     hi = min(lo + w, n)
                     dma("y", "rp", A(name, lo, hi), A(name, 0, hi - lo))
-    fields(0, (16, 3, 15))
-    e16, m4, q, t8, a32 = [A("pf", i, i + 1) for i in range(5)]
-    ei, mi = A("pa", 0, 1), A("pa", 1, 2)
+    fields(0, (16, 1, 15, 96, 3, 8, 4))
+    e16, odd, q, a32, m4, t8, t4 = [A("pf", i, i + 1) for i in range(7)]
+    ei, oi, mi = A("pa", 0, 1), A("pa", 1, 2), A("pa", 4, 5)
     d16, d64 = A("cs", 16, 32), A("cs", 16, 80)
     ts(K("sg"), ei, -0.125, M, 1.0, S)
-    ts(K("o1"), ei, 0.1875, M)
-    ts(K("o2"), ei, 0.0625, M, 1.0, S)
-    copy(A("pf", 0, 3), A("pa", 0, 3))
-    ts(K("z"), mi, K("sg"), M, K("o1"), S)
-    ts(K("z2"), mi, K("sg"), M, K("o2"), S)
+    ts(K("ns"), ei, 0.125, M, -1.0, S)
     ts(K("nl"), A("pi", 0, 1), 96.0, ALU.is_lt)
+    copy(A("pf"), A("pa"))
+    fill(A("lri", 104, 128), 0)
+    ts(K("o2"), oi, 2.0, M, -1.0, S)
+    copy(K("p"), A("pi", 0, 1))
+    ts(K("g"), oi, K("ns"), M, K("sg"), S)
+    ts(K("lo"), ei, 3.25, M, q, S)
+    ts(K("a"), K("o2"), K("sg"), M, K("nl"), M)
+    ts(K("mid"), A("pi", 0, 1), 32.0, ALU.is_ge, K("nl"), M)
+    ts(A("lo16"), few(4), 16.0, M, K("lo"), S)
     ts(d64, A("i32", 32, 96), q, ALU.subtract)
-    ts(A("cf", 0, 4), few(4), K("z"), EQ)
-    ts(A("cf", 4, 8), few(4), K("z2"), EQ)
-    ts(K("e1"), mi, 3.0, EQ, e16, M)
-    ts(K("e3"), A("pi", 0, 1), 96.0, ALU.is_ge, K("z"), M)
-    tt(A("cf", 8, 12), A("cf", 0, 4), A("cf", 4, 8), ALU.subtract)
-    ts(K("od"), ei, 0.0625, M)
-    ts(K("ev"), ei, -0.0625, M, 1.0, S)
-    ts(A("cf", 12, 16), A("cf", 8, 12), K("nl"), M)
-    act(A("biw"), A("iw"), scale=A("cf", 10, 11))
-    act(A("aiw"), A("iw"), scale=A("cf", 13, 14))
+    ts(K("far"), ei, 26.0, M, K("mid"), M)
     ts(A("cs", 80, 144), d64, 0.0, EQ, -4000.0, M)
     ts(A("cs", 144, 208), d64, 1.0, EQ, 2000.0, M)
-    ts(K("e2"), K("e1"), 26.0, M, K("nl"), M)
-    ts(K("e4"), K("e3"), 3.0, EQ, 16.0, M)
+    pick(A("lru"), A("lri"), A("lo16"))
     tt(A("dia", 0, 64), A("cs", 80, 144), A("cs", 144, 208), S)
-    repeat(["dia"], ((64, 416),))
-    ts(A("ls", 0, 52), A("lri", 0, 52), K("ev"), M)
-    ts(K("eps"), K("e4"), K("ev"), M, K("e2"), S)
-    lin(A("base"), A("iw"), A("cf", 15, 16), K("eps"))
-    ts(A("ls", 52, 104), A("lri", 52, 104), K("od"), M)
-    ts(K("ub"), ei, -256.0, M, 4112.0, S)
-    fields(3, (8,))
-    tt(A("ls", 104, 156), A("ls", 0, 52), A("ls", 52, 104), S)
     quant("c", 0, 128, A("xt", 0, 512))
     border_out(0)
-    copy(A("lru"), A("ls", 104, 156))
-    fields(4, (96,))
-    iota(A("zb"), [[0, 516]])
-    eb, zb = A("eb"), A("zb")
-    op("g", lambda: g.affine_select(eb["ap"], zb["ap"], [[1, 516]], ALU.not_equal, 1.0, -3, -4), [eb], [zb])
-    iota(A("offs"), [[416, 2], [0, 4]], base=-16)
-    iota(A("win", 832, 2496), [[0, 1664]])
-    for e in (0, 1):
-        for lo, first, step in ((0, 32 * e, 64), (32, 1024 + 64 * e, 32)):
-            iota(A("rlf", lo + 16 * e, lo + 16 * e + 8), [[step, 2], [8, 4]], 4, first)
-            iota(A("rlf", lo + 16 * e + 8, lo + 16 * e + 16), [[128, 2], [8, 4]], 1, 512 + 256 * e + 32 * lo)
-    for n in ("rb", "ra"):
-        iota(A(n), [[0, T[n].shape[1]]])
-    iota(A("iw2"), [[2, 416]])
-    iota(A("dsc"), [[0, 320]], base=1)
-    iota(A("dsc", 0, 320, 16), [[0, 20]])
-    iota(A("dsc", 15, 320, 16), [[0, 20]], base=1000)
-    iota(A("back"), [[-1, 320]], base=256)
-    l1, l2 = A("lru", 0, 26), A("lru", 26, 52)
-    act(A("r2"), A("iw"), off=l2)
-    tt(A("t1"), A("aiw"), A("base"), S, off=l1)
-    act(A("gr2"), A("r2"), scale=A("cf", 8, 9))
-    act(A("ur"), A("iw"), AF.Identity, bias=K("ub"), off=l1)
-    copy(K("p"), A("pi", 0, 1))
-    ts(K("r2"), mi, 3.0, EQ, -128.0, M)
-    tt(A("t2"), A("biw"), A("t1"), S, off=l2)
-    act(A("rc"), A("r2"), off=l1)
-    copy(A("pf", 3, 5), A("pa", 3, 5))
-    ts(K("r1"), mi, 32.0, M, K("r2"), S)
-    tt(A("t3"), A("gr2"), A("t2"), S, off=l1)
-    ts(K("r3"), t8, -2.0, M, K("r1"), S)
-    quant("u", 0, 128, A("ut"))
-    phase, region = (2, 0, 0, 0), (0, 0, 832, 1664)
+    lin(A("lzf"), few(8), 0.0, 0.0)
+    lin(K("u1"), t4, 8.0, 32.0)
+    lin(K("u3"), t8, -2.0, -32.0)
+    lin(A("lzf", 2, 4), few(2), 0.0, -16.0)
+    act(A("giw"), A("iw"), scale=K("g"))
+    act(A("aiw"), A("iw"), scale=K("a"))
 
-    def lay_stage(s):
-        c = phase[s]
-        for side in (0, 1):
-            gi, lo = 2 * s + side, region[s] + 416 * side
-            for src, dst, p in (("ur", (c + 1, 128, 16), (16 * gi, 16 * gi + 8)), ("t3", (c, 64, 4), grp(gi)), ("t3", (c + 64, 128, 4), grp(gi))):
-                dma("y", "k%d" % s, A("win", lo, lo + 416, p=dst), A(src, p=p))
-    lay_stage(0)
-    ts(K("hs"), q, 15.0, ALU.is_lt, 2000.0, M)
-    ts(A("lz"), A("zb", 0, 8), 48.0, S, K("r3"), S)
-    scan(A("t1"), A("dia"), A("rc"), S, ALU.max)
-    ts(K("w0"), q, 96.0, S)
-    ts(A("cs", 0, 16), d16, 0.0, ALU.is_ge, 1000.0, M)
-    ts(A("cpi"), A("t1", 15, 416, 16), K("hs"), ALU.subtract)
-    for s in (1, 2, 3):
-        for side in (0, 1):
-            dma("y", "lc", A("bli", 26 * s - 26, 26 * s, p=grp(6 * side)), A("cpi", p=grp(2 * s + side)))
-    dma("y", "lw", A("qw", bits=dt.uint8), T.wc[:, :])
-    dma("y", "lw", A("sw"), T.ws[:, :])
-    dma("y", "lv", A("vin"), T.v[:, :])
+    def empty(s):
+        iota(A("win", 832 * s, 832 * s + 832), [[-1, 2], [0, 416]], base=1)
+    l1, l2 = A("lru", 0, 26), A("lru", 26, 52)
+    act(A("two"), A("iw"), off=l2)
+    ts(K("b"), oi, K("ns"), M)
+    copy(A("dia", 64, 128), A("dia", 0, 64))
+    tt(A("dx"), A("giw"), A("aiw"), S, off=l2)
     lin(K("b0"), K("p"), 2.0, 0.0)
     lin(K("b2"), a32, 0.5, q)
+    act(A("both"), A("two"), AF.Identity, bias=K("far"), off=l1)
+    act(A("one"), A("iw"), off=l1)
+    act(A("dy"), A("two"), scale=K("b"))
+    copy(A("dia", 128, 256), A("dia", 0, 128))
+    ts(K("hs"), q, 15.0, ALU.is_lt, 2000.0, M)
+    ts(K("w1"), mi, 1.0, EQ, K("u1"), M)
+    copy(A("dia", 256, 416), A("dia", 0, 160))
+    ts(K("w3"), mi, 3.0, EQ, K("u3"), M)
+    tt(K("h2"), K("hs"), K("far"), S)
+    ts(K("r1"), mi, 3.0, ALU.not_equal)
+    quant("u", 0, 128, A("ut"))
+    ts(K("r3"), K("w1"), K("w3"), S, 48.0, S)
+    scan(A("sn", 0, 416), A("dia"), A("both"), S, ALU.max)
+    ts(A("lz"), A("lzf"), K("r1"), M, K("r3"), S)
+    ts(A("cpi"), A("sn", 15, 416, 16), K("h2"), ALU.subtract)
     lin(K("b4"), a32, 1.0, K("p"))
     lin(K("b0"), q, -1.0, K("b0"))
-    lin(K("b3"), K("b2"), 1.0, 256.0)
-    lin(K("b5"), K("b4"), 1.0, 32.0)
-    lin(K("b1"), K("b0"), 1.0, 16.0)
-    for i, b in enumerate(("b0", "b1", "b3", "b3", "b4", "b5", "b3", "b3")):
-        lo = 8 * (i // 4)
-        lin(A("l0f", lo + i % 4, lo + 8, 4), few(2), 416.0, K(b))
-    ts(A("wr", 0, 896, 4), A("iw", 0, 224), K("w0"), EQ)
-    pick(A("q0", bits=dt.uint32), A("qu", bits=dt.uint32), A("lz"))
     s0, su, lz = A("s0"), A("su"), A("lz")
     op("s", lambda: g.scalar.activation(s0["ap"], su["ap"].indirect(lz["ap"]), AF.Copy), [s0], [su, lz])
+    lin(A("l0f", 8, 10), few(2), 32.0, K("b4"))
+    lin(A("l0f", 0, 2), few(2), 16.0, K("b0"))
+    for c in (2, 3):
+        lin(A("l0f", c, 16, 8), A("df0", 0, 2), 16.0, K("b2"))
+    phase, region, first = (0, 0, 0, 0), (0, 832, 1664, 0), (7, 2, 2, 2)
+
+    def lay(sem, lo, c, src, gi, odd=0):
+        dma("y", sem, A("win", lo, lo + 416, p=(c, 128, 16)), A(src, p=(16 * gi + odd, 16 * gi + 16, 2)))
+
+    def lay_stage(s, late):
+        ends = (("dz", 0), ("dz", 1), ("dx", 0), ("iw", 0)), (("dx", 0), ("dz", 1), ("dz", 0), ("both", 0))
+        picks = (("both", 0), ("dy", 1), ("two", 0), ("dy", 0)), (("dx", 0), ("two", 0), ("dz", 0), ("both", 0))
+        for side in (0, 1):
+            gi, lo = 2 * s + side, region[s] + 416 * side
+            for c, (src, odd) in zip((0, 4, 8, 12, first[s]), (ends if s < 3 else picks)[side] + (("one", 0),)):
+                if (src == "dz") == late:
+                    lay("k%d" % s, lo, c, src, gi, odd)
+    lay("ka", 0, 15, "iw", 0)
+    for c, src in (((11, 3), "two"), ((3, 11), "both")):
+        for side in (0, 1):
+            lay("ka", 416 * side, c[side], src, side)
+    for side in (0, 1):
+        lay("ka", 416 * side, 7, "one", side)
+    for s in (1, 2, 3):
+        for side in (0, 1):
+            dma("y", "lc", A("bli", 26 * s - 26, 26 * s, p=grp(5 * side)), A("cpi", p=grp(2 * s + side)))
+    pick(A("q0", bits=dt.uint32), A("qu", bits=dt.uint32), A("lz"))
+    for c in (8, 0):
+        lin(A("l0f", c + 4, c + 8), A("l0f", c, c + 4), 1.0, 416.0)
     quant("c", 128, 320, A("xt", 512, 1280))
+    tt(A("dz"), A("dx"), A("dy"), S, off=l1)
+    copy(A("l0"), A("l0f"))
+    fill(A("zb"), 0.0)
+    empty(1)
+    lay_stage(1, False)
+    lay_stage(1, True)
+    dma("y", "lu", A("rb"), A("zb"))
+    empty(2)
+    lay_stage(2, False)
+    eb, zb = A("eb"), A("zb", 0, 516)
+    op("g", lambda: g.affine_select(eb["ap"], zb["ap"], [[1, 516]], ALU.not_equal, 1.0, -3, -4), [eb], [zb])
+    iota(A("offs"), [[416, 2], [0, 4]])
+    for e in (0, 1):
+        iota(A("rlf", 16 * e, 16 * e + 8), [[64, 2], [8, 4]], 4, 32 * e)
+        iota(A("rlf", 16 * e + 8, 16 * e + 16), [[128, 2], [8, 4]], 1, 512 + 256 * e)
+        for k in (0, 1):
+            lo = 32 + 16 * e + 8 * k
+            iota(A("rlf", lo, lo + 4), [[32, 2], [8, 2]], 4, 1024 + 64 * e + 16 * k)
+            iota(A("rlf", lo + 4, lo + 8), [[128, 2], [8, 2]], 1, 1536 + 256 * e + 16 * k)
+    iota(A("kpat"), [[0, 5], [1, 4]], base=4)
+    iota(A("back"), [[-1, 320]], base=256)
     score(0, 0, 128)
     score(6, 128, 320)
-    act(A("wr", 1, 896, 4), A("wr", 0, 896, 4))
-    for t in (2, 3):
-        act(A("wr", t, 64, 4), A("wr", 0, 64, 4))
-        act(A("wr", 64 + t, 896, 4), A("wr", 0, 832, 4))
-    copy(A("l0"), A("l0f"))
-    pick(A("g0", 128, 256), A("win", 0, 832), A("l0", 8, 16))
-    pick(A("g0", 0, 128), A("win", 0, 832), A("l0", 0, 8))
-    lay_stage(1)
-    turn(A("ts0", 128, 256), A("g0", 128, 256))
-    turn(A("ts0", 0, 128), A("g0", 0, 128))
-    v = [A("ts0", 128 + 14 - 4 * i, 256, 16) for i in range(4)]
-    tt(A("sums", 0, 8), v[0], v[1], S)
-    ts(A("lab", 12, 16), A("ts0", 192 + 14, 256, 16), 416.0, ALU.subtract)
-    copy(A("cidx"), few(20))
-    tt(A("sums", 8, 16), A("sums", 0, 8), v[2], S)
+    act(A("g0", 128, 256), A("win", 0, 832), off=A("l0", 8, 16))
+    act(A("gt"), A("win", 0, 832), off=A("l0", 0, 8))
+    ts(K("w0"), q, 96.0, S)
     copy(A("bl"), A("bli"))
-    copy(A("lab", 8, 12), A("sums", 0, 4))
-    ts(A("lab", 4, 8), A("sums", 4, 8), 416.0, ALU.subtract)
-    tt(A("sums", 16, 20), A("sums", 8, 12), A("ts0", 128 + 2, 192, 16), S)
-    copy(A("lab", 0, 4), A("sums", 8, 12))
-    ts(A("lab", 20, 24), A("sums", 12, 16), 416.0, ALU.subtract)
-    copy(A("lab", 16, 20), A("sums", 16, 20))
+    turn(A("ts0", 128, 256), A("g0", 128, 256))
+    ts(A("cs", 0, 16), d16, 0.0, EQ)
+    copy(A("cidx"), few(20))
+    for k, c in enumerate((7, 11, 3)):
+        copy(A("lab", 8 * k, 8 * k + 8), A("ts0", 128 + c, 256, 16))
+    turn(A("ts0", 0, 128), A("gt"))
+
+    def in_gaps():
+        yield lambda: (fill(A("ub", 384, 512), 0.0), fill(A("tt", C, 1344, 336), 0.0))
+        yield lambda: ts(A("wr", 0, 896, 4), A("iw", 0, 224), K("w0"), EQ)
+        for b in range(4):
+            yield lambda b=b: quant("e", 128 * b, 128 * b + 128, A("eb", 3 - b, 515 - b))
+
+    def first_differences():
+        yield lambda: tt(A("df0", 0, 16), A("ts0", 3, 64, 4), A("ts0", 7, 68, 4), ALU.subtract)
+        yield lambda: tt(A("df0", 17, 32), A("ts0", 67, 124, 4), A("ts0", 71, 128, 4), ALU.subtract)
+        yield lambda: copy(A("df0", 3, 16, 4), A("ts0", 15, 64, 16))
+        yield lambda: ts(A("df0", 19, 32, 4), A("ts0", 75, 128, 16), 416.0, S)
+        yield lambda: tt(A("df0", 16, 32, 4), A("ts0", 15, 64, 16), A("ts0", 67, 128, 16), ALU.subtract)
+
+    def leads():
+        act(A("wr", 1, 896, 4), A("wr", 0, 896, 4))
+        for t in (2, 3):
+            act(A("wr", t, 64, 4), A("wr", 0, 64, 4))
+            act(A("wr", 64 + t, 896, 4), A("wr", 0, 832, 4))
 
     def later_constants():
-        lin(A("late", 0, 16), A("cs", 0, 16), 1.0, 0.0)
-        lin(A("late", 16, 32), A("cs", 0, 16), 1.0, 1.0)
-        lin(A("dia2", 0, 32, 2), A("dia", 0, 16), 0.5, 0.0)
-        lin(A("dia2", 1, 32, 2), few(16), 0.0, 0.0)
-        for k in (0, 1):
-            lin(K("q%d" % k), q, 2.0, 832.0 + k)
+        for k in range(4):
+            lin(K("q%d" % k), q, 64.0, 2047.0 + 16 * k)
+        for k in range(4):
+            lin(A("dia4", k, 64, 4), A("dia", 0, 16), 0.0 if k else 0.5, 0.0)
+        for k in range(4):
+            lin(A("dsc", 16 * k, 16 * k + 16), A("cs", 0, 16), K("q%d" % k), 1.0)
         lin(K("h3"), K("hs"), 0.5, 256.0)
-        repeat(["late", "dia2"], ((32, 160), (160, 832)))
+        lin(A("dsc", 0, 64, 16), few(4), 0.0, 0.0)
+        repeat(["dsc", "dia4"], ((64, 384),))
 
     def tables(s):
         act(A("sn", 416 * s - 416, 416 * s), A("ss"), off=A("bl", 26 * s - 26, 26 * s))
+        if s == 1:
+            for h in range(6):
+                lo = region[1] + 416 * (h % 2)
+                dma("ys"[h % 2], "t1", A("win", lo, lo + 416, p=(5 + 4 * (h // 2), 128, 16)), A("sn", 0, 416, p=(16 * h, 16 * h + 16, 2)))
+            return
         for h in range(8):
-            c = 16 * h + phase[s] + 5
-            dma("s" if s == 1 and h % 2 else "y", "t%d" % s, A("win", region[s], region[s] + 832, p=(c, c + 9, 4)), A("sn", 416 * s - 416, 416 * s, p=(s - 1, s + 100, 20)))
+            dma("y", "t%d" % s, A("win", region[s], region[s] + 832, p=(16 * h + 5, 16 * h + 14, 4)), A("sn", 416 * s - 416, 416 * s, p=(4 * s - 7, 96, 16)))
 
     def carry(s):
         x, lo = "ba"[s // 2], 32 * (s % 2)
         mm(1, "k", 96 - 32 * s, x, lo, lo + 128, s == 0, s == 3)
 
-    def digits(lo, s):
-        n, low, c = A("ni", 8 * lo, 8 * s + 8), A("lo5", 8 * lo, 8 * s + 8), 2 * (lo % 2)
-        yield lambda: ts(low, n, 31, ALU.bitwise_and)
-        yield lambda: ts(A("dg", 16 * lo, 16 * s + 16, 2), n, 480, ALU.bitwise_and)
-        yield lambda: ts(A("dg", 16 * lo + 1, 16 * s + 16, 2), low, 16.0, ALU.subtract)
-        yield lambda: put(A("ra" if s == 3 else "rb"), A("rl", c, c + s - lo + 1), A("dg", 16 * lo, 16 * s + 16))
+    def high(n, lo, hi):
+        ts(A("dgf", lo, hi, 2), n, BIG, S, BIG, ALU.subtract)
+
+    def low(n, lo, hi):
+        tt(A("dgf", lo + 1, hi, 2), n, A("dgf", lo, hi, 2), ALU.subtract)
 
     def first_choice(s, tr):
-        bt, u, n = "bt%d" % s, phase[s] + 1, 16 + 8 * (s // 2)
+        bt, u, n = "bt%d" % s, first[s], 16 + 8 * (s // 2)
         yield lambda: tt(A("nd", n, n + 4), A(tr, u, 64, 16), A(tr, 64 + u, 128, 16), ALU.subtract)
         yield lambda: tt(A("nd", n + 4, n + 8), A("nd", n, n + 4), A(bt, 2, 16, 4), M)
-        yield lambda: tt(A("ni", 8 * s, 8 * s + 8, 2), A("nd", n + 4, n + 8), A(tr, 64 + u, 128, 16), S)
+        yield lambda: tt(A("nf", 8 * s, 8 * s + 4), A("nd", n + 4, n + 8), A(tr, 64 + u, 128, 16), S)
 
     def second_choice(s):
         fo = "fo%d" % s
         yield lambda: tt(A("nd", 48, 56), A(fo, 3, 32, 4), A("offs"), ALU.subtract)
         yield lambda: tt(A("nd", 56, 64), A("nd", 48, 56), A("ww", 32 * s + 3, 32 * s + 32, 4), M)
-        yield lambda: tt(A("ni", 8 * s + 1, 8 * s + 8, 2), A("nd", 56, 60), A("nd", 60, 64), S)
+        yield lambda: tt(A("nf", 12, 16), A("nd", 56, 60), A("nd", 60, 64), S)
 
     def choices(s, tr, r):
-        bt, fo, u, n = "bt%d" % s, "fo%d" % s, phase[s] + 1, 16 * s
+        bt, fo, u, n = "bt%d" % s, "fo%d" % s, first[s], 16 * s
 
         def one(name, i):
             return A(name, i, i + 1)
-        lin(A("nd", n, n + 4), A(fo, 19, 32, 4), 1.0, -400.0)
-        lin(A("nd", n + 12, n + 16), A(fo, 3, 16, 4), 1.0, 16.0)
+        lin(A("nd", n, n + 4), A(fo, 19, 32, 4), 1.0, -416.0)
         for m in range(3):
             if s or not r:
                 lin(one("nd", n + 4 + m), one(tr, 64 + u + 16 * m), -1.0, one(tr, u + 16 * m))
         for m in range(3):
-            lin(one("nd", n + 8 + m), one("nd", n + m), -1.0, one("nd", n + 12 + m))
+            lin(one("nd", n + 8 + m), one("nd", n + m), -1.0, one(fo, 3 + 4 * m))
         for m in range(3):
             lin(one("nf", 8 * s + 2 * m), one("nd", n + 4 + m), one(bt, 2 + 4 * m), one(tr, 64 + u + 16 * m))
         for m in range(3):
             lin(one("nf", 8 * s + 2 * m + 1), one("nd", n + 8 + m), one("ww", 32 * s + 3 + 4 * m), one("nd", n + m))
 
     def carry_first(r):
-        yield lambda: copy(A("ni", 0, 8), A("nf", 0, 8))
-        yield from digits(0, 1)
+        yield lambda: high(A("nf", 0, 16), 32, 64)
+        yield lambda: low(A("nf", 0, 16), 32, 64)
+        yield lambda: put(A("rb"), A("rl"), A("dgf", 32, 64))
 
         def out():
             quant("b", 0, 128 if r else 160, A("rb", 0, 512 if r else 640))
@@ -447,11 +467,24 @@ def rank_program(g, core, T, topo):
             if s == 0:
                 tr = "ts0"
                 if r == 0:
-                    todo.extend(lambda b=b: quant("e", 128 * b, 128 * b + 128, A("eb", 3 - b, 515 - b)) for b in range(4))
+                    todo.extend(first_differences())
                 for k in range(3):
                     pick(A("g0", 128 * k, 128 * k + 128), A("ss"), A("lab", 8 * k, 8 * k + 8))
+                gap(2)
                 for k in range(3):
                     turn(A("tr0", 128 * k, 128 * k + 128), A("g0", 128 * k, 128 * k + 128))
+                gap(3)
+                if r == 0:
+                    todo.extend(in_gaps())
+                    lay_stage(2, True)
+                    lay_stage(3, True)
+                    tables(2)
+                    lay_stage(3, False)
+                    tables(3)
+                    dma("y", "lz", A("ra"), A("zb"))
+                    dma("y", "lw", A("qw", bits=dt.uint8), T.wc[:, :])
+                    dma("y", "lw", A("sw"), T.ws[:, :])
+                    dma("y", "lv", A("vin"), T.v[:, :])
                 gap()
                 for k, (bit, cls) in enumerate(((2, 11), (3, 3), (1, 3))):
                     c = 128 * k + cls
@@ -462,48 +495,53 @@ def rank_program(g, core, T, topo):
                 gap()
                 turn(A(tr), A("gt"))
                 gap()
-                for side in (0, 1):
+                for side in (0, 1) if s < 3 else (0,):
                     tt(A(bt, 16 * side, 16 * side + 16), A(tr, ph + 1, 64, 4), A(tr, 64 + ph + 1, 128, 4), ALU.is_le)
             f = list(first_choice(s, tr)) if s % 2 else [gap] * 3
+            if s == 1:
+                gap()
             f[0]()
-            n = 32 if s else 16
+            if s == 3:
+                tt(A(fo, 16, 32), A(tr, 0, 64, 4), A(tr, 64, 128, 4), S)
+            n = 32 if s in (1, 2) else 16
             tt(A(bt, 3, n, 4), A(bt, 2, n, 4), A(bt, 3, n, 4), ALU.max)
             f[1]()
-            if s:
+            if s == 3:
+                scan(A(fo, 0, 16), A(bt, 0, 16), A(fo, 16, 32), M, S)
+            elif s:
                 scan(A(fo), A(bt), A(tr, ph, 128, 4), M, S)
             else:
                 for o in (0, 16):
-                    scan(A(fo, o, o + 16), A(bt, 0, 16), A(tr, 4 * o + ph, 4 * o + 64, 4), M, S)
+                    scan(A(fo, o, o + 16), A(bt, 0, 16), A("df0", o, o + 16), M, S)
             f[2]()
             if s < 3:
                 copy(A("ll"), A(fo, 3, 32, 4))
                 k = 32 if s == 1 else 16
                 scan(A("ww", 32 * s, 32 * s + k), A(bt, 0, k), A("pat", 0, k), M, S)
                 if s == 1:
+                    if r == 0:
+                        turn(A("rlf", 64, 128), A("rlf", 0, 64))
                     todo.extend(second_choice(s))
                     if r == 0:
-                        ts(A("rl", 0, 2), A("rlf", 64, 128, 32), 0.125, M)
+                        todo.insert(1, lambda: (ts(A("rl", 0, 2), A("rlf", 64, 128, 32), 0.125, M), quant("k", 0, 224, A("wr"))))
                     todo.extend(carry_first(r))
                 else:
                     choices(s, tr, r)
-                if s == 0:
-                    unpack((2, 3, 4, 5), 288, 416, 32)
                 if s == (0 if r else 2):
-                    if r == 0:
-                        unpack((2, 3, 4, 5), 0, 128)
+                    unpack((2, 3, 4, 5), 288, 416, 32)
                     unpack((0, 7, 2, 3), 128, 320)
+                    if r == 0:
+                        unpack((4, 5, 0, 7), 0, 128)
                 if s == 0 and r == 0:
+                    leads()
                     later_constants()
-                    todo.append(lambda: quant("k", 0, 224, A("wr")))
-                    todo.append(lambda: turn(A("rlf", 64, 128), A("rlf", 0, 64)))
-                else:
-                    gap()
+                gap()
             else:
-                tt(A("ni", 25, 32, 2), A(fo, 3, 16, 4), A(fo, 19, 32, 4), S)
                 gap(len(todo))
-                copy(A("ni", 16, 24), A("nf", 16, 24))
-                for f in digits(2, 3):
-                    f()
+                for digit in (high, low):
+                    digit(A(fo, 3, 16, 4), 24, 32)
+                    digit(A("nf", 16, 28), 0, 24)
+                put(A("ra"), A("rl"), A("dgf", 0, 32))
                 quant("a", 0, 128 if r else 160, A("ra", 0, 512 if r else 640))
                 carry(2)
                 carry(3)
@@ -512,47 +550,59 @@ def rank_program(g, core, T, topo):
     def take(t, z, how):
         how(A("mt", 640 * z + t, 640 * z + 640, 4), A("vt", E * t, E * t + E), off=A("nl", 10 * z, 10 * z + 10))
 
+    def scaled(out, i, c, vector):
+        if vector:
+            ts(out, i, c, M)
+        else:
+            act(out, i, scale=c)
+
     def layer(z):
         quant("m", 160 * z, 160 * z + 160, A("mt", 640 * z, 640 * z + 640))
         for b in range(4):
             mm(4 * z + b, "w", 128 * b, "m", 160 * z, 160 * z + 160)
-        for b in range(4):
-            act(A("tb", 640 * z + b, 640 * z + 640, 4), P(4 * z + b, 0, 160), scale=0.03125)
+
+    def into_t(z, banks, vector=False):
+        for b in banks:
+            scaled(A("tb", 640 * z + b, 640 * z + 640, 4), P(4 * z + b, 0, 160), 0.03125, vector)
 
     def unpack_t(z):
         quant("t", 160 * z, 160 * z + 160, A("tb", 640 * z, 640 * z + 640))
         for b in range(4):
             mm(4 * z + b, "e", 128 * b, "t", 160 * z, 160 * z + 160)
-        for b in range(4):
-            if z == 0 or b < 3:
-                act(A("tt", 336 * b + 160 * z, 336 * b + 160 * z + 160), P(4 * z + b, 0, 160), scale=-1.0)
 
-    def lists(lo, hi, out):
-        for k in (1, 0):
-            scan(A("dg%d" % k, 2 * lo, 2 * hi), A("dia2", 2 * lo, 2 * hi), A("inv%d" % k, 2 * lo, 2 * hi), S, ALU.max)
-        m = A("dm", lo // 16, hi // 16)
-        tt(m, A("dg0", 2 * lo + 31, 2 * hi, 32), A("dg1", 2 * lo + 31, 2 * hi, 32), ALU.max)
-        ts(out, m, -1.0, M, K("h3"), S)
+    def into_minus(z, banks, vector=False):
+        for b in banks:
+            scaled(A("tt", 336 * b + 160 * z, 336 * b + 160 * z + 160), P(4 * z + b, 0, 160), -1.0, vector)
+
+    def scatter(i):
+        put(A("inv"), A("adr", 4 * i, 4 * i + 4), A("back", 64 * i, 64 * i + 64))
+
+    def lists(lo, hi, name, out):
+        n = 4 * (hi - lo)
+        for a in range(0, n, 384):
+            b = min(a + 384, n)
+            scan(A(name, a, b), A("dia4", 0, b - a), A("inv", 4 + 4 * lo + a, 4 + 4 * lo + b), S, ALU.max)
+        ts(out, A(name, 63, n, 64), -1.0, M, K("h3"), S)
 
     def minus(t):
-        return A("tt", 336 * t, 336 * t + 336)
+        return A("tt", 336 * t, 336 * t + C + 1)
 
     def rest_picks():
         for t in range(4):
-            act(A("gone", 192 * t, 192 * t + 192), minus(t), off=A("ul", 8, 20))
-            mm(3 + t, "e", 128 * t, "c", 128, 320)
+            act(A("gone", 224 * t, 224 * t + 224), minus(t), off=A("ul", 6, 20))
+            mm(3 + t, "e", 128 * t, "c", H, C)
 
     def rest():
         for t in range(4):
-            tt(A("xt", 512 + t, 1280, 4), P(3 + t, 0, 192), A("gone", 192 * t, 192 * t + 192), S)
-        quant("c", 128, 320, A("xt", 512, 1280))
+            tt(A("xt", 4 * H + t, 4 * C, 4), P(3 + t, 0, 224), A("gone", 224 * t, 224 * t + 224), S)
+        quant("c", H, C, A("xt", 4 * H, 4 * C))
 
-    def store(lo, hi):
-        dma("y", "ob", T.oc[:, 4 * lo:4 * hi], A("qc", lo, hi, bits=dt.uint8))
-        for k in range(4):
-            dma("y", "ob", T.osc[4 * k:4 * k + 4, lo:hi], A("sc", lo, hi, p=(32 * k, 32 * k + 4)))
-        mm(6, "v", 0, "c", lo, hi)
-        act(A("ysb", lo, hi), P(6, 0, hi - lo))
+    def store(k, lo, hi, bank):
+        mm(bank, "v", 0, k, lo, max(hi, 128))
+        dma("y", "ob", T.oc[:, 4 * lo:4 * hi], A("q" + k, lo, hi, bits=dt.uint8))
+        for i in range(4):
+            dma("y", "ob", T.osc[4 * i:4 * i + 4, lo:hi], A("s" + k, lo, hi, p=(32 * i, 32 * i + 4)))
+        act(A("ysb", lo, hi), P(bank, 0, hi - lo))
         dma("s", "ob", T.y[:, lo:hi], A("ysb", lo, hi))
 
     n_in_b = 2 * len(topo.engines(nxt, core))
@@ -561,37 +611,43 @@ def rank_program(g, core, T, topo):
         last = r == ROUNDS - 1
         arrive("ba%d" % r, n_in_b, [A("qc", C, E), A("sc", C, E)])
         score(6, 288, 416, 32)
-        for s in (1, 2, 3):
-            if r == 0 and s > 1:
-                lay_stage(s)
+        for s in (1, 2, 3) if r else (1,):
             tables(s)
-        for k in range(2):
-            iota(A("inv%d" % k), [[0, 864]], base=-64)
-        if r == 0:
-            iota(A("ub", 384, 512), [[0, 128]])
-            for b in range(4):
-                iota(A("tt", 336 * b + 320, 336 * b + 336), [[0, 16]])
+        iota(A("inv", 0, 1680), [[0, 1680]], base=-64)
         growth(r)
-        for t, z in ((1, 0), (2, 0), (3, 0), (0, 1), (1, 1), (2, 1), (3, 1)):
-            take(t, z, act)
-        tt(A("nr"), A("iw2"), A("late"), S, off=A("nl"))
-        for k in (0, 1):
-            ts(A("nlf", k, 20, 2), A("nl", k, 20, 2), 2.0, M, float(k), S)
-        take(0, 0, pick)
-        tt(A("eq"), A("nlf"), A("nr"), EQ, off=A("cidx"))
-        layer(0)
-        scan(A("scn"), A("dsc"), A("eq"), M, S)
-        tt(A("ad"), A("nlf"), A("scn", 15, 320, 16), S)
-        for k in (0, 1):
-            ts(A("adr", k, 20, 2), A("ad", k, 20, 2), K("q%d" % k), ALU.min)
-        between = {0: lambda: layer(1), 4: lambda: unpack_t(0), 7: lambda: unpack_t(1)}
-        for i in range(10):
-            if i in between:
-                between[i]()
-            d = 18 - 10 * (i % 2) - 2 * (i // 2)
-            put(A("inv%d" % (d // 10)), A("adr", d, d + 2), A("back", 16 * d, 16 * d + 32))
-        lists(C, E, A("ulb"))
-        ts(A("tt", 336 * 3 + 160, 336 * 3 + 320), P(7, 0, 160), -1.0, M)
+        ts(A("nlf"), P(1, 0, 20), 4.0, M)
+        for name in FLUX.split():
+            kind, by, a = name[0], name[1], [int(c) for c in name[2:]]
+            if kind == "n":
+                lo, hi = ((0, 8), (8, 20), (0, 20))[a[0]]
+                act(A("nr4", 16 * lo, 16 * hi), A("iw"), scale=4.0, off=A("nl", lo, hi))
+            elif kind == "k":
+                tt(A("nlk"), A("nlf"), A("kpat"), S)
+            elif kind == "e":
+                lo, hi = ((0, 8), (8, 20), (0, 20))[a[0]]
+                tt(A("eq", 16 * lo, 16 * hi), A("nlf"), A("nr4", 16 * lo, 16 * hi), EQ, off=A("cidx", lo, hi))
+            elif kind == "s":
+                lo, hi = ((0, 8), (8, 20), (0, 20))[a[0]]
+                scan(A("scn", 16 * lo, 16 * hi), A("dsc", 16 * lo, 16 * hi), A("eq", 16 * lo, 16 * hi), M, ALU.max)
+            elif kind == "a":
+                lo, hi = ((0, 8), (8, 20), (0, 20))[a[0]]
+                tt(A("ad", lo, hi), A("nlk", lo, hi), A("scn", 16 * lo + 15, 16 * hi, 16), ALU.max)
+            elif kind == "b":
+                lo, hi = ((0, 8), (8, 20), (0, 20))[a[0]]
+                copy(A("adr", lo, hi), A("ad", lo, hi))
+            elif kind == "m":
+                take(a[1], a[0], pick if by == "v" else act)
+            elif kind == "l":
+                layer(a[0])
+            elif kind == "t":
+                into_t(a[0], a[1:], by == "v")
+            elif kind == "u":
+                unpack_t(a[0])
+            elif kind == "i":
+                into_minus(a[0], a[1:], by == "v")
+            elif kind == "p":
+                scatter(a[0])
+        lists(C, E, "dgb", A("ulb"))
         for t in (2, 3):
             act(A("ub", t, 384, 4), minus(t), scale=-1.0, off=A("ulb"))
         for t in (0, 1):
@@ -600,13 +656,13 @@ def rank_program(g, core, T, topo):
         send(nxt, "r", 0, H, 128, "ra%d" % r, "rtl")
         if r == 0:
             quant("r", 224, 352, A("zb", 0, 512))
-        lists(0, C, A("ul"))
+        lists(0, C, "dgo", A("ul"))
         if last:
             act(A("nr"), A("iw"), off=A("nl"))
             dma("y", "ob", T.on[:, :], A("nr", p=(0, 128, 16)))
         rest_picks()
         for t in range(4):
-            tt(A("xf", 128 * t, 128 * t + 128), minus(t), A("vt", E * t, E * t + 128), S, off=A("ul", 0, 8))
+            tt(A("xf", H * t, H * t + H), minus(t), A("vt", E * t, E * t + H), S, off=A("ul", 0, 6))
         if last:
             rest()
         arrive("ra%d" % r, n_in_r, [A("qr", 128, 224), A("sr", 128, 224)])
@@ -614,17 +670,17 @@ def rank_program(g, core, T, topo):
         for b in range(4):
             mm(bb[b], "e", 128 * b, "r", 128, 256)
         if last:
-            store(128, 320)
+            store("c", H, C, 6)
         for b in range(4):
-            tt(A("xt", b, 512, 4), A("xf", 128 * b, 128 * b + 128), P(bb[b], 0, 128), ALU.subtract)
-        quant("c", 0, 128, A("xt", 0, 512))
+            tt(A("xt", b, 4 * H, 4), A("xf", H * b, H * b + H), P(bb[b], 0, H), ALU.subtract)
+        quant("m" if last else "c", 0, 128, A("xt", 0, 512))
         if last:
-            store(0, 128)
+            store("m", 0, H, 3)
         else:
             border_out(r + 1)
-            score(0, 0, 128)
+            score(0, 0, 128, cut=32)
             rest()
-            score(6, 128, 320)
+            score(6, H, C)
             unpack((2, 3, 4, 5), 0, 128)
             if r == 0:
                 quant("v", 0, 128, A("vin"))

from concourse.mybir import dt, AluOpType as ALU, ActivationFunctionType as AF

ROUNDS = 3
C, H, E = 320, 96, 416
BIG = 1.5 * 2.0 ** 28
FLUX = "ns1 ms02 ns0 ms03 ms10 ms11 ms12 mv00 mv01 ev1 kv sv1 ev0 av1 lv0 sv0 bv1 mv13 pv4 lv1 ts00 ts01 ts02 ts03 ts10 ts11 ts12 ts13 av0 pv3 bv0 pv2 uv0 pv1 uv1 pv0 is00 is01 is02 is03 iv10 is11 is12 is13"
SCRATCH = {}


def _declare(kind, names):
    for w in names.split():
        n, c = w.split(":")
        SCRATCH[n] = ("psum" if n.startswith("ps") else "sbuf", [128, int(c)], kind)


_declare("bfloat16", "xt:1280 ut:512 vin:512 zb:640 eb:516 vt:1664 mt:1280 tb:1280 tt:1344 ub:512 wr:896 ra:640 rb:640 gone:896 dsc:320 eq:320 scn:320")
_declare("bfloat16", "inv:3072 dia:416 dia4:384 back:320")
_declare("float16", "dgb:384 dgo:1280")
_declare("int32", "lri:128 bli:78 cpi:26 pi:2 pa:7")
_declare("uint16", "lru:64 lo16:4 bl:78 l0:16 ll:8 cidx:20 nl:20 adr:20 ul:20 ulb:6 lz:8 lab:24 rl:2")
_declare("float8_e4m3fn_x4", "qw:512 qu:128 q0:128 qv:128 qe:512 qc:416 qm:320 qt:320 qr:352 qa:160 qb:160 qk:224")
_declare("uint8", "sw:512 su:128 s0:128 sv:128 se:512 sc:416 sm:320 st:320 sr:352 sa:160 sb:160 sk:224")
_declare("float32", "i32:96 iw:416 cs:208 offs:8 lzf:8 pf:7 kk:32 dgf:64 df0:32 l0f:16 rlf:128")
_declare("float32", "aiw:416 giw:416 one:416 two:416 both:416 dx:416 dy:416 dz:416 win:2496 pat:32")
_declare("float32", "g0:384 tr0:384 ts0:256 gt:128 tr1:128 tr2:128 tr3:128 bt0:32 bt1:32 bt2:32 bt3:32 fo0:32 fo1:32 fo2:32 fo3:32")
_declare("float32", "nd:64 nf:28 ww:96 nlf:20 nlk:20 kpat:20 ss:416 sn:1248 nr:320")
_declare("float32", "ad:20 xf:384 ysb:320 nr4:320")
_declare("float32", "ps0:512 ps1:512 ps2:512 ps3:512 ps4:512 ps5:512 ps6:512 ps7:512")
SEMAPHORES = "cv cs ct cg lx0 lx1 llr lb lc lu lv lw lz ka k0 k1 k2 k3 t1 t2 t3 rp bl rtl ba0 ba1 ba2 ra0 ra1 ra2 ob".split()


def rank_program(g, core, T, topo):
    rank = T.rank_of(core)
    if rank is None:
        return
    nxt, prv = T.cores[(rank + 1) % 4], T.cores[(rank - 1) % 4]
    eng = {"v": g.vector, "s": g.scalar, "t": g.tensor, "g": g, "y": g.sync}
    csem = {"v": "cv", "s": "cs", "t": "ct", "g": "cg"}
    cnt = {s: 0 for s in SEMAPHORES}
    know = {q: {} for q in eng}
    acc = {}
    serial = [0]
    M, S, EQ = ALU.mult, ALU.add, ALU.is_equal

    def A(name, lo=0, hi=None, step=1, p=None, bits=None):
        t = T[name]
        hi = t.shape[1] if hi is None else hi
        ps = slice(None) if p is None else slice(*p)
        ap = t[ps, lo:hi] if step == 1 else t[ps, lo:hi:step]
        if bits is not None:
            ap = ap.bitcast(bits)
        return {"ap": ap, "n": name, "lo": lo, "hi": hi, "st": step, "p": set(range(*(p or (128,))))}

    slots = {}

    def K(name):
        i = slots.setdefault(name, len(slots))
        return A("kk", i, i + 1)

    def meet(a, b):
        if a["n"].startswith("ps"):
            return True
        if a["hi"] <= b["lo"] or b["hi"] <= a["lo"] or not a["p"] & b["p"]:
            return False
        return not (a["st"] == b["st"] and a["st"] > 1 and (a["lo"] - b["lo"]) % a["st"])

    def learn(q, rec, val):
        k = know[q]
        k[rec["sem"]] = max(k.get(rec["sem"], 0), val)
        for s, c in rec["know"].items():
            if k.get(s, 0) < c:
                k[s] = c

    def settle(q, reads, writes, adds):
        need = []
        for kind, regs in ((0, reads), (1, writes)):
            for r in regs:
                for a in acc.get(r["n"], []):
                    if not meet(r, a["reg"]):
                        continue
                    same = a["rec"]["q"] == q and not a["rec"]["late"]
                    if kind == 0 and not a["w"] and (same or not r["n"].startswith("ps")):
                        continue
                    if kind == 1 and adds and same:
                        continue
                    need.append(a["rec"])
        need.sort(key=lambda rec: -rec["id"])
        for rec in need:
            if know[q].get(rec["sem"], 0) >= rec["val"]:
                continue
            val = cnt[rec["sem"]] if rec["late"] else rec["val"]
            eng[q].wait_ge(T.sem[rec["sem"]], val)
            learn(q, rec, val)

    def note(rec, reads, writes):
        for w, regs in ((False, reads), (True, writes)):
            for r in regs:
                old = acc.get(r["n"], [])
                if w and r["st"] == 1:
                    old = [a for a in old if not (a["reg"]["lo"] >= r["lo"] and a["reg"]["hi"] <= r["hi"] and a["reg"]["p"] <= r["p"])]
                old.append({"reg": r, "rec": rec, "w": w})
                acc[r["n"]] = old

    def op(q, fn, writes, reads, sem=None, inc=1, self_inc=False, adds=False):
        settle(q, reads, writes, adds)
        s = sem or csem[q]
        ins = fn()
        if not self_inc:
            ins.then_inc(T.sem[s], inc)
        cnt[s] += inc
        serial[0] += 1
        note({"q": q, "sem": s, "val": cnt[s], "late": sem is not None, "know": dict(know[q]), "id": serial[0]}, reads, writes)

    def arrive(sem, n, writes):
        cnt[sem] += n
        serial[0] += 1
        note({"q": "far", "sem": sem, "val": cnt[sem], "late": True, "know": {}, "id": serial[0]}, [], writes)

    def copy(out, i):
        op("v", lambda: g.vector.tensor_copy(out["ap"], i["ap"]), [out], [i])

    def pick(out, i, off):
        op("v", lambda: g.vector.tensor_copy(out["ap"], i["ap"].indirect(off["ap"])), [out], [i, off])

    def put(out, off, i):
        op("v", lambda: g.vector.tensor_copy(out["ap"].indirect(off["ap"]), i["ap"]), [out], [off, i])

    def tt(out, a, b, o, off=None):
        ia = a["ap"] if off is None else a["ap"].indirect(off["ap"])
        op("v", lambda: g.vector.tensor_tensor(out["ap"], ia, b["ap"], o), [out], [a, b] + ([off] if off else []))

    def ts(out, a, s1, o1, s2=None, o2=None, off=None):
        ia = a["ap"] if off is None else a["ap"].indirect(off["ap"])
        rd = [a] + [s for s in (s1, s2, off) if isinstance(s, dict)]
        v1 = s1["ap"] if isinstance(s1, dict) else s1
        v2 = s2["ap"] if isinstance(s2, dict) else s2
        if o2 is None:
            op("v", lambda: g.vector.tensor_scalar(out["ap"], ia, v1, None, o1), [out], rd)
        else:
            op("v", lambda: g.vector.tensor_scalar(out["ap"], ia, v1, v2, o1, o2), [out], rd)

    def scan(out, d0, d1, o0, o1):
        op("v", lambda: g.vector.tensor_tensor_scan(out["ap"], d0["ap"], d1["ap"], 0.0, o0, o1), [out], [d0, d1])

    def turn(out, i):
        op("v", lambda: g.vector.transpose(out["ap"], i["ap"]), [out], [i])

    def fill(out, c):
        op("v", lambda: g.vector.memset(out["ap"], c), [out], [])

    def act(out, i, func=AF.Copy, scale=1.0, off=None, bias=0.0):
        ia = i["ap"] if off is None else i["ap"].indirect(off["ap"])
        sv, bv = [s["ap"] if isinstance(s, dict) else s for s in (scale, bias)]
        rd = [i] + [s for s in (off, scale, bias) if isinstance(s, dict)]
        op("s", lambda: g.scalar.activation(out["ap"], ia, func, scale=sv, bias=bv), [out], rd)

    def lin(out, i, scale, bias):
        act(out, i, AF.Identity, scale=scale, bias=bias)

    def quant(k, lo, hi, src):
        o, s = A("q" + k, lo, hi), A("s" + k, lo, hi)
        op("v", lambda: g.vector.quantize_mx(o["ap"], s["ap"], src["ap"]), [o, s], [src])

    def mm(bank, w, wlo, x, lo, hi, start=True, stop=True):
        o = A("ps%d" % bank, 0, hi - lo)
        a, b, c, d = A("q" + w, wlo, wlo + 128), A("s" + w, wlo, wlo + 128), A("q" + x, lo, hi), A("s" + x, lo, hi)
        op("t", lambda: g.tensor.matmul_mx(o["ap"], a["ap"], b["ap"], c["ap"], d["ap"], start, stop), [o], [a, b, c, d], adds=not start)

    def P(bank, lo, hi):
        return A("ps%d" % bank, lo, hi)

    def dma(q, sem, out, i):
        w, rd = [[a] if isinstance(a, dict) else [] for a in (out, i)]
        oa, ia = [a["ap"] if isinstance(a, dict) else a for a in (out, i)]
        op(q, lambda: eng[q].dma_start(oa, ia), w, rd, sem=sem, inc=16)

    def iota(o, pattern, cm=0, base=0):
        op("g", lambda: g.iota(o["ap"], pattern, base, cm, allow_small_or_imprecise_dtypes=True), [o], [])

    def send(dst, k, a, b, c, rsem, lsem):
        rid, pid = topo.addr(dst)[:2]
        mask, n = topo.mask(core, dst), len(topo.engines(core, dst))
        for name, bits in (("q" + k, dt.uint8), ("s" + k, None)):
            i, o = A(name, a, b, bits=bits), A(name, c, c + b - a, bits=bits)
            op("g", lambda: g.remote_dma(o["ap"], i["ap"], T.sem[rsem], T.sem[lsem], pid, rid, mask), [], [i], sem=lsem, inc=n, self_inc=True)

    def unpack(banks, lo, hi, skip=0):
        for b in range(4):
            mm(banks[b], "e", 128 * b, "c", lo, hi)
        for b in range(4):
            act(A("vt", E * b + lo + skip, E * b + hi), P(banks[b], skip, hi - lo))

    def score(bank, lo, hi, skip=0, cut=0):
        mm(bank, "0", 0, "c", lo, hi)
        act(A("ss", lo + skip, hi - cut), P(bank, skip, hi - lo - cut), AF.Abs)

    def border_out(r):
        send(prv, "c", 0, H, C, "ba%d" % r, "bl")

    def grp(gi):
        return (16 * gi, 16 * gi + 16)

    def rows(t, gi):
        return t[16 * gi:16 * gi + 16, :]

    def few(n):
        return A("i32", 0, n)

    dma("s", "llr", A("lri", 0, 26), T.lf[:, :])
    dma("y", "llr", A("lri", 26, 52, p=(0, 112)), T.lf[16:128, :])
    dma("s", "llr", A("lri", 52, 78, p=(16, 128)), T.rt[0:112, :])
    dma("y", "llr", A("lri", 78, 104), T.rt[:, :])
    dma("s", "llr", A("lri", 52, 78, p=(0, 16)), rows(T.rt, 0))
    dma("y", "llr", A("lri", 26, 52, p=(112, 128)), rows(T.lf, 0))
    dma("s", "lx0", A("xt", 0, 512), T.x[:, 0:512])
    dma("y", "lu", A("ut"), T.u[:, :])
    dma("y", "lx1", A("xt", 512, 1280), T.x[:, 512:1280])
    pi = A("pi")
    op("g", lambda: g.iota(pi["ap"], [[0, 2]], 0, 1), [pi], [])
    iota(A("i32", 0, 32), [[1, 32]])
    iota(A("i32", 32, 96), [[0, 4], [1, 16]])
    iota(A("iw"), [[1, 416]])
    iota(A("win", 0, 416), [[0, 416]], base=1)
    fill(A("bli"), 0)
    fill(A("win", 416, 832), 0.0)
    for s in (1, 2, 3):
        for t, gi, h in ((T.rt, 2 * s + 1, 1), (T.lf, 2 * s, 2), (T.rt, 2 * s, 3), (T.lf, 2 * s + 1, 4)):
            dma("y", "lb", A("bli", 26 * s - 26, 26 * s, p=grp(h)), rows(t, gi))

    lin(A("bt0", 0, 16, 4), few(4), 0.0, 0.0)
    lin(A("nf"), few(28), 0.0, 0.0)
    lin(A("df0", 0, 2), few(2), 0.0, 16.0)
    for lo, hi, st, c in ((0, 16, 2, 1.0), (16, 32, 2, -1.0), (1, 16, 4, -1.0), (17, 32, 2, 1.0), (3, 16, 4, 0.0)):
        lin(A("pat", lo, hi, st), few(16 // st), 0.0, c)

    def fields(lo, masks):
        for i, bits in enumerate(masks):
            ts(A("pa", lo + i, lo + i + 1), A("pi", 0, 1), bits, ALU.bitwise_and)

    def repeat(names, steps):
        for w, n in steps:
            for name in names:
                for lo in range(w, min(n, T[name].shape[1]), w):
                    hi = min(lo + w, n)
                    dma("y", "rp", A(name, lo, hi), A(name, 0, hi - lo))
    fields(0, (16, 1, 15, 96, 3, 8, 4))
    e16, odd, q, a32, m4, t8, t4 = [A("pf", i, i + 1) for i in range(7)]
    ei, oi, mi = A("pa", 0, 1), A("pa", 1, 2), A("pa", 4, 5)
    d16, d64 = A("cs", 16, 32), A("cs", 16, 80)
    ts(K("sg"), ei, -0.125, M, 1.0, S)
    ts(K("ns"), ei, 0.125, M, -1.0, S)
    ts(K("nl"), A("pi", 0, 1), 96.0, ALU.is_lt)
    copy(A("pf"), A("pa"))
    fill(A("lri", 104, 128), 0)
    ts(K("o2"), oi, 2.0, M, -1.0, S)
    copy(K("p"), A("pi", 0, 1))
    ts(K("g"), oi, K("ns"), M, K("sg"), S)
    ts(K("lo"), ei, 3.25, M, q, S)
    ts(K("a"), K("o2"), K("sg"), M, K("nl"), M)
    ts(K("mid"), A("pi", 0, 1), 32.0, ALU.is_ge, K("nl"), M)
    ts(A("lo16"), few(4), 16.0, M, K("lo"), S)
    ts(d64, A("i32", 32, 96), q, ALU.subtract)
    ts(K("far"), ei, 26.0, M, K("mid"), M)
    ts(A("cs", 80, 144), d64, 0.0, EQ, -4000.0, M)
    ts(A("cs", 144, 208), d64, 1.0, EQ, 2000.0, M)
    pick(A("lru"), A("lri"), A("lo16"))
    tt(A("dia", 0, 64), A("cs", 80, 144), A("cs", 144, 208), S)
    quant("c", 0, 128, A("xt", 0, 512))
    border_out(0)
    lin(A("lzf"), few(8), 0.0, 0.0)
    lin(K("u1"), t4, 8.0, 32.0)
    lin(K("u3"), t8, -2.0, -32.0)
    lin(A("lzf", 2, 4), few(2), 0.0, -16.0)
    act(A("giw"), A("iw"), scale=K("g"))
    act(A("aiw"), A("iw"), scale=K("a"))

    def empty(s):
        iota(A("win", 832 * s, 832 * s + 832), [[-1, 2], [0, 416]], base=1)
    l1, l2 = A("lru", 0, 26), A("lru", 26, 52)
    act(A("two"), A("iw"), off=l2)
    ts(K("b"), oi, K("ns"), M)
    copy(A("dia", 64, 128), A("dia", 0, 64))
    tt(A("dx"), A("giw"), A("aiw"), S, off=l2)
    lin(K("b0"), K("p"), 2.0, 0.0)
    lin(K("b2"), a32, 0.5, q)
    act(A("both"), A("two"), AF.Identity, bias=K("far"), off=l1)
    act(A("one"), A("iw"), off=l1)
    act(A("dy"), A("two"), scale=K("b"))
    copy(A("dia", 128, 256), A("dia", 0, 128))
    ts(K("hs"), q, 15.0, ALU.is_lt, 2000.0, M)
    ts(K("w1"), mi, 1.0, EQ, K("u1"), M)
    copy(A("dia", 256, 416), A("dia", 0, 160))
    ts(K("w3"), mi, 3.0, EQ, K("u3"), M)
    tt(K("h2"), K("hs"), K("far"), S)
    ts(K("r1"), mi, 3.0, ALU.not_equal)
    quant("u", 0, 128, A("ut"))
    ts(K("r3"), K("w1"), K("w3"), S, 48.0, S)
    scan(A("sn", 0, 416), A("dia"), A("both"), S, ALU.max)
    ts(A("lz"), A("lzf"), K("r1"), M, K("r3"), S)
    ts(A("cpi"), A("sn", 15, 416, 16), K("h2"), ALU.subtract)
    lin(K("b4"), a32, 1.0, K("p"))
    lin(K("b0"), q, -1.0, K("b0"))
    s0, su, lz = A("s0"), A("su"), A("lz")
    op("s", lambda: g.scalar.activation(s0["ap"], su["ap"].indirect(lz["ap"]), AF.Copy), [s0], [su, lz])
    lin(A("l0f", 8, 10), few(2), 32.0, K("b4"))
    lin(A("l0f", 0, 2), few(2), 16.0, K("b0"))
    for c in (2, 3):
        lin(A("l0f", c, 16, 8), A("df0", 0, 2), 16.0, K("b2"))
    phase, region, first = (0, 0, 0, 0), (0, 832, 1664, 0), (7, 2, 2, 2)

    def lay(sem, lo, c, src, gi, odd=0):
        dma("y", sem, A("win", lo, lo + 416, p=(c, 128, 16)), A(src, p=(16 * gi + odd, 16 * gi + 16, 2)))

    def lay_stage(s, late):
        ends = (("dz", 0), ("dz", 1), ("dx", 0), ("iw", 0)), (("dx", 0), ("dz", 1), ("dz", 0), ("both", 0))
        picks = (("both", 0), ("dy", 1), ("two", 0), ("dy", 0)), (("dx", 0), ("two", 0), ("dz", 0), ("both", 0))
        for side in (0, 1):
            gi, lo = 2 * s + side, region[s] + 416 * side
            for c, (src, odd) in zip((0, 4, 8, 12, first[s]), (ends if s < 3 else picks)[side] + (("one", 0),)):
                if (src == "dz") == late:
                    lay("k%d" % s, lo, c, src, gi, odd)
    lay("ka", 0, 15, "iw", 0)
    for c, src in (((11, 3), "two"), ((3, 11), "both")):
        for side in (0, 1):
            lay("ka", 416 * side, c[side], src, side)
    for side in (0, 1):
        lay("ka", 416 * side, 7, "one", side)
    for s in (1, 2, 3):
        for side in (0, 1):
            dma("y", "lc", A("bli", 26 * s - 26, 26 * s, p=grp(5 * side)), A("cpi", p=grp(2 * s + side)))
    pick(A("q0", bits=dt.uint32), A("qu", bits=dt.uint32), A("lz"))
    for c in (8, 0):
        lin(A("l0f", c + 4, c + 8), A("l0f", c, c + 4), 1.0, 416.0)
    quant("c", 128, 320, A("xt", 512, 1280))
    tt(A("dz"), A("dx"), A("dy"), S, off=l1)
    copy(A("l0"), A("l0f"))
    fill(A("zb"), 0.0)
    empty(1)
    lay_stage(1, False)
    lay_stage(1, True)
    dma("y", "lu", A("rb"), A("zb"))
    empty(2)
    lay_stage(2, False)
    eb, zb = A("eb"), A("zb", 0, 516)
    op("g", lambda: g.affine_select(eb["ap"], zb["ap"], [[1, 516]], ALU.not_equal, 1.0, -3, -4), [eb], [zb])
    iota(A("offs"), [[416, 2], [0, 4]])
    for e in (0, 1):
        iota(A("rlf", 16 * e, 16 * e + 8), [[64, 2], [8, 4]], 4, 32 * e)
        iota(A("rlf", 16 * e + 8, 16 * e + 16), [[128, 2], [8, 4]], 1, 512 + 256 * e)
        for k in (0, 1):
            lo = 32 + 16 * e + 8 * k
            iota(A("rlf", lo, lo + 4), [[32, 2], [8, 2]], 4, 1024 + 64 * e + 16 * k)
            iota(A("rlf", lo + 4, lo + 8), [[128, 2], [8, 2]], 1, 1536 + 256 * e + 16 * k)
    iota(A("kpat"), [[0, 5], [1, 4]], base=4)
    iota(A("back"), [[-1, 320]], base=256)
    score(0, 0, 128)
    score(6, 128, 320)
    act(A("g0", 128, 256), A("win", 0, 832), off=A("l0", 8, 16))
    act(A("gt"), A("win", 0, 832), off=A("l0", 0, 8))
    ts(K("w0"), q, 96.0, S)
    copy(A("bl"), A("bli"))
    turn(A("ts0", 128, 256), A("g0", 128, 256))
    ts(A("cs", 0, 16), d16, 0.0, EQ)
    copy(A("cidx"), few(20))
    for k, c in enumerate((7, 11, 3)):
        copy(A("lab", 8 * k, 8 * k + 8), A("ts0", 128 + c, 256, 16))
    turn(A("ts0", 0, 128), A("gt"))

    def in_gaps():
        yield lambda: (fill(A("ub", 384, 512), 0.0), fill(A("tt", C, 1344, 336), 0.0))
        yield lambda: ts(A("wr", 0, 896, 4), A("iw", 0, 224), K("w0"), EQ)
        for b in range(4):
            yield lambda b=b: quant("e", 128 * b, 128 * b + 128, A("eb", 3 - b, 515 - b))

    def first_differences():
        yield lambda: tt(A("df0", 0, 16), A("ts0", 3, 64, 4), A("ts0", 7, 68, 4), ALU.subtract)
        yield lambda: tt(A("df0", 17, 32), A("ts0", 67, 124, 4), A("ts0", 71, 128, 4), ALU.subtract)
        yield lambda: copy(A("df0", 3, 16, 4), A("ts0", 15, 64, 16))
        yield lambda: ts(A("df0", 19, 32, 4), A("ts0", 75, 128, 16), 416.0, S)
        yield lambda: tt(A("df0", 16, 32, 4), A("ts0", 15, 64, 16), A("ts0", 67, 128, 16), ALU.subtract)

    def leads():
        act(A("wr", 1, 896, 4), A("wr", 0, 896, 4))
        for t in (2, 3):
            act(A("wr", t, 64, 4), A("wr", 0, 64, 4))
            act(A("wr", 64 + t, 896, 4), A("wr", 0, 832, 4))

    def later_constants():
        for k in range(4):
            lin(K("q%d" % k), q, 64.0, 2047.0 + 16 * k)
        for k in range(4):
            lin(A("dia4", k, 64, 4), A("dia", 0, 16), 0.0 if k else 0.5, 0.0)
        for k in range(4):
            lin(A("dsc", 16 * k, 16 * k + 16), A("cs", 0, 16), K("q%d" % k), 1.0)
        lin(K("h3"), K("hs"), 0.5, 256.0)
        lin(A("dsc", 0, 64, 16), few(4), 0.0, 0.0)
        repeat(["dsc", "dia4"], ((64, 384),))

    def tables(s):
        act(A("sn", 416 * s - 416, 416 * s), A("ss"), off=A("bl", 26 * s - 26, 26 * s))
        if s == 1:
            for h in range(6):
                lo = region[1] + 416 * (h % 2)
                dma("ys"[h % 2], "t1", A("win", lo, lo + 416, p=(5 + 4 * (h // 2), 128, 16)), A("sn", 0, 416, p=(16 * h, 16 * h + 16, 2)))
            return
        for h in range(8):
            dma("y", "t%d" % s, A("win", region[s], region[s] + 832, p=(16 * h + 5, 16 * h + 14, 4)), A("sn", 416 * s - 416, 416 * s, p=(4 * s - 7, 96, 16)))

    def carry(s):
        x, lo = "ba"[s // 2], 32 * (s % 2)
        mm(1, "k", 96 - 32 * s, x, lo, lo + 128, s == 0, s == 3)

    def high(n, lo, hi):
        ts(A("dgf", lo, hi, 2), n, BIG, S, BIG, ALU.subtract)

    def low(n, lo, hi):
        tt(A("dgf", lo + 1, hi, 2), n, A("dgf", lo, hi, 2), ALU.subtract)

    def first_choice(s, tr):
        bt, u, n = "bt%d" % s, first[s], 16 + 8 * (s // 2)
        yield lambda: tt(A("nd", n, n + 4), A(tr, u, 64, 16), A(tr, 64 + u, 128, 16), ALU.subtract)
        yield lambda: tt(A("nd", n + 4, n + 8), A("nd", n, n + 4), A(bt, 2, 16, 4), M)
        yield lambda: tt(A("nf", 8 * s, 8 * s + 4), A("nd", n + 4, n + 8), A(tr, 64 + u, 128, 16), S)

    def second_choice(s):
        fo = "fo%d" % s
        yield lambda: tt(A("nd", 48, 56), A(fo, 3, 32, 4), A("offs"), ALU.subtract)
        yield lambda: tt(A("nd", 56, 64), A("nd", 48, 56), A("ww", 32 * s + 3, 32 * s + 32, 4), M)
        yield lambda: tt(A("nf", 12, 16), A("nd", 56, 60), A("nd", 60, 64), S)

    def choices(s, tr, r):
        bt, fo, u, n = "bt%d" % s, "fo%d" % s, first[s], 16 * s

        def one(name, i):
            return A(name, i, i + 1)
        lin(A("nd", n, n + 4), A(fo, 19, 32, 4), 1.0, -416.0)
        for m in range(3):
            if s or not r:
                lin(one("nd", n + 4 + m), one(tr, 64 + u + 16 * m), -1.0, one(tr, u + 16 * m))
        for m in range(3):
            lin(one("nd", n + 8 + m), one("nd", n + m), -1.0, one(fo, 3 + 4 * m))
        for m in range(3):
            lin(one("nf", 8 * s + 2 * m), one("nd", n + 4 + m), one(bt, 2 + 4 * m), one(tr, 64 + u + 16 * m))
        for m in range(3):
            lin(one("nf", 8 * s + 2 * m + 1), one("nd", n + 8 + m), one("ww", 32 * s + 3 + 4 * m), one("nd", n + m))

    def carry_first(r):
        yield lambda: high(A("nf", 0, 16), 32, 64)
        yield lambda: low(A("nf", 0, 16), 32, 64)
        yield lambda: put(A("rb"), A("rl"), A("dgf", 32, 64))

        def out():
            quant("b", 0, 128 if r else 160, A("rb", 0, 512 if r else 640))
            carry(0)
            carry(1)
        yield out

    def growth(r):
        todo = []

        def gap(n=1):
            for _ in range(n):
                if todo:
                    todo.pop(0)()
        for s in range(4):
            bt, fo, ph = "bt%d" % s, "fo%d" % s, phase[s]
            if s == 0:
                tr = "ts0"
                if r == 0:
                    todo.extend(first_differences())
                for k in range(3):
                    pick(A("g0", 128 * k, 128 * k + 128), A("ss"), A("lab", 8 * k, 8 * k + 8))
                gap(2)
                for k in range(3):
                    turn(A("tr0", 128 * k, 128 * k + 128), A("g0", 128 * k, 128 * k + 128))
                gap(3)
                if r == 0:
                    todo.extend(in_gaps())
                    lay_stage(2, True)
                    lay_stage(3, True)
                    tables(2)
                    lay_stage(3, False)
                    tables(3)
                    dma("y", "lz", A("ra"), A("zb"))
                    dma("y", "lw", A("qw", bits=dt.uint8), T.wc[:, :])
                    dma("y", "lw", A("sw"), T.ws[:, :])
                    dma("y", "lv", A("vin"), T.v[:, :])
                gap()
                for k, (bit, cls) in enumerate(((2, 11), (3, 3), (1, 3))):
                    c = 128 * k + cls
                    tt(A(bt, bit, 16, 4), A("tr0", c, 128 * k + 64, 16), A("tr0", c + 64, 128 * k + 128, 16), ALU.is_le)
            else:
                tr = "tr%d" % s
                pick(A("gt"), A("win", region[s], region[s] + 832), A("ll"))
                gap()
                turn(A(tr), A("gt"))
                gap()
                for side in (0, 1) if s < 3 else (0,):
                    tt(A(bt, 16 * side, 16 * side + 16), A(tr, ph + 1, 64, 4), A(tr, 64 + ph + 1, 128, 4), ALU.is_le)
            f = list(first_choice(s, tr)) if s % 2 else [gap] * 3
            if s == 1:
                gap()
            f[0]()
            if s == 3:
                tt(A(fo, 16, 32), A(tr, 0, 64, 4), A(tr, 64, 128, 4), S)
            n = 32 if s in (1, 2) else 16
            tt(A(bt, 3, n, 4), A(bt, 2, n, 4), A(bt, 3, n, 4), ALU.max)
            f[1]()
            if s == 3:
                scan(A(fo, 0, 16), A(bt, 0, 16), A(fo, 16, 32), M, S)
            elif s:
                scan(A(fo), A(bt), A(tr, ph, 128, 4), M, S)
            else:
                for o in (0, 16):
                    scan(A(fo, o, o + 16), A(bt, 0, 16), A("df0", o, o + 16), M, S)
            f[2]()
            if s < 3:
                copy(A("ll"), A(fo, 3, 32, 4))
                k = 32 if s == 1 else 16
                scan(A("ww", 32 * s, 32 * s + k), A(bt, 0, k), A("pat", 0, k), M, S)
                if s == 1:
                    if r == 0:
                        turn(A("rlf", 64, 128), A("rlf", 0, 64))
                    todo.extend(second_choice(s))
                    if r == 0:
                        todo.insert(1, lambda: (ts(A("rl", 0, 2), A("rlf", 64, 128, 32), 0.125, M), quant("k", 0, 224, A("wr"))))
                    todo.extend(carry_first(r))
                else:
                    choices(s, tr, r)
                if s == (0 if r else 2):
                    unpack((2, 3, 4, 5), 288, 416, 32)
                    unpack((0, 7, 2, 3), 128, 320)
                    if r == 0:
                        unpack((4, 5, 0, 7), 0, 128)
                if s == 0 and r == 0:
                    leads()
                    later_constants()
                gap()
            else:
                gap(len(todo))
                for digit in (high, low):
                    digit(A(fo, 3, 16, 4), 24, 32)
                    digit(A("nf", 16, 28), 0, 24)
                put(A("ra"), A("rl"), A("dgf", 0, 32))
                quant("a", 0, 128 if r else 160, A("ra", 0, 512 if r else 640))
                carry(2)
                carry(3)
                copy(A("nl"), P(1, 0, 20))

    def take(t, z, how):
        how(A("mt", 640 * z + t, 640 * z + 640, 4), A("vt", E * t, E * t + E), off=A("nl", 10 * z, 10 * z + 10))

    def scaled(out, i, c, vector):
        if vector:
            ts(out, i, c, M)
        else:
            act(out, i, scale=c)

    def layer(z):
        quant("m", 160 * z, 160 * z + 160, A("mt", 640 * z, 640 * z + 640))
        for b in range(4):
            mm(4 * z + b, "w", 128 * b, "m", 160 * z, 160 * z + 160)

    def into_t(z, banks, vector=False):
        for b in banks:
            scaled(A("tb", 640 * z + b, 640 * z + 640, 4), P(4 * z + b, 0, 160), 0.03125, vector)

    def unpack_t(z):
        quant("t", 160 * z, 160 * z + 160, A("tb", 640 * z, 640 * z + 640))
        for b in range(4):
            mm(4 * z + b, "e", 128 * b, "t", 160 * z, 160 * z + 160)

    def into_minus(z, banks, vector=False):
        for b in banks:
            scaled(A("tt", 336 * b + 160 * z, 336 * b + 160 * z + 160), P(4 * z + b, 0, 160), -1.0, vector)

    def scatter(i):
        put(A("inv"), A("adr", 4 * i, 4 * i + 4), A("back", 64 * i, 64 * i + 64))

    def lists(lo, hi, name, out):
        n = 4 * (hi - lo)
        for a in range(0, n, 384):
            b = min(a + 384, n)
            scan(A(name, a, b), A("dia4", 0, b - a), A("inv", 4 + 4 * lo + a, 4 + 4 * lo + b), S, ALU.max)
        ts(out, A(name, 63, n, 64), -1.0, M, K("h3"), S)

    def minus(t):
        return A("tt", 336 * t, 336 * t + C + 1)

    def rest_picks():
        for t in range(4):
            act(A("gone", 224 * t, 224 * t + 224), minus(t), off=A("ul", 6, 20))
            mm(3 + t, "e", 128 * t, "c", H, C)

    def rest():
        for t in range(4):
            tt(A("xt", 4 * H + t, 4 * C, 4), P(3 + t, 0, 224), A("gone", 224 * t, 224 * t + 224), S)
        quant("c", H, C, A("xt", 4 * H, 4 * C))

    def store(k, lo, hi, bank):
        mm(bank, "v", 0, k, lo, max(hi, 128))
        dma("y", "ob", T.oc[:, 4 * lo:4 * hi], A("q" + k, lo, hi, bits=dt.uint8))
        for i in range(4):
            dma("y", "ob", T.osc[4 * i:4 * i + 4, lo:hi], A("s" + k, lo, hi, p=(32 * i, 32 * i + 4)))
        act(A("ysb", lo, hi), P(bank, 0, hi - lo))
        dma("s", "ob", T.y[:, lo:hi], A("ysb", lo, hi))

    n_in_b = 2 * len(topo.engines(nxt, core))
    n_in_r = 2 * len(topo.engines(prv, core))
    for r in range(ROUNDS):
        last = r == ROUNDS - 1
        arrive("ba%d" % r, n_in_b, [A("qc", C, E), A("sc", C, E)])
        score(6, 288, 416, 32)
        for s in (1, 2, 3) if r else (1,):
            tables(s)
        iota(A("inv", 0, 1680), [[0, 1680]], base=-64)
        growth(r)
        ts(A("nlf"), P(1, 0, 20), 4.0, M)
        for name in FLUX.split():
            kind, by, a = name[0], name[1], [int(c) for c in name[2:]]
            if kind == "n":
                lo, hi = ((0, 8), (8, 20), (0, 20))[a[0]]
                act(A("nr4", 16 * lo, 16 * hi), A("iw"), scale=4.0, off=A("nl", lo, hi))
            elif kind == "k":
                tt(A("nlk"), A("nlf"), A("kpat"), S)
            elif kind == "e":
                lo, hi = ((0, 8), (8, 20), (0, 20))[a[0]]
                tt(A("eq", 16 * lo, 16 * hi), A("nlf"), A("nr4", 16 * lo, 16 * hi), EQ, off=A("cidx", lo, hi))
            elif kind == "s":
                lo, hi = ((0, 8), (8, 20), (0, 20))[a[0]]
                scan(A("scn", 16 * lo, 16 * hi), A("dsc", 16 * lo, 16 * hi), A("eq", 16 * lo, 16 * hi), M, ALU.max)
            elif kind == "a":
                lo, hi = ((0, 8), (8, 20), (0, 20))[a[0]]
                tt(A("ad", lo, hi), A("nlk", lo, hi), A("scn", 16 * lo + 15, 16 * hi, 16), ALU.max)
            elif kind == "b":
                lo, hi = ((0, 8), (8, 20), (0, 20))[a[0]]
                copy(A("adr", lo, hi), A("ad", lo, hi))
            elif kind == "m":
                take(a[1], a[0], pick if by == "v" else act)
            elif kind == "l":
                layer(a[0])
            elif kind == "t":
                into_t(a[0], a[1:], by == "v")
            elif kind == "u":
                unpack_t(a[0])
            elif kind == "i":
                into_minus(a[0], a[1:], by == "v")
            elif kind == "p":
                scatter(a[0])
        lists(C, E, "dgb", A("ulb"))
        for t in (2, 3):
            act(A("ub", t, 384, 4), minus(t), scale=-1.0, off=A("ulb"))
        for t in (0, 1):
            ts(A("ub", t, 384, 4), minus(t), -1.0, M, off=A("ulb"))
        quant("r", 0, 128, A("ub"))
        send(nxt, "r", 0, H, 128, "ra%d" % r, "rtl")
        if r == 0:
            quant("r", 224, 352, A("zb", 0, 512))
        lists(0, C, "dgo", A("ul"))
        if last:
            act(A("nr"), A("iw"), off=A("nl"))
            dma("y", "ob", T.on[:, :], A("nr", p=(0, 128, 16)))
        rest_picks()
        for t in range(4):
            tt(A("xf", H * t, H * t + H), minus(t), A("vt", E * t, E * t + H), S, off=A("ul", 0, 6))
        if last:
            rest()
        arrive("ra%d" % r, n_in_r, [A("qr", 128, 224), A("sr", 128, 224)])
        bb = (0, 1, 7, 2)
        for b in range(4):
            mm(bb[b], "e", 128 * b, "r", 128, 256)
        if last:
            store("c", H, C, 6)
        for b in range(4):
            tt(A("xt", b, 4 * H, 4), A("xf", H * b, H * b + H), P(bb[b], 0, H), ALU.subtract)
        quant("m" if last else "c", 0, 128, A("xt", 0, 512))
        if last:
            store("m", 0, H, 3)
        else:
            border_out(r + 1)
            score(0, 0, 128, cut=32)
            rest()
            score(6, H, C)
            unpack((2, 3, 4, 5), 0, 128)
            if r == 0:
                quant("v", 0, 128, A("vin"))
    for s in SEMAPHORES:
        if know["g"].get(s, 0) < cnt[s]:
            g.wait_ge(T.sem[s], cnt[s])
